import numpy as np
import ml_dtypes


def mxq(x, axis, fmt="e4m3"):
    dtype, down = {"e4m3": (ml_dtypes.float8_e4m3fn, 7), "e5m2": (ml_dtypes.float8_e5m2, 14)}[fmt]
    v = np.moveaxis(np.asarray(x, np.float32).astype(ml_dtypes.bfloat16).astype(np.float64), axis, -1)
    blocks = v.reshape(v.shape[:-1] + (-1, 32))
    amax = np.abs(blocks).max(-1, keepdims=True)
    byte = np.maximum(np.where(amax > 0, np.frexp(amax)[1] - 1 + 127, 0) - down, 1)
    scale = np.exp2(byte - 127.0)
    codes = (blocks / scale).astype(np.float32).astype(dtype).astype(np.float64)
    return np.moveaxis((codes * scale).reshape(v.shape), -1, axis)


WIDE = False


def mx_kscale(k):
    if not WIDE:
        return np.ones(k)
    levels = np.array([18, -18])
    if k % 512:
        return np.exp2(np.random.permutation(np.resize(levels, k // 32))).repeat(32)
    a = np.empty((k // 512, 16))
    for p in range(k // 512):
        a[p, :8] = np.random.permutation(np.resize(levels, 8))
        for g in range(8):
            far = levels[np.abs(levels - a[p, g]) >= 10]
            a[p, g + 8] = far[np.random.randint(len(far))]
    return np.exp2(a.ravel()).repeat(32)


def f64(x):
    return np.asarray(x).astype(np.float64)


def striped(idx):
    return np.tile(np.asarray(idx).reshape(-1, 16).T, (8, 1)).astype(np.uint16)


def unstriped(offs):
    return offs[:16].T.reshape(-1).astype(np.int64)


B, N, T, D, R = 2, 512, 2048, 512, 512


def setup_inputs():
    n = np.random.standard_normal
    idx = np.random.permutation(T)[:B * N]
    s = mx_kscale(D)[:, None]
    z = mx_kscale(R)[:, None]
    x = n((B, D, R))
    return {
        "xT": (x * s).astype(np.float32),
        "wT": (n((D, T)) * (1.00 / np.sqrt(D)) / s).astype(np.float32),
        "y": n((B, R, N)).astype(np.float32),
        "wt": (np.random.uniform(0.5, 1.5, (B, R, 1)) * 1.0 / np.sqrt(R) * z).astype(np.float32),
        "xm": (x.transpose(0, 2, 1) / z).astype(np.float32),
        "offs": striped(idx),
    }


def reference(xT, wT, y, wt, xm, offs):
    idx = unstriped(offs)
    pick = lambda x: x[:, idx].reshape(x.shape[0], B, N).transpose(1, 0, 2)
    a = mxq(f64(xT), 1, "e4m3").transpose(0, 2, 1) @ mxq(pick(f64(wT)), 1, "e4m3")
    g = f64(wt) * np.tanh(a - f64(y))
    dw = mxq(f64(xm), 1, "e4m3").transpose(0, 2, 1) @ mxq(g, 1, "e5m2")
    gw = np.zeros((D, T))
    gw[:, idx] = dw.transpose(1, 0, 2).reshape(D, B * N)
    return gw

@@ -1,0 +1,175 @@
+from contextlib import ExitStack
+
+import concourse.mybir as mybir
+
+B, N, T, D, R = 2, 512, 2048, 512, 512
+FLOPS = 2 * B * (R * N * D + D * N * R)
+
+F32 = mybir.dt.float32
+BF16 = mybir.dt.bfloat16
+U32 = mybir.dt.uint32
+U16 = mybir.dt.uint16
+U8 = mybir.dt.uint8
+E4M3 = mybir.dt.float8_e4m3fn_x4
+E5M2 = mybir.dt.float8_e5m2_x4
+ACT = mybir.ActivationFunctionType
+ALU = mybir.AluOpType
+
+P = 128
+PACK = 4
+CHUNK = 128
+W_PIECE = 1024
+W_ON_VECTOR = 688
+COLS = N // 16
+
+
+def tile_attend_glch_w_kernel(tc, xT, wT, y, wt, xm, offs, out):
+    nc = tc.nc
+    with ExitStack() as ctx:
+        sb = ctx.enter_context(tc.tile_pool(name="sb", bufs=1))
+        ps_a = ctx.enter_context(tc.psum_pool(name="ps_a", bufs=4))
+        ps_dw = ctx.enter_context(tc.psum_pool(name="ps_dw", bufs=4))
+
+        def tile(shape, dtype, name):
+            return sb.tile(shape, dtype, name=name, align_bytes=64)
+
+        def quantize(name, grouped, fmt, pieces=1):
+            width = grouped.shape[1] // PACK
+            codes = tile([P, width], U32, name + "_codes")
+            scales = tile([P, width], U8, name + "_scales")
+            step = width // pieces
+            for c0 in range(0, width, step):
+                nc.vector.quantize_mx(out=codes[:, c0:c0 + step].bitcast(fmt), scales=scales[:, c0:c0 + step],
+                                      in_=grouped[:, PACK * c0:PACK * (c0 + step)])
+            return codes, scales
+
+        offsets = tile([P, B * COLS], U16, "offsets")
+        nc.sync.dma_start(offsets[:], offs)
+        w_rows = wT.rearrange("(p u e) c -> p u e c", u=2, e=2)
+        w_raw = {}
+        for u in range(2):
+            for h in range(T // W_PIECE):
+                w_raw[u, h] = tile([P, 2, W_PIECE], F32, "w_raw%d%d" % (u, h))
+                nc.sync.dma_start(w_raw[u, h][:], w_rows[:, u, :, h * W_PIECE:(h + 1) * W_PIECE])
+        x_raw, y_sb, xm_raw = {}, {}, {}
+        wt_sb = tile([P, B, PACK], F32, "wt_sb")
+        for b in range(B):
+            x_rows = xT[b].rearrange("(p j) r -> p j r", j=PACK)
+            for h in range(2):
+                x_raw[b, h] = tile([P, PACK, R // 2], F32, "x_raw%d%d" % (b, h))
+                nc.sync.dma_start(x_raw[b, h][:], x_rows[:, :, h * (R // 2):(h + 1) * (R // 2)])
+            y_sb[b] = tile([P, PACK, N], F32, "y_sb%d" % b)
+            nc.sync.dma_start(y_sb[b][:], y[b].rearrange("(p t) i -> p t i", t=PACK))
+            if b == 0:
+                nc.sync.dma_start(wt_sb[:], wt.rearrange("b (p t) o -> p b (t o)", t=PACK))
+            xm_raw[b] = tile([P, PACK, D], F32, "xm_raw%d" % b)
+            nc.sync.dma_start(xm_raw[b][:], xm[b].rearrange("(p t) d -> p t d", t=PACK))
+
+        windows = []
+        for j in range(D // P):
+            window = tile([P, T], F32, "window%d" % j)
+            nc.vector.memset(window[:], 0.0)
+            windows.append(window)
+
+        w_pairs = [tile([P, T * 2], BF16, "w_pairs%d" % u) for u in range(2)]
+        w_picked = [tile([P, N * PACK], BF16, "w_picked%d" % b) for b in range(B)]
+
+        def cast_table(u):
+            for h in range(T // W_PIECE):
+                src = w_raw[u, h][:].rearrange("p e (c i) -> p c e i", i=4)
+                dst = w_pairs[u][:, 2 * h * W_PIECE:2 * (h + 1) * W_PIECE].rearrange("p (c i e) -> p c e i", i=4, e=2)
+                cv = W_ON_VECTOR // 4
+                nc.vector.tensor_copy(dst[:, :cv], src[:, :cv])
+                nc.scalar.activation(dst[:, cv:], src[:, cv:], ACT.Copy)
+
+        def gather(b, u):
+            dst = w_picked[b][:].bitcast(U32).rearrange("p (i u) -> p i u", u=2)
+            nc.vector.tensor_copy(dst[:, :, u], w_pairs[u][:].bitcast(U32).indirect(offsets[:, b * COLS:(b + 1) * COLS]))
+
+        def cast_x(b):
+            grouped = tile([P, R * PACK], BF16, "x_grouped%d" % b)
+            dst = grouped[:].rearrange("p (t m j) -> p m j t", t=PACK, j=PACK)
+            for h in range(2):
+                nc.scalar.copy(dst[:, h * 64:(h + 1) * 64], x_raw[b, h][:].rearrange("p j (m t) -> p m j t", t=PACK))
+            return grouped
+
+        def cast_xm(b):
+            grouped = tile([P, D * PACK], BF16, "xm_grouped%d" % b)
+            dst = grouped[:].rearrange("p (c i t) -> p c t i", i=4, t=PACK)
+            src = xm_raw[b][:].rearrange("p t (c i) -> p c t i", i=4)
+            for j in range(4):
+                nc.scalar.copy(dst[:, j * 32:(j + 1) * 32], src[:, j * 32:(j + 1) * 32])
+            return grouped
+
+        def residual(b, c, x_q, w_q, dst):
+            cols = slice(c * CHUNK, (c + 1) * CHUNK)
+            a_ps = ps_a.tile([P, PACK, CHUNK], F32, name="a_ps")
+            for t in range(PACK):
+                rows = slice(t * P, (t + 1) * P)
+                nc.tensor.matmul_mx(out=a_ps[:, t, :], lhsT=x_q[0][:, rows].bitcast(E4M3), lhsT_scale=x_q[1][:, rows],
+                                    rhs=w_q[0][:, cols].bitcast(E4M3), rhs_scale=w_q[1][:, cols], start=True, stop=True)
+            nc.vector.tensor_tensor(dst, a_ps[:], y_sb[b][:, :, cols], ALU.subtract)
+
+        def second_product(b, xm_q, g_q):
+            res = []
+            for j in range(D // P):
+                rows = slice(j * P, (j + 1) * P)
+                dw_ps = ps_dw.tile([P, N], F32, name="dw_ps")
+                nc.tensor.matmul_mx(out=dw_ps[:], lhsT=xm_q[0][:, rows].bitcast(E4M3), lhsT_scale=xm_q[1][:, rows],
+                                    rhs=g_q[0][:].bitcast(E5M2), rhs_scale=g_q[1][:], start=True, stop=True)
+                dw = tile([P, N], F32, "dw%d%d" % (b, j))
+                nc.scalar.copy(dw[:], dw_ps[:])
+                res.append(dw)
+            return res
+
+        cast_table(0)
+        gather(0, 0)
+        gather(1, 0)
+        cast_table(1)
+        gather(0, 1)
+        w_q0 = quantize("w0", w_picked[0], E4M3)
+        x_q0 = quantize("x0", cast_x(0), E4M3)
+
+        g0 = tile([P, N * PACK], BF16, "g0")
+        th0 = []
+        for c in range(N // CHUNK):
+            u0 = tile([P, PACK, CHUNK], F32, "u0%d" % c)
+            residual(0, c, x_q0, w_q0, u0[:])
+            th = tile([P, CHUNK * PACK], F32, "th0%d" % c)
+            nc.scalar.activation(th[:].rearrange("p (c i t) -> p c t i", i=2, t=PACK),
+                                 u0[:].rearrange("p t (c i) -> p c t i", i=2), ACT.Tanh)
+            th0.append(th)
+        for c in range(N // CHUNK):
+            nc.vector.tensor_tensor(g0[:, c * CHUNK * PACK:(c + 1) * CHUNK * PACK].rearrange("p (i t) -> p i t", t=PACK),
+                                    th0[c][:].rearrange("p (i t) -> p i t", t=PACK),
+                                    wt_sb[:, 0:1, :].to_broadcast([P, CHUNK, PACK]), ALU.mult)
+        xm_q0 = quantize("xm0", cast_xm(0), E4M3)
+        g_q0 = quantize("g0", g0, E5M2)
+        dw0 = second_product(0, xm_q0, g_q0)
+
+        gather(1, 1)
+        w_q1 = quantize("w1", w_picked[1], E4M3)
+        x_q1 = quantize("x1", cast_x(1), E4M3)
+        g1 = tile([P, N * PACK], BF16, "g1")
+        half = N // 2
+        for h in range(2):
+            u1 = tile([P, PACK, half], F32, "u1%d" % h)
+            for c in range(2):
+                residual(1, 2 * h + c, x_q1, w_q1, u1[:, :, c * CHUNK:(c + 1) * CHUNK])
+            th = tile([P, PACK, half], F32, "th1%d" % h)
+            nc.scalar.activation(th[:], u1[:], ACT.Tanh)
+            g_rows = tile([P, PACK, half], BF16, "g_rows%d" % h)
+            for t in range(PACK):
+                nc.scalar.activation(g_rows[:, t, :], th[:, t, :], ACT.Copy, scale=wt_sb[:, 1, t:t + 1])
+            nc.scalar.copy(g1[:, h * half * PACK:(h + 1) * half * PACK].rearrange("p (c i t) -> p c t i", i=4, t=PACK),
+                           g_rows[:].rearrange("p t (c i) -> p c t i", i=4))
+        xm_q1 = quantize("xm1", cast_xm(1), E4M3)
+        g_q1 = quantize("g1", g1, E5M2, pieces=2)
+        dw1 = second_product(1, xm_q1, g_q1)
+
+        for j in range(D // P):
+            for h in range(2):
+                nc.vector.tensor_copy(windows[j][:].indirect(offsets[:, h * 16:(h + 1) * 16]), dw0[j][:, h * half:(h + 1) * half])
+        for j in range(D // P):
+            nc.vector.tensor_copy(windows[j][:].indirect(offsets[:, COLS:2 * COLS]), dw1[j][:])
+            nc.sync.dma_start(out[j * P:(j + 1) * P, :], windows[j][:])

@@ -17,159 +17,223 @@ ALU = mybir.AluOpType
 
 P = 128
 PACK = 4
+PER_COLUMN = 16
 CHUNK = 128
-W_PIECE = 1024
-W_ON_VECTOR = 688
-COLS = N // 16
+HALF = 256
+PIECE = 128
+RUN = 4
+
+TABLE_PARTS = [(0, 0, 2048, 1368), (1, 0, 1024, 0), (1, 1024, 2048, 688)]
 
 
 def tile_attend_glch_w_kernel(tc, xT, wT, y, wt, xm, offs, out):
     nc = tc.nc
     with ExitStack() as ctx:
         sb = ctx.enter_context(tc.tile_pool(name="sb", bufs=1))
-        ps_a = ctx.enter_context(tc.psum_pool(name="ps_a", bufs=4))
-        ps_dw = ctx.enter_context(tc.psum_pool(name="ps_dw", bufs=4))
+        ps_a = ctx.enter_context(tc.psum_pool(name="ps_a", bufs=N // CHUNK))
+        ps_dw = ctx.enter_context(tc.psum_pool(name="ps_dw", bufs=D // P))
 
-        def tile(shape, dtype, name):
-            return sb.tile(shape, dtype, name=name, align_bytes=64)
+        def tile(shape, dtype, name, reuse=None):
+            return sb.tile(shape, dtype, name=name, tag=reuse or name, align_bytes=64)
 
-        def quantize(name, grouped, fmt, pieces=1):
+        def by_fours(rows):
+            return rows.rearrange("(p t) c -> p t c", t=PACK)
+
+        def quantize(name, grouped, fmt, reuse=None):
             width = grouped.shape[1] // PACK
-            codes = tile([P, width], U32, name + "_codes")
+            codes = tile([P, width], U32, name + "_codes", reuse)
             scales = tile([P, width], U8, name + "_scales")
-            step = width // pieces
-            for c0 in range(0, width, step):
-                nc.vector.quantize_mx(out=codes[:, c0:c0 + step].bitcast(fmt), scales=scales[:, c0:c0 + step],
-                                      in_=grouped[:, PACK * c0:PACK * (c0 + step)])
+            nc.vector.quantize_mx(out=codes[:].bitcast(fmt), scales=scales[:], in_=grouped[:])
             return codes, scales
 
-        offsets = tile([P, B * COLS], U16, "offsets")
-        nc.sync.dma_start(offsets[:], offs)
+        offsets = tile([P, B * N // PER_COLUMN], U16, "offsets")
         w_rows = wT.rearrange("(p u e) c -> p u e c", u=2, e=2)
-        w_raw = {}
-        for u in range(2):
-            for h in range(T // W_PIECE):
-                w_raw[u, h] = tile([P, 2, W_PIECE], F32, "w_raw%d%d" % (u, h))
-                nc.sync.dma_start(w_raw[u, h][:], w_rows[:, u, :, h * W_PIECE:(h + 1) * W_PIECE])
-        x_raw, y_sb, xm_raw = {}, {}, {}
-        wt_sb = tile([P, B, PACK], F32, "wt_sb")
-        for b in range(B):
-            x_rows = xT[b].rearrange("(p j) r -> p j r", j=PACK)
-            for h in range(2):
-                x_raw[b, h] = tile([P, PACK, R // 2], F32, "x_raw%d%d" % (b, h))
-                nc.sync.dma_start(x_raw[b, h][:], x_rows[:, :, h * (R // 2):(h + 1) * (R // 2)])
-            y_sb[b] = tile([P, PACK, N], F32, "y_sb%d" % b)
-            nc.sync.dma_start(y_sb[b][:], y[b].rearrange("(p t) i -> p t i", t=PACK))
-            if b == 0:
-                nc.sync.dma_start(wt_sb[:], wt.rearrange("b (p t) o -> p b (t o)", t=PACK))
-            xm_raw[b] = tile([P, PACK, D], F32, "xm_raw%d" % b)
-            nc.sync.dma_start(xm_raw[b][:], xm[b].rearrange("(p t) d -> p t d", t=PACK))
+        w_raw = []
+        for part, (u, c0, c1, on_vector) in enumerate(TABLE_PARTS):
+            w_raw.append(tile([P, 2, c1 - c0], F32, "w_raw%d" % part))
+            nc.sync.dma_start(w_raw[part][:], w_rows[:, u, :, c0:c1])
+            if part == 0:
+                nc.sync.dma_start(offsets[:], offs)
+        wt_rows = tile([P, B * 2 * PACK], F32, "wt_rows")
+        wt_sb = wt_rows[:].rearrange("p (b t) -> p b t", b=B)
+        x0_raw = [tile([P, PACK, HALF], F32, "x0_raw%d" % h) for h in range(2)]
+        y0 = tile([P, PACK, N], F32, "y0")
+        xm0_raw = tile([P, PACK, D], F32, "xm0_raw")
+        x1_raw = tile([P, PACK, R], F32, "x1_raw")
+        y1 = tile([P, PACK, N], F32, "y1")
+        xm1_raw = tile([P, PACK, D], F32, "xm1_raw")
+        for h in range(2):
+            nc.sync.dma_start(x0_raw[h][:], by_fours(xT[0])[:, :, h * HALF:(h + 1) * HALF])
+        nc.sync.dma_start(xm0_raw[:, :, :HALF], by_fours(xm[0])[:, :, :HALF])
+        nc.sync.dma_start(y0[:], by_fours(y[0]))
+        nc.sync.dma_start(wt_sb[:, :, :PACK], wt.rearrange("b (p t) o -> p b (t o)", t=PACK))
+        nc.sync.dma_start(x1_raw[:], by_fours(xT[1]))
+        nc.sync.dma_start(xm0_raw[:, :, HALF:], by_fours(xm[0])[:, :, HALF:])
+        nc.sync.dma_start(y1[:], by_fours(y[1]))
+        nc.sync.dma_start(xm1_raw[:], by_fours(xm[1]))
 
         windows = []
         for j in range(D // P):
-            window = tile([P, T], F32, "window%d" % j)
-            nc.vector.memset(window[:], 0.0)
-            windows.append(window)
+            windows.append(tile([P, T], F32, "window%d" % j))
+            (nc.vector if j < 2 else nc.gpsimd).memset(windows[j][:], 0.0)
 
         w_pairs = [tile([P, T * 2], BF16, "w_pairs%d" % u) for u in range(2)]
-        w_picked = [tile([P, N * PACK], BF16, "w_picked%d" % b) for b in range(B)]
+        w_grouped = [tile([P, N * PACK], BF16, "w_grouped%d" % b) for b in range(B)]
 
-        def cast_table(u):
-            for h in range(T // W_PIECE):
-                src = w_raw[u, h][:].rearrange("p e (c i) -> p c e i", i=4)
-                dst = w_pairs[u][:, 2 * h * W_PIECE:2 * (h + 1) * W_PIECE].rearrange("p (c i e) -> p c e i", i=4, e=2)
-                cv = W_ON_VECTOR // 4
-                nc.vector.tensor_copy(dst[:, :cv], src[:, :cv])
-                nc.scalar.activation(dst[:, cv:], src[:, cv:], ACT.Copy)
+        def cast_table(pair):
+            for raw, (u, c0, c1, on_vector) in zip(w_raw, TABLE_PARTS):
+                if u == pair:
+                    src = raw[:].rearrange("p e (c i) -> p c e i", i=RUN)
+                    dst = w_pairs[u][:, 2 * c0:2 * c1].rearrange("p (c i e) -> p c e i", i=RUN, e=2)
+                    split = on_vector // RUN
+                    if on_vector > 0:
+                        nc.vector.tensor_copy(dst[:, :split], src[:, :split])
+                    nc.scalar.activation(dst[:, split:], src[:, split:], ACT.Copy)
+
+        def slots(first, end):
+            return offsets[:, first // PER_COLUMN:end // PER_COLUMN]
 
         def gather(b, u):
-            dst = w_picked[b][:].bitcast(U32).rearrange("p (i u) -> p i u", u=2)
-            nc.vector.tensor_copy(dst[:, :, u], w_pairs[u][:].bitcast(U32).indirect(offsets[:, b * COLS:(b + 1) * COLS]))
+            words = w_grouped[b][:].bitcast(U32).rearrange("p (i u) -> p u i", u=2)
+            nc.vector.tensor_copy(words[:, u, :], w_pairs[u][:].bitcast(U32).indirect(slots(b * N, (b + 1) * N)))
 
-        def cast_x(b):
-            grouped = tile([P, R * PACK], BF16, "x_grouped%d" % b)
+        def cast_x(name, pieces):
+            grouped = tile([P, R * PACK], BF16, name)
             dst = grouped[:].rearrange("p (t m j) -> p m j t", t=PACK, j=PACK)
-            for h in range(2):
-                nc.scalar.copy(dst[:, h * 64:(h + 1) * 64], x_raw[b, h][:].rearrange("p j (m t) -> p m j t", t=PACK))
+            m0 = 0
+            for raw in pieces:
+                count = raw.shape[2] // PACK
+                nc.scalar.copy(dst[:, m0:m0 + count], raw.rearrange("p j (m t) -> p m j t", t=PACK))
+                m0 += count
             return grouped
 
-        def cast_xm(b):
-            grouped = tile([P, D * PACK], BF16, "xm_grouped%d" % b)
-            dst = grouped[:].rearrange("p (c i t) -> p c t i", i=4, t=PACK)
-            src = xm_raw[b][:].rearrange("p t (c i) -> p c t i", i=4)
-            for j in range(4):
-                nc.scalar.copy(dst[:, j * 32:(j + 1) * 32], src[:, j * 32:(j + 1) * 32])
+        def cast_xm(name, raw, reuse=None):
+            grouped = tile([P, raw.shape[2] * PACK], BF16, name, reuse)
+            dst = grouped[:].rearrange("p (c i t) -> p c t i", i=RUN, t=PACK)
+            src = raw.rearrange("p t (c i) -> p c t i", i=RUN)
+            for c0 in range(0, raw.shape[2] // RUN, PIECE // RUN):
+                nc.scalar.copy(dst[:, c0:c0 + PIECE // RUN], src[:, c0:c0 + PIECE // RUN])
             return grouped
 
-        def residual(b, c, x_q, w_q, dst):
+        def scores(c, x_q, w_q):
             cols = slice(c * CHUNK, (c + 1) * CHUNK)
             a_ps = ps_a.tile([P, PACK, CHUNK], F32, name="a_ps")
             for t in range(PACK):
                 rows = slice(t * P, (t + 1) * P)
                 nc.tensor.matmul_mx(out=a_ps[:, t, :], lhsT=x_q[0][:, rows].bitcast(E4M3), lhsT_scale=x_q[1][:, rows],
                                     rhs=w_q[0][:, cols].bitcast(E4M3), rhs_scale=w_q[1][:, cols], start=True, stop=True)
-            nc.vector.tensor_tensor(dst, a_ps[:], y_sb[b][:, :, cols], ALU.subtract)
+            return a_ps
 
-        def second_product(b, xm_q, g_q):
-            res = []
-            for j in range(D // P):
-                rows = slice(j * P, (j + 1) * P)
-                dw_ps = ps_dw.tile([P, N], F32, name="dw_ps")
-                nc.tensor.matmul_mx(out=dw_ps[:], lhsT=xm_q[0][:, rows].bitcast(E4M3), lhsT_scale=xm_q[1][:, rows],
-                                    rhs=g_q[0][:].bitcast(E5M2), rhs_scale=g_q[1][:], start=True, stop=True)
-                dw = tile([P, N], F32, "dw%d%d" % (b, j))
-                nc.scalar.copy(dw[:], dw_ps[:])
-                res.append(dw)
-            return res
+        def tanh_grouped(name, residual):
+            th = tile([P, CHUNK * PACK], F32, name)
+            nc.scalar.activation(th[:].rearrange("p (c i t) -> p c t i", i=2, t=PACK),
+                                 residual[:].rearrange("p t (c i) -> p c t i", i=2), ACT.Tanh)
+            return th
+
+        def chunk_of(g, c):
+            return g[:, c * CHUNK * PACK:(c + 1) * CHUNK * PACK]
+
+        def weigh(engine, g, c, th, b):
+            engine.tensor_tensor(chunk_of(g, c).rearrange("p (i t) -> p i t", t=PACK),
+                                 th[:].rearrange("p (i t) -> p i t", t=PACK),
+                                 wt_sb[:, b:b + 1, :PACK].to_broadcast([P, CHUNK, PACK]), ALU.mult)
+
+        def gradient(j, xm_q, g_q):
+            rows = slice(j * P, (j + 1) * P)
+            dw_ps = ps_dw.tile([P, N], F32, name="dw_ps")
+            nc.tensor.matmul_mx(out=dw_ps[:], lhsT=xm_q[0][:, rows].bitcast(E4M3), lhsT_scale=xm_q[1][:, rows],
+                                rhs=g_q[0][:].bitcast(E5M2), rhs_scale=g_q[1][:], start=True, stop=True)
+            return dw_ps
 
         cast_table(0)
         gather(0, 0)
         gather(1, 0)
         cast_table(1)
         gather(0, 1)
-        w_q0 = quantize("w0", w_picked[0], E4M3)
-        x_q0 = quantize("x0", cast_x(0), E4M3)
+        w0_q = quantize("w0", w_grouped[0], E4M3)
+        x0_q = quantize("x0", cast_x("x0_grouped", [raw[:] for raw in x0_raw]), E4M3)
 
         g0 = tile([P, N * PACK], BF16, "g0")
         th0 = []
         for c in range(N // CHUNK):
-            u0 = tile([P, PACK, CHUNK], F32, "u0%d" % c)
-            residual(0, c, x_q0, w_q0, u0[:])
-            th = tile([P, CHUNK * PACK], F32, "th0%d" % c)
-            nc.scalar.activation(th[:].rearrange("p (c i t) -> p c t i", i=2, t=PACK),
-                                 u0[:].rearrange("p t (c i) -> p c t i", i=2), ACT.Tanh)
-            th0.append(th)
+            residual = tile([P, PACK, CHUNK], F32, "residual0%d" % c)
+            nc.vector.tensor_tensor(residual[:], scores(c, x0_q, w0_q)[:], y0[:, :, c * CHUNK:(c + 1) * CHUNK], ALU.subtract)
+            th0.append(tanh_grouped("th0%d" % c, residual))
         for c in range(N // CHUNK):
-            nc.vector.tensor_tensor(g0[:, c * CHUNK * PACK:(c + 1) * CHUNK * PACK].rearrange("p (i t) -> p i t", t=PACK),
-                                    th0[c][:].rearrange("p (i t) -> p i t", t=PACK),
-                                    wt_sb[:, 0:1, :].to_broadcast([P, CHUNK, PACK]), ALU.mult)
-        xm_q0 = quantize("xm0", cast_xm(0), E4M3)
-        g_q0 = quantize("g0", g0, E5M2)
-        dw0 = second_product(0, xm_q0, g_q0)
+            weigh(nc.vector, g0, c, th0[c], 0)
+
+        xm0_q = (tile([P, D], U32, "xm0_codes"), tile([P, D], U8, "xm0_scales"))
+
+        def quantize_xm0(h, reuse=None):
+            cols = slice(h * HALF, (h + 1) * HALF)
+            grouped = cast_xm("xm0_grouped%d" % h, xm0_raw[:, :, cols], reuse)
+            nc.vector.quantize_mx(out=xm0_q[0][:, cols].bitcast(E4M3), scales=xm0_q[1][:, cols], in_=grouped[:])
+
+        quantize_xm0(0)
+        g0_q = quantize("g0", g0, E5M2)
+        dw0_ps = [gradient(j, xm0_q, g0_q) for j in range(2)]
+
+        dw0 = []
+
+        def copy_out(name, pieces, reuse=None):
+            dw = tile([P, sum(end - first for j, first, end in pieces)], F32, name, reuse)
+            at = 0
+            for j, first, end in pieces:
+                nc.scalar.copy(dw[:, at:at + end - first], dw0_ps[j][:, first:end])
+                dw0.append((j, first, end, dw[:, at:at + end - first]))
+                at += end - first
+
+        copy_out("dw0a", [(0, 0, HALF)])
 
         gather(1, 1)
-        w_q1 = quantize("w1", w_picked[1], E4M3)
-        x_q1 = quantize("x1", cast_x(1), E4M3)
-        g1 = tile([P, N * PACK], BF16, "g1")
-        half = N // 2
-        for h in range(2):
-            u1 = tile([P, PACK, half], F32, "u1%d" % h)
-            for c in range(2):
-                residual(1, 2 * h + c, x_q1, w_q1, u1[:, :, c * CHUNK:(c + 1) * CHUNK])
-            th = tile([P, PACK, half], F32, "th1%d" % h)
-            nc.scalar.activation(th[:], u1[:], ACT.Tanh)
-            g_rows = tile([P, PACK, half], BF16, "g_rows%d" % h)
-            for t in range(PACK):
-                nc.scalar.activation(g_rows[:, t, :], th[:, t, :], ACT.Copy, scale=wt_sb[:, 1, t:t + 1])
-            nc.scalar.copy(g1[:, h * half * PACK:(h + 1) * half * PACK].rearrange("p (c i t) -> p c t i", i=4, t=PACK),
-                           g_rows[:].rearrange("p t (c i) -> p c t i", i=4))
-        xm_q1 = quantize("xm1", cast_xm(1), E4M3)
-        g_q1 = quantize("g1", g1, E5M2, pieces=2)
-        dw1 = second_product(1, xm_q1, g_q1)
+        w1_q = quantize("w1", w_grouped[1], E4M3, reuse="th00")
+        x1_q = quantize("x1", cast_x("x1_grouped", [x1_raw[:, :, r0:r0 + PIECE] for r0 in range(0, R, PIECE)]), E4M3)
+        copy_out("dw0b", [(1, 0, N)], reuse="x1_raw")
 
+        g1 = tile([P, N * PACK], BF16, "g1")
+        residual1 = []
+
+        def subtract1(c):
+            residual1.append(tile([P, PACK, CHUNK], F32, "residual1%d" % c))
+            a_ps = scores(c, x1_q, w1_q)
+            a_sb = tile([P, PACK, CHUNK], F32, "a_sb%d" % c)
+            nc.scalar.copy(a_sb[:], a_ps[:])
+            nc.gpsimd.tensor_tensor(residual1[c][:], a_sb[:], y1[:, :, c * CHUNK:(c + 1) * CHUNK], ALU.subtract)
+
+        subtract1(0)
+        subtract1(1)
+        quantize_xm0(1, reuse="x0_raw0")
+        dw0_ps += [gradient(j, xm0_q, g0_q) for j in range(2, 4)]
+        copy_out("dw0c", [(0, HALF, N), (2, 0, N)], reuse="a_sb1")
+        subtract1(2)
+        subtract1(3)
+
+        last = N // CHUNK - 1
+        for c in range(last):
+            th = tanh_grouped("th1%d" % c, residual1[c])
+            if c == 0:
+                copy_out("dw0d", [(3, 0, HALF)], reuse="residual10")
+            weigh(nc.gpsimd, g1, c, th, 1)
+        xm1_q = quantize("xm1", cast_xm("xm1_grouped", xm1_raw[:]), E4M3)
+
+        th = tile([P, CHUNK * PACK], F32, "th1_last")
+        nc.scalar.activation(th[:], residual1[last][:].rearrange("p t i -> p (t i)"), ACT.Tanh)
+        g_rows = tile([P, PACK, CHUNK], BF16, "g_rows")
+        for t in range(PACK):
+            nc.scalar.activation(g_rows[:, t, :], th[:, t * CHUNK:(t + 1) * CHUNK], ACT.Copy, scale=wt_sb[:, 1, t:t + 1])
+        nc.scalar.copy(chunk_of(g1, last).rearrange("p (c i t) -> p c t i", i=RUN, t=PACK),
+                       g_rows[:].rearrange("p t (c i) -> p c t i", i=RUN))
+        copy_out("dw0e", [(3, HALF, N)], reuse="g_rows")
+
+        g1_q = quantize("g1", g1, E5M2)
+        dw1_ps = [gradient(j, xm1_q, g1_q) for j in range(D // P)]
+        dw1 = []
         for j in range(D // P):
-            for h in range(2):
-                nc.vector.tensor_copy(windows[j][:].indirect(offsets[:, h * 16:(h + 1) * 16]), dw0[j][:, h * half:(h + 1) * half])
+            dw1.append(tile([P, N], F32, "dw1%d" % j))
+            nc.scalar.copy(dw1[j][:], dw1_ps[j][:])
+
+        for j, first, end, dw in dw0:
+            nc.vector.tensor_copy(windows[j][:].indirect(slots(first, end)), dw)
         for j in range(D // P):
-            nc.vector.tensor_copy(windows[j][:].indirect(offsets[:, COLS:2 * COLS]), dw1[j][:])
+            nc.vector.tensor_copy(windows[j][:].indirect(slots(N, 2 * N)), dw1[j][:])
             nc.sync.dma_start(out[j * P:(j + 1) * P, :], windows[j][:])

@@ -47,6 +47,8 @@ def tile_attend_glch_w_kernel(tc, xT, wT, y, wt, xm, offs, out):
             return codes, scales
 
         offsets = tile([P, B * N // PER_COLUMN], U16, "offsets")
+        wt_rows = tile([P, B * 2 * PACK], F32, "wt_rows")
+        wt_sb = wt_rows[:].rearrange("p (b t) -> p b t", b=B)
         w_rows = wT.rearrange("(p u e) c -> p u e c", u=2, e=2)
         w_raw = []
         for part, (u, c0, c1, on_vector) in enumerate(TABLE_PARTS):
@@ -54,31 +56,29 @@ def tile_attend_glch_w_kernel(tc, xT, wT, y, wt, xm, offs, out):
             nc.sync.dma_start(w_raw[part][:], w_rows[:, u, :, c0:c1])
             if part == 0:
                 nc.sync.dma_start(offsets[:], offs)
-        wt_rows = tile([P, B * 2 * PACK], F32, "wt_rows")
-        wt_sb = wt_rows[:].rearrange("p (b t) -> p b t", b=B)
-        x0_raw = [tile([P, PACK, HALF], F32, "x0_raw%d" % h) for h in range(2)]
-        y0 = tile([P, PACK, N], F32, "y0")
-        xm0_raw = tile([P, PACK, D], F32, "xm0_raw")
-        x1_raw = tile([P, PACK, R], F32, "x1_raw")
-        y1 = tile([P, PACK, N], F32, "y1")
-        xm1_raw = tile([P, PACK, D], F32, "xm1_raw")
-        for h in range(2):
-            nc.sync.dma_start(x0_raw[h][:], by_fours(xT[0])[:, :, h * HALF:(h + 1) * HALF])
-        nc.sync.dma_start(xm0_raw[:, :, :HALF], by_fours(xm[0])[:, :, :HALF])
-        nc.sync.dma_start(y0[:], by_fours(y[0]))
+
+        def load(name, rows, first=0, end=512):
+            raw = tile([P, PACK, end - first], F32, name)
+            nc.sync.dma_start(raw[:], by_fours(rows)[:, :, first:end])
+            return raw
+
+        x0_raw = [load("x0_raw%d" % h, xT[0], h * HALF, (h + 1) * HALF) for h in range(2)]
+        xm0a_raw = load("xm0a_raw", xm[0], 0, HALF)
+        y0 = load("y0", y[0])
         nc.sync.dma_start(wt_sb[:, :, :PACK], wt.rearrange("b (p t) o -> p b (t o)", t=PACK))
-        nc.sync.dma_start(x1_raw[:], by_fours(xT[1]))
-        nc.sync.dma_start(xm0_raw[:, :, HALF:], by_fours(xm[0])[:, :, HALF:])
-        nc.sync.dma_start(y1[:], by_fours(y[1]))
-        nc.sync.dma_start(xm1_raw[:], by_fours(xm[1]))
+        x1_raw = load("x1_raw", xT[1])
+        xm0b_raw = load("xm0b_raw", xm[0], HALF, D)
+        y1 = load("y1", y[1])
+        xm1_raw = load("xm1_raw", xm[1])
 
         windows = []
         for j in range(D // P):
             windows.append(tile([P, T], F32, "window%d" % j))
-            (nc.vector if j < 2 else nc.gpsimd).memset(windows[j][:], 0.0)
+            (nc.vector if j < 3 else nc.gpsimd).memset(windows[j][:], 0.0)
 
         w_pairs = [tile([P, T * 2], BF16, "w_pairs%d" % u) for u in range(2)]
-        w_grouped = [tile([P, N * PACK], BF16, "w_grouped%d" % b) for b in range(B)]
+        w0_grouped = tile([P, N * PACK], BF16, "w0_grouped")
+        w1_words = tile([P, 2, N], U32, "w1_words")
 
         def cast_table(pair):
             for raw, (u, c0, c1, on_vector) in zip(w_raw, TABLE_PARTS):
@@ -88,32 +88,41 @@ def tile_attend_glch_w_kernel(tc, xT, wT, y, wt, xm, offs, out):
                     split = on_vector // RUN
                     if on_vector > 0:
                         nc.vector.tensor_copy(dst[:, :split], src[:, :split])
-                    nc.scalar.activation(dst[:, split:], src[:, split:], ACT.Copy)
+                    if on_vector < c1 - c0:
+                        nc.scalar.activation(dst[:, split:], src[:, split:], ACT.Copy)
 
         def slots(first, end):
             return offsets[:, first // PER_COLUMN:end // PER_COLUMN]
 
-        def gather(b, u):
-            words = w_grouped[b][:].bitcast(U32).rearrange("p (i u) -> p u i", u=2)
-            nc.vector.tensor_copy(words[:, u, :], w_pairs[u][:].bitcast(U32).indirect(slots(b * N, (b + 1) * N)))
+        def gather(u):
+            table = w_pairs[u][:].bitcast(U32)
+            words = w0_grouped[:].bitcast(U32).rearrange("p (i u) -> p u i", u=2)
+            nc.vector.tensor_copy(words[:, u, :], table.indirect(slots(0, N)))
+            nc.vector.tensor_copy(w1_words[:, u, :], table.indirect(slots(N, 2 * N)))
 
-        def cast_x(name, pieces):
-            grouped = tile([P, R * PACK], BF16, name)
+        def cast_x(grouped, raw, first):
             dst = grouped[:].rearrange("p (t m j) -> p m j t", t=PACK, j=PACK)
-            m0 = 0
-            for raw in pieces:
-                count = raw.shape[2] // PACK
-                nc.scalar.copy(dst[:, m0:m0 + count], raw.rearrange("p j (m t) -> p m j t", t=PACK))
-                m0 += count
-            return grouped
+            nc.scalar.copy(dst[:, first // PACK:(first + raw.shape[2]) // PACK], raw.rearrange("p j (m t) -> p m j t", t=PACK))
 
-        def cast_xm(name, raw, reuse=None):
-            grouped = tile([P, raw.shape[2] * PACK], BF16, name, reuse)
+        xm_q = [None, None]
+        g_q = []
+        for b in range(B):
+            g_q.append((tile([P, N], U32, "g%d_codes" % b), tile([P, N], U8, "g%d_scales" % b)))
+            nc.gpsimd.memset(g_q[b][0][:, HALF:], 0)
+            nc.gpsimd.memset(g_q[b][1][:, HALF:].bitcast(U32), 0)
+
+        def quantize_g(b, h, g):
+            cols = slice(h * HALF, (h + 1) * HALF)
+            nc.vector.quantize_mx(out=g_q[b][0][:, cols].bitcast(E5M2), scales=g_q[b][1][:, cols], in_=g[:])
+
+        def cast_xm(grouped, raw, first):
             dst = grouped[:].rearrange("p (c i t) -> p c t i", i=RUN, t=PACK)
             src = raw.rearrange("p t (c i) -> p c t i", i=RUN)
-            for c0 in range(0, raw.shape[2] // RUN, PIECE // RUN):
-                nc.scalar.copy(dst[:, c0:c0 + PIECE // RUN], src[:, c0:c0 + PIECE // RUN])
-            return grouped
+            nc.scalar.copy(dst[:, first // RUN:(first + PIECE) // RUN], src[:, first // RUN:(first + PIECE) // RUN])
+
+        def quantize_xm(b, first, grouped):
+            cols = slice(first, first + grouped.shape[1] // PACK)
+            nc.vector.quantize_mx(out=xm_q[b][0][:, cols].bitcast(E4M3), scales=xm_q[b][1][:, cols], in_=grouped[:])
 
         def scores(c, x_q, w_q):
             cols = slice(c * CHUNK, (c + 1) * CHUNK)
@@ -124,116 +133,122 @@ def tile_attend_glch_w_kernel(tc, xT, wT, y, wt, xm, offs, out):
                                     rhs=w_q[0][:, cols].bitcast(E4M3), rhs_scale=w_q[1][:, cols], start=True, stop=True)
             return a_ps
 
-        def tanh_grouped(name, residual):
-            th = tile([P, CHUNK * PACK], F32, name)
+        def tanh_grouped(name, residual, reuse=None):
+            th = tile([P, CHUNK * PACK], F32, name, reuse)
             nc.scalar.activation(th[:].rearrange("p (c i t) -> p c t i", i=2, t=PACK),
                                  residual[:].rearrange("p t (c i) -> p c t i", i=2), ACT.Tanh)
             return th
 
-        def chunk_of(g, c):
-            return g[:, c * CHUNK * PACK:(c + 1) * CHUNK * PACK]
+        def weigh(engine, g, c, th, weights):
+            engine.tensor_tensor(g[:, c * CHUNK * PACK:(c + 1) * CHUNK * PACK].rearrange("p (i t) -> p i t", t=PACK),
+                                 th[:].rearrange("p (i t) -> p i t", t=PACK), weights, ALU.mult)
 
-        def weigh(engine, g, c, th, b):
-            engine.tensor_tensor(chunk_of(g, c).rearrange("p (i t) -> p i t", t=PACK),
-                                 th[:].rearrange("p (i t) -> p i t", t=PACK),
-                                 wt_sb[:, b:b + 1, :PACK].to_broadcast([P, CHUNK, PACK]), ALU.mult)
+        def wt_of(b):
+            return wt_sb[:, b:b + 1, :PACK].to_broadcast([P, CHUNK, PACK])
 
-        def gradient(j, xm_q, g_q):
+        def gradient(b, j):
             rows = slice(j * P, (j + 1) * P)
             dw_ps = ps_dw.tile([P, N], F32, name="dw_ps")
-            nc.tensor.matmul_mx(out=dw_ps[:], lhsT=xm_q[0][:, rows].bitcast(E4M3), lhsT_scale=xm_q[1][:, rows],
-                                rhs=g_q[0][:].bitcast(E5M2), rhs_scale=g_q[1][:], start=True, stop=True)
-            return dw_ps
+            nc.tensor.matmul_mx(out=dw_ps[:], lhsT=xm_q[b][0][:, rows].bitcast(E4M3), lhsT_scale=xm_q[b][1][:, rows],
+                                rhs=g_q[b][0][:].bitcast(E5M2), rhs_scale=g_q[b][1][:], start=True, stop=True)
+            return b, j, dw_ps
+
+        def copy_out(product, first, end, reuse=None, dw=None):
+            b, j, dw_ps = product
+            if dw is None:
+                dw = tile([P, end - first], F32, "dw%d%d_%d" % (b, j, first), reuse)
+            nc.scalar.copy(dw[:], dw_ps[:, first:end])
+            return b, j, first, end, dw
+
+        def scatter(piece):
+            b, j, first, end, dw = piece
+            nc.vector.tensor_copy(windows[j][:].indirect(slots(b * N + first, b * N + end)), dw[:])
+            if b == B - 1 and end == N:
+                nc.sync.dma_start(out[j * P:(j + 1) * P, :], windows[j][:])
+
+        def copy_scores(name, a_ps, reuse=None):
+            a_sb = tile([P, PACK, CHUNK], F32, "a_" + name, reuse)
+            nc.scalar.copy(a_sb[:], a_ps[:])
+            return a_sb
+
+        def subtract(engine, name, a, y_sb, c, reuse=None):
+            residual = tile([P, PACK, CHUNK], F32, "residual" + name, reuse)
+            engine.tensor_tensor(residual[:], a[:], y_sb[:, :, c * CHUNK:(c + 1) * CHUNK], ALU.subtract)
+            return residual
 
         cast_table(0)
-        gather(0, 0)
-        gather(1, 0)
+        gather(0)
         cast_table(1)
-        gather(0, 1)
-        w0_q = quantize("w0", w_grouped[0], E4M3)
-        x0_q = quantize("x0", cast_x("x0_grouped", [raw[:] for raw in x0_raw]), E4M3)
+        gather(1)
+        w0_q = quantize("w0", w0_grouped, E4M3)
+        x0_grouped = tile([P, R * PACK], BF16, "x0_grouped")
+        for h in range(2):
+            cast_x(x0_grouped, x0_raw[h][:], h * HALF)
+        x0_q = quantize("x0", x0_grouped, E4M3)
+        after_x0 = tile([P, (N + HALF) * PACK], BF16, "after_x0", "x0_raw1")
+        w1_grouped = after_x0[:, :N * PACK]
+        for h in range(2):
+            nc.scalar.copy(w1_grouped[:].bitcast(U32).rearrange("p (i u) -> p i u", u=2)[:, h * HALF:(h + 1) * HALF],
+                           w1_words[:].rearrange("p u i -> p i u")[:, h * HALF:(h + 1) * HALF])
+        w1_q = quantize("w1", w1_grouped, E4M3)
+        xm0a_grouped = after_x0[:, N * PACK:]
+        for h in range(2):
+            cast_xm(xm0a_grouped, xm0a_raw[:], h * PIECE)
 
-        g0 = tile([P, N * PACK], BF16, "g0")
-        th0 = []
-        for c in range(N // CHUNK):
-            residual = tile([P, PACK, CHUNK], F32, "residual0%d" % c)
-            nc.vector.tensor_tensor(residual[:], scores(c, x0_q, w0_q)[:], y0[:, :, c * CHUNK:(c + 1) * CHUNK], ALU.subtract)
-            th0.append(tanh_grouped("th0%d" % c, residual))
-        for c in range(N // CHUNK):
-            weigh(nc.vector, g0, c, th0[c], 0)
-
-        xm0_q = (tile([P, D], U32, "xm0_codes"), tile([P, D], U8, "xm0_scales"))
-
-        def quantize_xm0(h, reuse=None):
-            cols = slice(h * HALF, (h + 1) * HALF)
-            grouped = cast_xm("xm0_grouped%d" % h, xm0_raw[:, :, cols], reuse)
-            nc.vector.quantize_mx(out=xm0_q[0][:, cols].bitcast(E4M3), scales=xm0_q[1][:, cols], in_=grouped[:])
-
-        quantize_xm0(0)
-        g0_q = quantize("g0", g0, E5M2)
-        dw0_ps = [gradient(j, xm0_q, g0_q) for j in range(2)]
-
-        dw0 = []
-
-        def copy_out(name, pieces, reuse=None):
-            dw = tile([P, sum(end - first for j, first, end in pieces)], F32, name, reuse)
-            at = 0
-            for j, first, end in pieces:
-                nc.scalar.copy(dw[:, at:at + end - first], dw0_ps[j][:, first:end])
-                dw0.append((j, first, end, dw[:, at:at + end - first]))
-                at += end - first
-
-        copy_out("dw0a", [(0, 0, HALF)])
-
-        gather(1, 1)
-        w1_q = quantize("w1", w_grouped[1], E4M3, reuse="th00")
-        x1_q = quantize("x1", cast_x("x1_grouped", [x1_raw[:, :, r0:r0 + PIECE] for r0 in range(0, R, PIECE)]), E4M3)
-        copy_out("dw0b", [(1, 0, N)], reuse="x1_raw")
-
-        g1 = tile([P, N * PACK], BF16, "g1")
-        residual1 = []
-
-        def subtract1(c):
-            residual1.append(tile([P, PACK, CHUNK], F32, "residual1%d" % c))
-            a_ps = scores(c, x1_q, w1_q)
-            a_sb = tile([P, PACK, CHUNK], F32, "a_sb%d" % c)
-            nc.scalar.copy(a_sb[:], a_ps[:])
-            nc.gpsimd.tensor_tensor(residual1[c][:], a_sb[:], y1[:, :, c * CHUNK:(c + 1) * CHUNK], ALU.subtract)
-
-        subtract1(0)
-        subtract1(1)
-        quantize_xm0(1, reuse="x0_raw0")
-        dw0_ps += [gradient(j, xm0_q, g0_q) for j in range(2, 4)]
-        copy_out("dw0c", [(0, HALF, N), (2, 0, N)], reuse="a_sb1")
-        subtract1(2)
-        subtract1(3)
-
-        last = N // CHUNK - 1
-        for c in range(last):
-            th = tanh_grouped("th1%d" % c, residual1[c])
-            if c == 0:
-                copy_out("dw0d", [(3, 0, HALF)], reuse="residual10")
-            weigh(nc.gpsimd, g1, c, th, 1)
-        xm1_q = quantize("xm1", cast_xm("xm1_grouped", xm1_raw[:]), E4M3)
-
-        th = tile([P, CHUNK * PACK], F32, "th1_last")
-        nc.scalar.activation(th[:], residual1[last][:].rearrange("p t i -> p (t i)"), ACT.Tanh)
-        g_rows = tile([P, PACK, CHUNK], BF16, "g_rows")
-        for t in range(PACK):
-            nc.scalar.activation(g_rows[:, t, :], th[:, t * CHUNK:(t + 1) * CHUNK], ACT.Copy, scale=wt_sb[:, 1, t:t + 1])
-        nc.scalar.copy(chunk_of(g1, last).rearrange("p (c i t) -> p c t i", i=RUN, t=PACK),
-                       g_rows[:].rearrange("p t (c i) -> p c t i", i=RUN))
-        copy_out("dw0e", [(3, HALF, N)], reuse="g_rows")
-
-        g1_q = quantize("g1", g1, E5M2)
-        dw1_ps = [gradient(j, xm1_q, g1_q) for j in range(D // P)]
-        dw1 = []
-        for j in range(D // P):
-            dw1.append(tile([P, N], F32, "dw1%d" % j))
-            nc.scalar.copy(dw1[j][:], dw1_ps[j][:])
-
-        for j, first, end, dw in dw0:
-            nc.vector.tensor_copy(windows[j][:].indirect(slots(first, end)), dw)
-        for j in range(D // P):
-            nc.vector.tensor_copy(windows[j][:].indirect(slots(N, 2 * N)), dw1[j][:])
-            nc.sync.dma_start(out[j * P:(j + 1) * P, :], windows[j][:])
+        res0 = [subtract(nc.vector, "0%d" % c, scores(c, x0_q, w0_q), y0, c) for c in range(4)]
+        th0 = [tanh_grouped("th0%d" % c, res0[c]) for c in range(4)]
+        g0 = [tile([P, HALF * PACK], BF16, "g0%d" % h) for h in range(2)]
+        for c in range(2):
+            weigh(nc.vector, g0[0], c, th0[c], wt_of(0))
+        xm_q[0] = (tile([P, D], U32, "xm0_codes", "th00"), tile([P, D], U8, "xm0_scales"))
+        quantize_xm(0, 0, xm0a_grouped)
+        quantize_g(0, 0, g0[0])
+        first = gradient(0, 0)
+        for c in range(2):
+            weigh(nc.vector, g0[1], c, th0[2 + c], wt_of(0))
+        quantize_g(0, 1, g0[1])
+        prod = [gradient(0, j) for j in (1, 0)]
+        x1_grouped = tile([P, R * PACK], BF16, "x1_grouped")
+        for r0 in range(0, R, PIECE):
+            cast_x(x1_grouped, x1_raw[:, :, r0:r0 + PIECE], r0)
+        x1_q = quantize("x1", x1_grouped, E4M3)
+        after_x1 = tile([P, 3 * HALF], F32, "after_x1", "x1_raw")
+        scatter(copy_out(first, 0, HALF, dw=after_x1[:, :HALF]))
+        xm0b_grouped = after_x1[:, HALF:].bitcast(BF16)
+        for h in range(2):
+            cast_xm(xm0b_grouped, xm0b_raw[:], h * PIECE)
+        quantize_xm(0, HALF, xm0b_grouped)
+        scatter(copy_out(prod[0], 0, N, "xm0b_raw"))
+        a1 = [scores(c, x1_q, w1_q) for c in range(4)]
+        a_sb = [copy_scores("1%d" % c, a1[c]) for c in range(2)]
+        res1 = [subtract(nc.gpsimd, "1%d" % c, a_sb[c], y1, c) for c in range(2)]
+        scatter(copy_out(prod[1], HALF, N))
+        weights1 = tile([P, CHUNK, PACK], F32, "weights1", "x1_grouped")
+        nc.scalar.copy(weights1[:], wt_of(1))
+        prod = [gradient(0, j) for j in range(2, 4)]
+        th1 = [tanh_grouped("th1%d" % c, res1[c]) for c in range(2)]
+        scatter(copy_out(prod[0], 0, N))
+        g1 = [tile([P, HALF * PACK], BF16, "g10")]
+        for c in range(2):
+            weigh(nc.gpsimd, g1[0], c, th1[c], weights1[:])
+        a_sb += [copy_scores("1%d" % c, a1[c]) for c in range(2, 4)]
+        xm1_grouped = tile([P, D * PACK], BF16, "xm1_grouped")
+        for c0 in range(0, D, PIECE):
+            cast_xm(xm1_grouped, xm1_raw[:], c0)
+        xm_q[1] = (tile([P, D], U32, "xm1_codes", "th10"), tile([P, D], U8, "xm1_scales"))
+        quantize_xm(1, 0, xm1_grouped)
+        quantize_g(1, 0, g1[0])
+        scatter(copy_out(prod[1], 0, N, "th11"))
+        res1 += [subtract(nc.gpsimd, "12", a_sb[2], y1, 2, "g10"), subtract(nc.gpsimd, "13", a_sb[3], y1, 3, "xm1_grouped")]
+        prod = [gradient(1, j) for j in range(3)]
+        scatter(copy_out(prod[0], 0, HALF))
+        scatter(copy_out(prod[1], 0, HALF))
+        th1 += [tanh_grouped("th1%d" % c, res1[c]) for c in range(2, 4)]
+        g1.append(tile([P, HALF * PACK], BF16, "g11"))
+        for c in range(2):
+            weigh(nc.gpsimd, g1[1], c, th1[2 + c], weights1[:])
+        quantize_g(1, 1, g1[1])
+        scatter(copy_out(prod[2], 0, HALF, "th13"))
+        for j in range(3):
+            scatter(copy_out(gradient(1, j), HALF, N))
+        scatter(copy_out(gradient(1, 3), 0, N))

@@ -21,6 +21,7 @@ PER_COLUMN = 16
 CHUNK = 128
 HALF = 256
 PIECE = 128
+X0_ON_VECTOR = 152
 RUN = 4
 
 TABLE_PARTS = [(0, 0, 2048, 1368), (1, 0, 1024, 0), (1, 1024, 2048, 688)]
@@ -62,7 +63,9 @@ def tile_attend_glch_w_kernel(tc, xT, wT, y, wt, xm, offs, out):
             nc.sync.dma_start(raw[:], by_fours(rows)[:, :, first:end])
             return raw
 
-        x0_raw = [load("x0_raw%d" % h, xT[0], h * HALF, (h + 1) * HALF) for h in range(2)]
+        w1_words = tile([P, N + PACK * R], F32, "w1_words")
+        x0_raw = w1_words[:, N:].rearrange("p (j r) -> p j r", j=PACK)
+        nc.sync.dma_start(x0_raw, by_fours(xT[0]))
         xm0a_raw = load("xm0a_raw", xm[0], 0, HALF)
         y0 = load("y0", y[0])
         nc.sync.dma_start(wt_sb[:, :, :PACK], wt.rearrange("b (p t) o -> p b (t o)", t=PACK))
@@ -78,7 +81,6 @@ def tile_attend_glch_w_kernel(tc, xT, wT, y, wt, xm, offs, out):
 
         w_pairs = [tile([P, T * 2], BF16, "w_pairs%d" % u) for u in range(2)]
         w0_grouped = tile([P, N * PACK], BF16, "w0_grouped")
-        w1_words = tile([P, 2, N], U32, "w1_words")
 
         def cast_table(pair):
             for raw, (u, c0, c1, on_vector) in zip(w_raw, TABLE_PARTS):
@@ -94,15 +96,18 @@ def tile_attend_glch_w_kernel(tc, xT, wT, y, wt, xm, offs, out):
         def slots(first, end):
             return offsets[:, first // PER_COLUMN:end // PER_COLUMN]
 
-        def gather(u):
+        def gather0(u):
             table = w_pairs[u][:].bitcast(U32)
             words = w0_grouped[:].bitcast(U32).rearrange("p (i u) -> p u i", u=2)
             nc.vector.tensor_copy(words[:, u, :], table.indirect(slots(0, N)))
-            nc.vector.tensor_copy(w1_words[:, u, :], table.indirect(slots(N, 2 * N)))
 
-        def cast_x(grouped, raw, first):
+        def gather1(u):
+            table = w_pairs[u][:].bitcast(U32)
+            nc.vector.tensor_copy(w1_words[:, u * N:(u + 1) * N].bitcast(U32), table.indirect(slots(N, 2 * N)))
+
+        def cast_x(grouped, raw, first, copy=nc.scalar.copy):
             dst = grouped[:].rearrange("p (t m j) -> p m j t", t=PACK, j=PACK)
-            nc.scalar.copy(dst[:, first // PACK:(first + raw.shape[2]) // PACK], raw.rearrange("p j (m t) -> p m j t", t=PACK))
+            copy(dst[:, first // PACK:(first + raw.shape[2]) // PACK], raw.rearrange("p j (m t) -> p m j t", t=PACK))
 
         xm_q = [None, None]
         g_q = []
@@ -166,9 +171,8 @@ def tile_attend_glch_w_kernel(tc, xT, wT, y, wt, xm, offs, out):
             if b == B - 1 and end == N:
                 nc.sync.dma_start(out[j * P:(j + 1) * P, :], windows[j][:])
 
-        def copy_scores(name, a_ps, reuse=None):
-            a_sb = tile([P, PACK, CHUNK], F32, "a_" + name, reuse)
-            nc.scalar.copy(a_sb[:], a_ps[:])
+        def copy_scores(a_sb, a_ps):
+            nc.scalar.copy(a_sb, a_ps[:])
             return a_sb
 
         def subtract(engine, name, a, y_sb, c, reuse=None):
@@ -177,23 +181,25 @@ def tile_attend_glch_w_kernel(tc, xT, wT, y, wt, xm, offs, out):
             return residual
 
         cast_table(0)
-        gather(0)
+        gather0(0)
+        gather1(0)
         cast_table(1)
-        gather(1)
+        gather0(1)
         w0_q = quantize("w0", w0_grouped, E4M3)
         x0_grouped = tile([P, R * PACK], BF16, "x0_grouped")
-        for h in range(2):
-            cast_x(x0_grouped, x0_raw[h][:], h * HALF)
+        cast_x(x0_grouped, x0_raw[:, :, :R - X0_ON_VECTOR], 0)
+        cast_x(x0_grouped, x0_raw[:, :, R - X0_ON_VECTOR:], R - X0_ON_VECTOR, nc.vector.tensor_copy)
         x0_q = quantize("x0", x0_grouped, E4M3)
-        after_x0 = tile([P, (N + HALF) * PACK], BF16, "after_x0", "x0_raw1")
-        w1_grouped = after_x0[:, :N * PACK]
-        for h in range(2):
-            nc.scalar.copy(w1_grouped[:].bitcast(U32).rearrange("p (i u) -> p i u", u=2)[:, h * HALF:(h + 1) * HALF],
-                           w1_words[:].rearrange("p u i -> p i u")[:, h * HALF:(h + 1) * HALF])
-        w1_q = quantize("w1", w1_grouped, E4M3)
-        xm0a_grouped = after_x0[:, N * PACK:]
+        gather1(1)
+        xm0a_grouped = tile([P, HALF * PACK], BF16, "xm0a_grouped")
         for h in range(2):
             cast_xm(xm0a_grouped, xm0a_raw[:], h * PIECE)
+        w1_grouped = tile([P, N * PACK], BF16, "w1_grouped")
+        nc.scalar.copy(w1_grouped[:].bitcast(U32).rearrange("p (i u) -> p i u", u=2)[:, :HALF],
+                       w1_words[:, :2 * N].bitcast(U32).rearrange("p (u i) -> p i u", u=2)[:, :HALF])
+        nc.gpsimd.tensor_scalar(w1_grouped[:].rearrange("p (i u e) -> p i u e", u=2, e=2)[:, HALF:],
+                                w1_words[:, :2 * N].bitcast(BF16).rearrange("p (u i e) -> p i u e", u=2, e=2)[:, HALF:],
+                                1.0, 0.0, ALU.mult, ALU.add)
 
         res0 = [subtract(nc.vector, "0%d" % c, scores(c, x0_q, w0_q), y0, c) for c in range(4)]
         th0 = [tanh_grouped("th0%d" % c, res0[c]) for c in range(4)]
@@ -206,8 +212,9 @@ def tile_attend_glch_w_kernel(tc, xT, wT, y, wt, xm, offs, out):
         first = gradient(0, 0)
         for c in range(2):
             weigh(nc.vector, g0[1], c, th0[2 + c], wt_of(0))
+        w1_q = quantize("w1", w1_grouped, E4M3, "th02")
         quantize_g(0, 1, g0[1])
-        prod = [gradient(0, j) for j in (1, 0)]
+        prod = [gradient(0, j) for j in (0, 1)][::-1]
         x1_grouped = tile([P, R * PACK], BF16, "x1_grouped")
         for r0 in range(0, R, PIECE):
             cast_x(x1_grouped, x1_raw[:, :, r0:r0 + PIECE], r0)
@@ -218,20 +225,22 @@ def tile_attend_glch_w_kernel(tc, xT, wT, y, wt, xm, offs, out):
         for h in range(2):
             cast_xm(xm0b_grouped, xm0b_raw[:], h * PIECE)
         quantize_xm(0, HALF, xm0b_grouped)
-        scatter(copy_out(prod[0], 0, N, "xm0b_raw"))
-        a1 = [scores(c, x1_q, w1_q) for c in range(4)]
-        a_sb = [copy_scores("1%d" % c, a1[c]) for c in range(2)]
-        res1 = [subtract(nc.gpsimd, "1%d" % c, a_sb[c], y1, c) for c in range(2)]
-        scatter(copy_out(prod[1], HALF, N))
+        after_xm0 = tile([P, 3 * HALF + PACK * N], F32, "after_xm0", "xm0b_raw")
+        scatter(copy_out(prod[1], HALF, N, dw=after_xm0[:, :HALF]))
+        scatter(copy_out(prod[0], 0, N, dw=after_xm0[:, HALF:3 * HALF]))
+        a1_sb = after_xm0[:, 3 * HALF:].rearrange("p (c t i) -> p c t i", t=PACK, i=CHUNK)
         weights1 = tile([P, CHUNK, PACK], F32, "weights1", "x1_grouped")
-        nc.scalar.copy(weights1[:], wt_of(1))
+        nc.gpsimd.tensor_scalar(weights1[:], wt_of(1), 1.0, 0.0, ALU.mult, ALU.add)
+        a1 = [scores(c, x1_q, w1_q) for c in range(4)]
+        a_sb = [copy_scores(a1_sb[:, c], a1[c]) for c in range(2)]
+        res1 = [subtract(nc.gpsimd, "1%d" % c, a_sb[c], y1, c) for c in range(2)]
         prod = [gradient(0, j) for j in range(2, 4)]
         th1 = [tanh_grouped("th1%d" % c, res1[c]) for c in range(2)]
         scatter(copy_out(prod[0], 0, N))
         g1 = [tile([P, HALF * PACK], BF16, "g10")]
         for c in range(2):
             weigh(nc.gpsimd, g1[0], c, th1[c], weights1[:])
-        a_sb += [copy_scores("1%d" % c, a1[c]) for c in range(2, 4)]
+        a_sb += [copy_scores(a1_sb[:, c], a1[c]) for c in range(2, 4)]
         xm1_grouped = tile([P, D * PACK], BF16, "xm1_grouped")
         for c0 in range(0, D, PIECE):
             cast_xm(xm1_grouped, xm1_raw[:], c0)

@@ -216,12 +216,12 @@ def tile_attend_glch_w_kernel(tc, xT, wT, y, wt, xm, offs, out):
         quantize_g(0, 1, g0[1])
         prod = [gradient(0, j) for j in (0, 1)][::-1]
         x1_grouped = tile([P, R * PACK], BF16, "x1_grouped")
-        for r0 in range(0, R, PIECE):
+        cast_x(x1_grouped, x1_raw[:, :, :HALF], 0)
+        scatter(copy_out(first, 0, HALF, dw=x1_raw[:, 0, :HALF]))
+        for r0 in range(HALF, R, PIECE):
             cast_x(x1_grouped, x1_raw[:, :, r0:r0 + PIECE], r0)
-        x1_q = quantize("x1", x1_grouped, E4M3)
-        after_x1 = tile([P, 3 * HALF], F32, "after_x1", "x1_raw")
-        scatter(copy_out(first, 0, HALF, dw=after_x1[:, :HALF]))
-        xm0b_grouped = after_x1[:, HALF:].bitcast(BF16)
+        x1_q = quantize("x1", x1_grouped, E4M3, "g01")
+        xm0b_grouped = x1_raw[:, 1, :].bitcast(BF16)
         for h in range(2):
             cast_xm(xm0b_grouped, xm0b_raw[:], h * PIECE)
         quantize_xm(0, HALF, xm0b_grouped)

@@ -21,10 +21,8 @@ PER_COLUMN = 16
 CHUNK = 128
 HALF = 256
 PIECE = 128
-X0_ON_VECTOR = 152
+X0_ON_VECTOR = 200
 RUN = 4
-
-TABLE_PARTS = [(0, 0, 2048, 1368), (1, 0, 1024, 0), (1, 1024, 2048, 688)]
 
 
 def tile_attend_glch_w_kernel(tc, xT, wT, y, wt, xm, offs, out):
@@ -50,12 +48,11 @@ def tile_attend_glch_w_kernel(tc, xT, wT, y, wt, xm, offs, out):
         offsets = tile([P, B * N // PER_COLUMN], U16, "offsets")
         wt_rows = tile([P, B * 2 * PACK], F32, "wt_rows")
         wt_sb = wt_rows[:].rearrange("p (b t) -> p b t", b=B)
-        w_rows = wT.rearrange("(p u e) c -> p u e c", u=2, e=2)
-        w_raw = []
-        for part, (u, c0, c1, on_vector) in enumerate(TABLE_PARTS):
-            w_raw.append(tile([P, 2, c1 - c0], F32, "w_raw%d" % part))
-            nc.sync.dma_start(w_raw[part][:], w_rows[:, u, :, c0:c1])
-            if part == 0:
+        planes = []
+        for t in range(PACK):
+            planes.append(tile([P, T], F32, "plane%d" % t))
+            nc.sync.dma_start(planes[t][:], by_fours(wT)[:, t, :])
+            if t == 0:
                 nc.sync.dma_start(offsets[:], offs)
 
         def load(name, rows, first=0, end=512):
@@ -63,8 +60,8 @@ def tile_attend_glch_w_kernel(tc, xT, wT, y, wt, xm, offs, out):
             nc.sync.dma_start(raw[:], by_fours(rows)[:, :, first:end])
             return raw
 
-        w1_words = tile([P, N + PACK * R], F32, "w1_words")
-        x0_raw = w1_words[:, N:].rearrange("p (j r) -> p j r", j=PACK)
+        w1_late = tile([P, N + PACK * R], F32, "w1_late")
+        x0_raw = w1_late[:, N:].rearrange("p (j r) -> p j r", j=PACK)
         nc.sync.dma_start(x0_raw, by_fours(xT[0]))
         xm0a_raw = load("xm0a_raw", xm[0], 0, HALF)
         y0 = load("y0", y[0])
@@ -77,44 +74,38 @@ def tile_attend_glch_w_kernel(tc, xT, wT, y, wt, xm, offs, out):
         windows = []
         for j in range(D // P):
             windows.append(tile([P, T], F32, "window%d" % j))
-            (nc.vector if j < 3 else nc.gpsimd).memset(windows[j][:], 0.0)
+            nc.vector.memset(windows[j][:], 0.0)
 
-        w_pairs = [tile([P, T * 2], BF16, "w_pairs%d" % u) for u in range(2)]
-        w0_grouped = tile([P, N * PACK], BF16, "w0_grouped")
-
-        def cast_table(pair):
-            for raw, (u, c0, c1, on_vector) in zip(w_raw, TABLE_PARTS):
-                if u == pair:
-                    src = raw[:].rearrange("p e (c i) -> p c e i", i=RUN)
-                    dst = w_pairs[u][:, 2 * c0:2 * c1].rearrange("p (c i e) -> p c e i", i=RUN, e=2)
-                    split = on_vector // RUN
-                    if on_vector > 0:
-                        nc.vector.tensor_copy(dst[:, :split], src[:, :split])
-                    if on_vector < c1 - c0:
-                        nc.scalar.activation(dst[:, split:], src[:, split:], ACT.Copy)
+        w_grouped = [tile([P, N * PACK], BF16, "w0_grouped")]
+        early = [tile([P, 2, N], BF16, "w%d_early" % b) for b in range(B)]
+        late = w1_late[:, :2 * N].rearrange("p (e i) -> p e i", e=2)
 
         def slots(first, end):
             return offsets[:, first // PER_COLUMN:end // PER_COLUMN]
 
-        def gather0(u):
-            table = w_pairs[u][:].bitcast(U32)
-            words = w0_grouped[:].bitcast(U32).rearrange("p (i u) -> p u i", u=2)
-            nc.vector.tensor_copy(words[:, u, :], table.indirect(slots(0, N)))
-
-        def gather1(u):
-            table = w_pairs[u][:].bitcast(U32)
-            nc.vector.tensor_copy(w1_words[:, u * N:(u + 1) * N].bitcast(U32), table.indirect(slots(N, 2 * N)))
+        def gather(b, t):
+            if t < 2:
+                dst = early[b][:, t, :]
+            elif b == 0:
+                dst = w_grouped[0][:].rearrange("p (i t) -> p t i", t=PACK)[:, t, :]
+            else:
+                dst = late[:, t - 2, :]
+            nc.vector.tensor_copy(dst, planes[t][:].indirect(slots(b * N, (b + 1) * N)))
 
         def cast_x(grouped, raw, first, copy=nc.scalar.copy):
             dst = grouped[:].rearrange("p (t m j) -> p m j t", t=PACK, j=PACK)
             copy(dst[:, first // PACK:(first + raw.shape[2]) // PACK], raw.rearrange("p j (m t) -> p m j t", t=PACK))
 
-        xm_q = [None, None]
+        xm_q = {}
         g_q = []
-        for b in range(B):
-            g_q.append((tile([P, N], U32, "g%d_codes" % b), tile([P, N], U8, "g%d_scales" % b)))
-            nc.gpsimd.memset(g_q[b][0][:, HALF:], 0)
-            nc.gpsimd.memset(g_q[b][1][:, HALF:].bitcast(U32), 0)
+
+        def zero_second_half(words, engine):
+            g_q.append((words[:, :N], words[:, N:].bitcast(U8)))
+            engine.memset(g_q[-1][0][:, HALF:], 0)
+            engine.memset(g_q[-1][1][:, HALF:].bitcast(U32), 0)
+
+        zero_second_half(tile([P, N + N // PACK], U32, "g0_quantised"), nc.gpsimd)
+        zero_second_half(tile([P, N + N // PACK], U32, "g1_quantised"), nc.vector)
 
         def quantize_g(b, h, g):
             cols = slice(h * HALF, (h + 1) * HALF)
@@ -125,9 +116,8 @@ def tile_attend_glch_w_kernel(tc, xT, wT, y, wt, xm, offs, out):
             src = raw.rearrange("p t (c i) -> p c t i", i=RUN)
             nc.scalar.copy(dst[:, first // RUN:(first + PIECE) // RUN], src[:, first // RUN:(first + PIECE) // RUN])
 
-        def quantize_xm(b, first, grouped):
-            cols = slice(first, first + grouped.shape[1] // PACK)
-            nc.vector.quantize_mx(out=xm_q[b][0][:, cols].bitcast(E4M3), scales=xm_q[b][1][:, cols], in_=grouped[:])
+        def quantize_xm(b, first, grouped, reuse=None):
+            xm_q[b, first // HALF] = quantize("xm%d%d" % (b, first // HALF), grouped, E4M3, reuse)
 
         def scores(c, x_q, w_q):
             cols = slice(c * CHUNK, (c + 1) * CHUNK)
@@ -138,8 +128,9 @@ def tile_attend_glch_w_kernel(tc, xT, wT, y, wt, xm, offs, out):
                                     rhs=w_q[0][:, cols].bitcast(E4M3), rhs_scale=w_q[1][:, cols], start=True, stop=True)
             return a_ps
 
-        def tanh_grouped(name, residual, reuse=None):
-            th = tile([P, CHUNK * PACK], F32, name, reuse)
+        def tanh_grouped(name, residual, th=None):
+            if th is None:
+                th = tile([P, CHUNK * PACK], F32, name)
             nc.scalar.activation(th[:].rearrange("p (c i t) -> p c t i", i=2, t=PACK),
                                  residual[:].rearrange("p t (c i) -> p c t i", i=2), ACT.Tanh)
             return th
@@ -152,9 +143,10 @@ def tile_attend_glch_w_kernel(tc, xT, wT, y, wt, xm, offs, out):
             return wt_sb[:, b:b + 1, :PACK].to_broadcast([P, CHUNK, PACK])
 
         def gradient(b, j):
-            rows = slice(j * P, (j + 1) * P)
+            rows = slice(j % 2 * P, (j % 2 + 1) * P)
+            codes, scales = xm_q[b, j // 2]
             dw_ps = ps_dw.tile([P, N], F32, name="dw_ps")
-            nc.tensor.matmul_mx(out=dw_ps[:], lhsT=xm_q[b][0][:, rows].bitcast(E4M3), lhsT_scale=xm_q[b][1][:, rows],
+            nc.tensor.matmul_mx(out=dw_ps[:], lhsT=codes[:, rows].bitcast(E4M3), lhsT_scale=scales[:, rows],
                                 rhs=g_q[b][0][:].bitcast(E5M2), rhs_scale=g_q[b][1][:], start=True, stop=True)
             return b, j, dw_ps
 
@@ -175,30 +167,35 @@ def tile_attend_glch_w_kernel(tc, xT, wT, y, wt, xm, offs, out):
             nc.scalar.copy(a_sb, a_ps[:])
             return a_sb
 
-        def subtract(engine, name, a, y_sb, c, reuse=None):
-            residual = tile([P, PACK, CHUNK], F32, "residual" + name, reuse)
+        def subtract(engine, name, a, y_sb, c, residual=None):
+            if residual is None:
+                residual = tile([P, PACK, CHUNK], F32, "residual" + name)
             engine.tensor_tensor(residual[:], a[:], y_sb[:, :, c * CHUNK:(c + 1) * CHUNK], ALU.subtract)
             return residual
 
-        cast_table(0)
-        gather0(0)
-        gather1(0)
-        cast_table(1)
-        gather0(1)
-        w0_q = quantize("w0", w0_grouped, E4M3)
+        gather(0, 0)
+        gather(1, 0)
+        gather(0, 1)
+        plane1_bf = tile([P, T], BF16, "plane1_bf")
+        nc.scalar.activation(plane1_bf[:], planes[1][:], ACT.Copy)
+        nc.scalar.activation(early[1][:, 1, :HALF], plane1_bf[:].indirect(slots(N, N + HALF)), ACT.Copy)
+        nc.vector.tensor_copy(early[1][:, 1, HALF:], planes[1][:].indirect(slots(N + HALF, 2 * N)))
+        nc.scalar.copy(w_grouped[0][:].rearrange("p (i t) -> p i t", t=PACK)[:, :, :2], early[0][:].rearrange("p e i -> p i e"))
+        gather(0, 2)
+        gather(1, 2)
+        gather(0, 3)
         x0_grouped = tile([P, R * PACK], BF16, "x0_grouped")
         cast_x(x0_grouped, x0_raw[:, :, :R - X0_ON_VECTOR], 0)
         cast_x(x0_grouped, x0_raw[:, :, R - X0_ON_VECTOR:], R - X0_ON_VECTOR, nc.vector.tensor_copy)
+        w0_q = quantize("w0", w_grouped[0], E4M3)
         x0_q = quantize("x0", x0_grouped, E4M3)
-        gather1(1)
+        gather(1, 3)
         xm0a_grouped = tile([P, HALF * PACK], BF16, "xm0a_grouped")
         for h in range(2):
             cast_xm(xm0a_grouped, xm0a_raw[:], h * PIECE)
         w1_grouped = tile([P, N * PACK], BF16, "w1_grouped")
-        nc.scalar.copy(w1_grouped[:].bitcast(U32).rearrange("p (i u) -> p i u", u=2)[:, :HALF],
-                       w1_words[:, :2 * N].bitcast(U32).rearrange("p (u i) -> p i u", u=2)[:, :HALF])
-        nc.gpsimd.tensor_scalar(w1_grouped[:].rearrange("p (i u e) -> p i u e", u=2, e=2)[:, HALF:],
-                                w1_words[:, :2 * N].bitcast(BF16).rearrange("p (u i e) -> p i u e", u=2, e=2)[:, HALF:],
+        nc.scalar.copy(w1_grouped[:].rearrange("p (i t) -> p i t", t=PACK)[:, :, :2], early[1][:].rearrange("p e i -> p i e"))
+        nc.gpsimd.tensor_scalar(w1_grouped[:].rearrange("p (i t) -> p i t", t=PACK)[:, :, 2:], late.rearrange("p e i -> p i e"),
                                 1.0, 0.0, ALU.mult, ALU.add)
 
         res0 = [subtract(nc.vector, "0%d" % c, scores(c, x0_q, w0_q), y0, c) for c in range(4)]
@@ -206,8 +203,7 @@ def tile_attend_glch_w_kernel(tc, xT, wT, y, wt, xm, offs, out):
         g0 = [tile([P, HALF * PACK], BF16, "g0%d" % h) for h in range(2)]
         for c in range(2):
             weigh(nc.vector, g0[0], c, th0[c], wt_of(0))
-        xm_q[0] = (tile([P, D], U32, "xm0_codes", "th00"), tile([P, D], U8, "xm0_scales"))
-        quantize_xm(0, 0, xm0a_grouped)
+        quantize_xm(0, 0, xm0a_grouped, "th00")
         quantize_g(0, 0, g0[0])
         first = gradient(0, 0)
         for c in range(2):
@@ -216,48 +212,55 @@ def tile_attend_glch_w_kernel(tc, xT, wT, y, wt, xm, offs, out):
         quantize_g(0, 1, g0[1])
         prod = [gradient(0, j) for j in (0, 1)][::-1]
         x1_grouped = tile([P, R * PACK], BF16, "x1_grouped")
-        cast_x(x1_grouped, x1_raw[:, :, :HALF], 0)
-        scatter(copy_out(first, 0, HALF, dw=x1_raw[:, 0, :HALF]))
-        for r0 in range(HALF, R, PIECE):
+        for r0 in range(0, R, PIECE):
             cast_x(x1_grouped, x1_raw[:, :, r0:r0 + PIECE], r0)
-        x1_q = quantize("x1", x1_grouped, E4M3, "g01")
-        xm0b_grouped = x1_raw[:, 1, :].bitcast(BF16)
+        x1_q = quantize("x1", x1_grouped, E4M3)
+        after_x1 = tile([P, 3 * HALF], F32, "after_x1", "x1_raw")
+        scatter(copy_out(first, 0, HALF, dw=after_x1[:, :HALF]))
+        xm0b_grouped = after_x1[:, HALF:].bitcast(BF16)
         for h in range(2):
             cast_xm(xm0b_grouped, xm0b_raw[:], h * PIECE)
         quantize_xm(0, HALF, xm0b_grouped)
-        after_xm0 = tile([P, 3 * HALF + PACK * N], F32, "after_xm0", "xm0b_raw")
-        scatter(copy_out(prod[1], HALF, N, dw=after_xm0[:, :HALF]))
-        scatter(copy_out(prod[0], 0, N, dw=after_xm0[:, HALF:3 * HALF]))
-        a1_sb = after_xm0[:, 3 * HALF:].rearrange("p (c t i) -> p c t i", t=PACK, i=CHUNK)
+        after_xm0 = tile([P, N + PACK * HALF], F32, "after_xm0", "xm0b_raw")
+        scatter(copy_out(prod[0], 0, N, dw=after_xm0[:, :N]))
+        a1_sb = after_xm0[:, N:].rearrange("p (c t i) -> p c t i", t=PACK, i=CHUNK)
         weights1 = tile([P, CHUNK, PACK], F32, "weights1", "x1_grouped")
         nc.gpsimd.tensor_scalar(weights1[:], wt_of(1), 1.0, 0.0, ALU.mult, ALU.add)
         a1 = [scores(c, x1_q, w1_q) for c in range(4)]
         a_sb = [copy_scores(a1_sb[:, c], a1[c]) for c in range(2)]
         res1 = [subtract(nc.gpsimd, "1%d" % c, a_sb[c], y1, c) for c in range(2)]
+        held = [prod[1]]
         prod = [gradient(0, j) for j in range(2, 4)]
         th1 = [tanh_grouped("th1%d" % c, res1[c]) for c in range(2)]
         scatter(copy_out(prod[0], 0, N))
         g1 = [tile([P, HALF * PACK], BF16, "g10")]
         for c in range(2):
             weigh(nc.gpsimd, g1[0], c, th1[c], weights1[:])
-        a_sb += [copy_scores(a1_sb[:, c], a1[c]) for c in range(2, 4)]
-        xm1_grouped = tile([P, D * PACK], BF16, "xm1_grouped")
-        for c0 in range(0, D, PIECE):
-            cast_xm(xm1_grouped, xm1_raw[:], c0)
-        xm_q[1] = (tile([P, D], U32, "xm1_codes", "th10"), tile([P, D], U8, "xm1_scales"))
-        quantize_xm(1, 0, xm1_grouped)
+        xm1a_grouped = tile([P, HALF * PACK], BF16, "xm1a_grouped", "residual11")
+        for c0 in range(0, HALF, PIECE):
+            cast_xm(xm1a_grouped, xm1_raw[:], c0)
+        a1b_sb = tile([P, 2, PACK, CHUNK], F32, "a1b_sb", "residual10")
+        a_sb += [copy_scores(a1b_sb[:, c], a1[2 + c]) for c in range(2)]
+        quantize_xm(1, 0, xm1a_grouped, "th10")
         quantize_g(1, 0, g1[0])
-        scatter(copy_out(prod[1], 0, N, "th11"))
-        res1 += [subtract(nc.gpsimd, "12", a_sb[2], y1, 2, "g10"), subtract(nc.gpsimd, "13", a_sb[3], y1, 3, "xm1_grouped")]
-        prod = [gradient(1, j) for j in range(3)]
+        after_g1a = tile([P, 5 * HALF], F32, "after_g1a", "th11")
+        scatter(copy_out(held[0], HALF, N, dw=after_g1a[:, :HALF]))
+        scatter(copy_out(prod[1], 0, N, dw=after_g1a[:, HALF:3 * HALF]))
+        xm1b_grouped = after_g1a[:, 3 * HALF:].bitcast(BF16)
+        for c0 in range(0, HALF, PIECE):
+            cast_xm(xm1b_grouped, xm1_raw[:, :, HALF:], c0)
+        res1b = tile([P, 2, PACK, CHUNK], F32, "residual1b", "g10")
+        res1 += [subtract(nc.gpsimd, "", a_sb[2 + c], y1, 2 + c, res1b[:, c]) for c in range(2)]
+        prod = [gradient(1, j) for j in range(2)]
         scatter(copy_out(prod[0], 0, HALF))
-        scatter(copy_out(prod[1], 0, HALF))
         th1 += [tanh_grouped("th1%d" % c, res1[c]) for c in range(2, 4)]
         g1.append(tile([P, HALF * PACK], BF16, "g11"))
         for c in range(2):
             weigh(nc.gpsimd, g1[1], c, th1[2 + c], weights1[:])
+        quantize_xm(1, HALF, xm1b_grouped, "th12")
         quantize_g(1, 1, g1[1])
-        scatter(copy_out(prod[2], 0, HALF, "th13"))
-        for j in range(3):
+        scatter(copy_out(prod[1], 0, HALF, "th13"))
+        for j in range(2):
             scatter(copy_out(gradient(1, j), HALF, N))
-        scatter(copy_out(gradient(1, 3), 0, N))
+        for j in range(2, 4):
+            scatter(copy_out(gradient(1, j), 0, N))

@@ -20,8 +20,7 @@ PACK = 4
 PER_COLUMN = 16
 CHUNK = 128
 HALF = 256
-PIECE = 128
-X0_ON_VECTOR = 200
+X0_ON_VECTOR = 240
 RUN = 4
 
 
@@ -30,7 +29,7 @@ def tile_attend_glch_w_kernel(tc, xT, wT, y, wt, xm, offs, out):
     with ExitStack() as ctx:
         sb = ctx.enter_context(tc.tile_pool(name="sb", bufs=1))
         ps_a = ctx.enter_context(tc.psum_pool(name="ps_a", bufs=N // CHUNK))
-        ps_dw = ctx.enter_context(tc.psum_pool(name="ps_dw", bufs=D // P))
+        ps_dw = ctx.enter_context(tc.psum_pool(name="ps_dw", bufs=1))
 
         def tile(shape, dtype, name, reuse=None):
             return sb.tile(shape, dtype, name=name, tag=reuse or name, align_bytes=64)
@@ -38,11 +37,14 @@ def tile_attend_glch_w_kernel(tc, xT, wT, y, wt, xm, offs, out):
         def by_fours(rows):
             return rows.rearrange("(p t) c -> p t c", t=PACK)
 
-        def quantize(name, grouped, fmt, reuse=None):
+        def quantize(name, grouped, fmt, reuse=None, parts=1):
             width = grouped.shape[1] // PACK
             codes = tile([P, width], U32, name + "_codes", reuse)
             scales = tile([P, width], U8, name + "_scales")
-            nc.vector.quantize_mx(out=codes[:].bitcast(fmt), scales=scales[:], in_=grouped[:])
+            step = width // parts
+            for c in range(0, width, step):
+                nc.vector.quantize_mx(out=codes[:, c:c + step].bitcast(fmt), scales=scales[:, c:c + step],
+                                      in_=grouped[:, c * PACK:(c + step) * PACK])
             return codes, scales
 
         offsets = tile([P, B * N // PER_COLUMN], U16, "offsets")
@@ -64,7 +66,7 @@ def tile_attend_glch_w_kernel(tc, xT, wT, y, wt, xm, offs, out):
         x0_raw = w1_late[:, N:].rearrange("p (j r) -> p j r", j=PACK)
         nc.sync.dma_start(x0_raw, by_fours(xT[0]))
         xm0a_raw = load("xm0a_raw", xm[0], 0, HALF)
-        y0 = load("y0", y[0])
+        y0 = [load("y0a", y[0], 0, HALF), load("y0b", y[0], HALF, N)]
         nc.sync.dma_start(wt_sb[:, :, :PACK], wt.rearrange("b (p t) o -> p b (t o)", t=PACK))
         x1_raw = load("x1_raw", xT[1])
         xm0b_raw = load("xm0b_raw", xm[0], HALF, D)
@@ -72,7 +74,7 @@ def tile_attend_glch_w_kernel(tc, xT, wT, y, wt, xm, offs, out):
         xm1_raw = load("xm1_raw", xm[1])
 
         windows = []
-        for j in range(D // P):
+        for j in range(D // P - 1):
             windows.append(tile([P, T], F32, "window%d" % j))
             nc.vector.memset(windows[j][:], 0.0)
 
@@ -111,10 +113,10 @@ def tile_attend_glch_w_kernel(tc, xT, wT, y, wt, xm, offs, out):
             cols = slice(h * HALF, (h + 1) * HALF)
             nc.vector.quantize_mx(out=g_q[b][0][:, cols].bitcast(E5M2), scales=g_q[b][1][:, cols], in_=g[:])
 
-        def cast_xm(grouped, raw, first):
+        def cast_xm(grouped, raw):
             dst = grouped[:].rearrange("p (c i t) -> p c t i", i=RUN, t=PACK)
             src = raw.rearrange("p t (c i) -> p c t i", i=RUN)
-            nc.scalar.copy(dst[:, first // RUN:(first + PIECE) // RUN], src[:, first // RUN:(first + PIECE) // RUN])
+            nc.scalar.copy(dst, src)
 
         def quantize_xm(b, first, grouped, reuse=None):
             xm_q[b, first // HALF] = quantize("xm%d%d" % (b, first // HALF), grouped, E4M3, reuse)
@@ -142,10 +144,10 @@ def tile_attend_glch_w_kernel(tc, xT, wT, y, wt, xm, offs, out):
         def wt_of(b):
             return wt_sb[:, b:b + 1, :PACK].to_broadcast([P, CHUNK, PACK])
 
-        def gradient(b, j):
+        def gradient(b, j, bank=None):
             rows = slice(j % 2 * P, (j % 2 + 1) * P)
             codes, scales = xm_q[b, j // 2]
-            dw_ps = ps_dw.tile([P, N], F32, name="dw_ps")
+            dw_ps = ps_dw.tile([P, N], F32, name="dw_ps", tag="dw%d" % (j if bank is None else bank))
             nc.tensor.matmul_mx(out=dw_ps[:], lhsT=codes[:, rows].bitcast(E4M3), lhsT_scale=scales[:, rows],
                                 rhs=g_q[b][0][:].bitcast(E5M2), rhs_scale=g_q[b][1][:], start=True, stop=True)
             return b, j, dw_ps
@@ -175,6 +177,8 @@ def tile_attend_glch_w_kernel(tc, xT, wT, y, wt, xm, offs, out):
 
         gather(0, 0)
         gather(1, 0)
+        windows.append(tile([P, T], F32, "window3", "plane0"))
+        nc.gpsimd.memset(windows[3][:], 0.0)
         gather(0, 1)
         plane1_bf = tile([P, T], BF16, "plane1_bf")
         nc.scalar.activation(plane1_bf[:], planes[1][:], ACT.Copy)
@@ -188,19 +192,18 @@ def tile_attend_glch_w_kernel(tc, xT, wT, y, wt, xm, offs, out):
         cast_x(x0_grouped, x0_raw[:, :, :R - X0_ON_VECTOR], 0)
         cast_x(x0_grouped, x0_raw[:, :, R - X0_ON_VECTOR:], R - X0_ON_VECTOR, nc.vector.tensor_copy)
         w0_q = quantize("w0", w_grouped[0], E4M3)
-        x0_q = quantize("x0", x0_grouped, E4M3)
+        x0_q = quantize("x0", x0_grouped, E4M3, parts=2)
         gather(1, 3)
         xm0a_grouped = tile([P, HALF * PACK], BF16, "xm0a_grouped")
-        for h in range(2):
-            cast_xm(xm0a_grouped, xm0a_raw[:], h * PIECE)
+        cast_xm(xm0a_grouped, xm0a_raw[:])
         w1_grouped = tile([P, N * PACK], BF16, "w1_grouped")
         nc.scalar.copy(w1_grouped[:].rearrange("p (i t) -> p i t", t=PACK)[:, :, :2], early[1][:].rearrange("p e i -> p i e"))
         nc.gpsimd.tensor_scalar(w1_grouped[:].rearrange("p (i t) -> p i t", t=PACK)[:, :, 2:], late.rearrange("p e i -> p i e"),
                                 1.0, 0.0, ALU.mult, ALU.add)
 
-        res0 = [subtract(nc.vector, "0%d" % c, scores(c, x0_q, w0_q), y0, c) for c in range(4)]
+        res0 = [subtract(nc.vector, "0%d" % c, scores(c, x0_q, w0_q), y0[c // 2], c % 2) for c in range(4)]
         th0 = [tanh_grouped("th0%d" % c, res0[c]) for c in range(4)]
-        g0 = [tile([P, HALF * PACK], BF16, "g0%d" % h) for h in range(2)]
+        g0 = [tile([P, HALF * PACK], BF16, "g00"), tile([P, HALF * PACK], BF16, "g01")]
         for c in range(2):
             weigh(nc.vector, g0[0], c, th0[c], wt_of(0))
         quantize_xm(0, 0, xm0a_grouped, "th00")
@@ -210,45 +213,42 @@ def tile_attend_glch_w_kernel(tc, xT, wT, y, wt, xm, offs, out):
             weigh(nc.vector, g0[1], c, th0[2 + c], wt_of(0))
         w1_q = quantize("w1", w1_grouped, E4M3, "th02")
         quantize_g(0, 1, g0[1])
-        prod = [gradient(0, j) for j in (0, 1)][::-1]
+        prod = [gradient(0, 1)]
         x1_grouped = tile([P, R * PACK], BF16, "x1_grouped")
-        for r0 in range(0, R, PIECE):
-            cast_x(x1_grouped, x1_raw[:, :, r0:r0 + PIECE], r0)
+        cast_x(x1_grouped, x1_raw[:], 0)
         x1_q = quantize("x1", x1_grouped, E4M3)
         after_x1 = tile([P, 3 * HALF], F32, "after_x1", "x1_raw")
         scatter(copy_out(first, 0, HALF, dw=after_x1[:, :HALF]))
         xm0b_grouped = after_x1[:, HALF:].bitcast(BF16)
-        for h in range(2):
-            cast_xm(xm0b_grouped, xm0b_raw[:], h * PIECE)
+        cast_xm(xm0b_grouped, xm0b_raw[:])
         quantize_xm(0, HALF, xm0b_grouped)
-        after_xm0 = tile([P, N + PACK * HALF], F32, "after_xm0", "xm0b_raw")
+        after_xm0 = tile([P, N + 3 * PACK * CHUNK], F32, "after_xm0", "xm0b_raw")
         scatter(copy_out(prod[0], 0, N, dw=after_xm0[:, :N]))
         a1_sb = after_xm0[:, N:].rearrange("p (c t i) -> p c t i", t=PACK, i=CHUNK)
         weights1 = tile([P, CHUNK, PACK], F32, "weights1", "x1_grouped")
         nc.gpsimd.tensor_scalar(weights1[:], wt_of(1), 1.0, 0.0, ALU.mult, ALU.add)
-        a1 = [scores(c, x1_q, w1_q) for c in range(4)]
-        a_sb = [copy_scores(a1_sb[:, c], a1[c]) for c in range(2)]
+        a1 = [scores(c, x1_q, w1_q) for c in range(3)]
+        a_sb = [copy_scores(a1_sb[:, c], a1[c]) for c in range(3)]
         res1 = [subtract(nc.gpsimd, "1%d" % c, a_sb[c], y1, c) for c in range(2)]
-        held = [prod[1]]
-        prod = [gradient(0, j) for j in range(2, 4)]
+        scatter(copy_out(gradient(0, 2), 0, N))
+        a1.append(scores(3, x1_q, w1_q))
+        held = [gradient(0, 0, 1)]
+        prod = [None, gradient(0, 3)]
         th1 = [tanh_grouped("th1%d" % c, res1[c]) for c in range(2)]
-        scatter(copy_out(prod[0], 0, N))
         g1 = [tile([P, HALF * PACK], BF16, "g10")]
         for c in range(2):
             weigh(nc.gpsimd, g1[0], c, th1[c], weights1[:])
-        xm1a_grouped = tile([P, HALF * PACK], BF16, "xm1a_grouped", "residual11")
-        for c0 in range(0, HALF, PIECE):
-            cast_xm(xm1a_grouped, xm1_raw[:], c0)
-        a1b_sb = tile([P, 2, PACK, CHUNK], F32, "a1b_sb", "residual10")
-        a_sb += [copy_scores(a1b_sb[:, c], a1[2 + c]) for c in range(2)]
+        after_th11 = tile([P, 2 * PACK * CHUNK], F32, "after_th11", "residual11")
+        xm1a_grouped = after_th11[:, :PACK * CHUNK].bitcast(BF16)
+        cast_xm(xm1a_grouped, xm1_raw[:, :, :HALF])
+        a_sb.append(copy_scores(after_th11[:, PACK * CHUNK:].rearrange("p (t i) -> p t i", t=PACK), a1[3]))
         quantize_xm(1, 0, xm1a_grouped, "th10")
         quantize_g(1, 0, g1[0])
         after_g1a = tile([P, 5 * HALF], F32, "after_g1a", "th11")
         scatter(copy_out(held[0], HALF, N, dw=after_g1a[:, :HALF]))
         scatter(copy_out(prod[1], 0, N, dw=after_g1a[:, HALF:3 * HALF]))
         xm1b_grouped = after_g1a[:, 3 * HALF:].bitcast(BF16)
-        for c0 in range(0, HALF, PIECE):
-            cast_xm(xm1b_grouped, xm1_raw[:, :, HALF:], c0)
+        cast_xm(xm1b_grouped, xm1_raw[:, :, HALF:])
         res1b = tile([P, 2, PACK, CHUNK], F32, "residual1b", "g10")
         res1 += [subtract(nc.gpsimd, "", a_sb[2 + c], y1, 2 + c, res1b[:, c]) for c in range(2)]
         prod = [gradient(1, j) for j in range(2)]

@@ -1,6 +1,7 @@
 from contextlib import ExitStack
 
 import concourse.mybir as mybir
+from concourse.masks import make_identity
 
 B, N, T, D, R = 2, 512, 2048, 512, 512
 FLOPS = 2 * B * (R * N * D + D * N * R)
@@ -21,6 +22,7 @@ PER_COLUMN = 16
 CHUNK = 128
 HALF = 256
 X0_ON_VECTOR = 240
+WEAVE_ON_SCALAR = 96
 RUN = 4
 
 
@@ -175,6 +177,30 @@ def tile_attend_glch_w_kernel(tc, xT, wT, y, wt, xm, offs, out):
             engine.tensor_tensor(residual[:], a[:], y_sb[:, :, c * CHUNK:(c + 1) * CHUNK], ALU.subtract)
             return residual
 
+        def scores_turned(c, x_q, w_q):
+            cols = slice(c * CHUNK, (c + 1) * CHUNK)
+            a_ps = ps_a.tile([P, PACK, CHUNK], F32, name="a_ps")
+            nc.tensor.matmul_mx(out=a_ps[:].rearrange("p t i -> p (t i)"), lhsT=w_q[0][:, cols].bitcast(E4M3), lhsT_scale=w_q[1][:, cols],
+                                rhs=x_q[0][:].bitcast(E4M3), rhs_scale=x_q[1][:], start=True, stop=True)
+            return a_ps
+
+        def minus_y_turned(minus_y, y_sb, c):
+            y_ps = ps_a.tile([P, PACK, CHUNK], F32, name="a_ps")
+            for t in range(PACK):
+                nc.tensor.transpose(y_ps[:, t, :], y_sb[:, t, c * CHUNK:(c + 1) * CHUNK], identity[:])
+            nc.scalar.activation(minus_y[:], y_ps[:], ACT.Copy, scale=-1.0)
+            return minus_y
+
+        def add_turned(first, second):
+            total = ps_a.tile([P, PACK, CHUNK], F32, name="a_ps")
+            for t in range(PACK):
+                nc.tensor.matmul(total[:, t, :], first[:, t, :], identity[:], start=True, stop=False, is_transpose=True)
+                nc.tensor.matmul(total[:, t, :], second[:, t, :], identity[:], start=False, stop=True, is_transpose=True)
+            return total
+
+        identity = tile([P, P], F32, "identity")
+        make_identity(nc, identity[:])
+
         gather(0, 0)
         gather(1, 0)
         windows.append(tile([P, T], F32, "window3", "plane0"))
@@ -198,8 +224,10 @@ def tile_attend_glch_w_kernel(tc, xT, wT, y, wt, xm, offs, out):
         cast_xm(xm0a_grouped, xm0a_raw[:])
         w1_grouped = tile([P, N * PACK], BF16, "w1_grouped")
         nc.scalar.copy(w1_grouped[:].rearrange("p (i t) -> p i t", t=PACK)[:, :, :2], early[1][:].rearrange("p e i -> p i e"))
-        nc.gpsimd.tensor_scalar(w1_grouped[:].rearrange("p (i t) -> p i t", t=PACK)[:, :, 2:], late.rearrange("p e i -> p i e"),
-                                1.0, 0.0, ALU.mult, ALU.add)
+        w1_places = w1_grouped[:].rearrange("p (i t) -> p i t", t=PACK)[:, :, 2:]
+        late_by_slot = late.rearrange("p e i -> p i e")
+        nc.scalar.copy(w1_places[:, :WEAVE_ON_SCALAR], late_by_slot[:, :WEAVE_ON_SCALAR])
+        nc.gpsimd.tensor_scalar(w1_places[:, WEAVE_ON_SCALAR:], late_by_slot[:, WEAVE_ON_SCALAR:], 1.0, 0.0, ALU.mult, ALU.add)
 
         res0 = [subtract(nc.vector, "0%d" % c, scores(c, x0_q, w0_q), y0[c // 2], c % 2) for c in range(4)]
         th0 = [tanh_grouped("th0%d" % c, res0[c]) for c in range(4)]
@@ -227,37 +255,38 @@ def tile_attend_glch_w_kernel(tc, xT, wT, y, wt, xm, offs, out):
         a1_sb = after_xm0[:, N:].rearrange("p (c t i) -> p c t i", t=PACK, i=CHUNK)
         weights1 = tile([P, CHUNK, PACK], F32, "weights1", "x1_grouped")
         nc.gpsimd.tensor_scalar(weights1[:], wt_of(1), 1.0, 0.0, ALU.mult, ALU.add)
-        a1 = [scores(c, x1_q, w1_q) for c in range(3)]
+        a1 = [scores(c, x1_q, w1_q) for c in range(2)] + [scores_turned(2, x1_q, w1_q)]
         a_sb = [copy_scores(a1_sb[:, c], a1[c]) for c in range(3)]
         res1 = [subtract(nc.gpsimd, "1%d" % c, a_sb[c], y1, c) for c in range(2)]
         scatter(copy_out(gradient(0, 2), 0, N))
-        a1.append(scores(3, x1_q, w1_q))
+        a1.append(scores_turned(3, x1_q, w1_q))
         held = [gradient(0, 0, 1)]
         prod = [None, gradient(0, 3)]
         th1 = [tanh_grouped("th1%d" % c, res1[c]) for c in range(2)]
+        scatter(copy_out(held[0], HALF, N, "residual10"))
         g1 = [tile([P, HALF * PACK], BF16, "g10")]
         for c in range(2):
             weigh(nc.gpsimd, g1[0], c, th1[c], weights1[:])
-        after_th11 = tile([P, 2 * PACK * CHUNK], F32, "after_th11", "residual11")
+        res1.append(add_turned(a_sb[2], minus_y_turned(tile([P, PACK, CHUNK], F32, "minus_y2"), y1, 2)))
+        after_th11 = tile([P, 3 * PACK * CHUNK], F32, "after_th11", "residual11")
         xm1a_grouped = after_th11[:, :PACK * CHUNK].bitcast(BF16)
+        last = after_th11[:].rearrange("p (c t i) -> p c t i", t=PACK, i=CHUNK)
+        res1.append(add_turned(copy_scores(last[:, 1], a1[3]), minus_y_turned(last[:, 2], y1, 3)))
         cast_xm(xm1a_grouped, xm1_raw[:, :, :HALF])
-        a_sb.append(copy_scores(after_th11[:, PACK * CHUNK:].rearrange("p (t i) -> p t i", t=PACK), a1[3]))
         quantize_xm(1, 0, xm1a_grouped, "th10")
         quantize_g(1, 0, g1[0])
-        after_g1a = tile([P, 5 * HALF], F32, "after_g1a", "th11")
-        scatter(copy_out(held[0], HALF, N, dw=after_g1a[:, :HALF]))
-        scatter(copy_out(prod[1], 0, N, dw=after_g1a[:, HALF:3 * HALF]))
-        xm1b_grouped = after_g1a[:, 3 * HALF:].bitcast(BF16)
-        cast_xm(xm1b_grouped, xm1_raw[:, :, HALF:])
-        res1b = tile([P, 2, PACK, CHUNK], F32, "residual1b", "g10")
-        res1 += [subtract(nc.gpsimd, "", a_sb[2 + c], y1, 2 + c, res1b[:, c]) for c in range(2)]
+        after_g1a = tile([P, N + PACK * CHUNK], F32, "after_g1a", "th11")
+        scatter(copy_out(prod[1], 0, N, dw=after_g1a[:, :N]))
+        th1.append(tanh_grouped("", res1[2], after_g1a[:, N:]))
         prod = [gradient(1, j) for j in range(2)]
         scatter(copy_out(prod[0], 0, HALF))
-        th1 += [tanh_grouped("th1%d" % c, res1[c]) for c in range(2, 4)]
-        g1.append(tile([P, HALF * PACK], BF16, "g11"))
+        th1.append(tanh_grouped("th13", res1[3]))
+        xm1b_grouped = after_th11[:, 2 * PACK * CHUNK:].bitcast(BF16)
+        cast_xm(xm1b_grouped, xm1_raw[:, :, HALF:])
+        g1.append(tile([P, HALF * PACK], BF16, "g11", "g10"))
         for c in range(2):
             weigh(nc.gpsimd, g1[1], c, th1[2 + c], weights1[:])
-        quantize_xm(1, HALF, xm1b_grouped, "th12")
+        quantize_xm(1, HALF, xm1b_grouped, "th11")
         quantize_g(1, 1, g1[1])
         scatter(copy_out(prod[1], 0, HALF, "th13"))
         for j in range(2):

@@ -1,7 +1,6 @@
 from contextlib import ExitStack
 
 import concourse.mybir as mybir
-from concourse.masks import make_identity
 
 B, N, T, D, R = 2, 512, 2048, 512, 512
 FLOPS = 2 * B * (R * N * D + D * N * R)
@@ -21,8 +20,6 @@ PACK = 4
 PER_COLUMN = 16
 CHUNK = 128
 HALF = 256
-X0_ON_VECTOR = 240
-WEAVE_ON_SCALAR = 96
 RUN = 4
 
 
@@ -30,266 +27,250 @@ def tile_attend_glch_w_kernel(tc, xT, wT, y, wt, xm, offs, out):
     nc = tc.nc
     with ExitStack() as ctx:
         sb = ctx.enter_context(tc.tile_pool(name="sb", bufs=1))
-        ps_a = ctx.enter_context(tc.psum_pool(name="ps_a", bufs=N // CHUNK))
-        ps_dw = ctx.enter_context(tc.psum_pool(name="ps_dw", bufs=1))
+        ps = ctx.enter_context(tc.psum_pool(name="ps", bufs=1))
 
         def tile(shape, dtype, name, reuse=None):
             return sb.tile(shape, dtype, name=name, tag=reuse or name, align_bytes=64)
 
+        def bank(name, number, shape):
+            return ps.tile(shape, F32, name=name, tag="bank%d" % number)
+
         def by_fours(rows):
             return rows.rearrange("(p t) c -> p t c", t=PACK)
-
-        def quantize(name, grouped, fmt, reuse=None, parts=1):
-            width = grouped.shape[1] // PACK
-            codes = tile([P, width], U32, name + "_codes", reuse)
-            scales = tile([P, width], U8, name + "_scales")
-            step = width // parts
-            for c in range(0, width, step):
-                nc.vector.quantize_mx(out=codes[:, c:c + step].bitcast(fmt), scales=scales[:, c:c + step],
-                                      in_=grouped[:, c * PACK:(c + step) * PACK])
-            return codes, scales
-
-        offsets = tile([P, B * N // PER_COLUMN], U16, "offsets")
-        wt_rows = tile([P, B * 2 * PACK], F32, "wt_rows")
-        wt_sb = wt_rows[:].rearrange("p (b t) -> p b t", b=B)
-        planes = []
-        for t in range(PACK):
-            planes.append(tile([P, T], F32, "plane%d" % t))
-            nc.sync.dma_start(planes[t][:], by_fours(wT)[:, t, :])
-            if t == 0:
-                nc.sync.dma_start(offsets[:], offs)
 
         def load(name, rows, first=0, end=512):
             raw = tile([P, PACK, end - first], F32, name)
             nc.sync.dma_start(raw[:], by_fours(rows)[:, :, first:end])
             return raw
 
-        w1_late = tile([P, N + PACK * R], F32, "w1_late")
-        x0_raw = w1_late[:, N:].rearrange("p (j r) -> p j r", j=PACK)
-        nc.sync.dma_start(x0_raw, by_fours(xT[0]))
-        xm0a_raw = load("xm0a_raw", xm[0], 0, HALF)
-        y0 = [load("y0a", y[0], 0, HALF), load("y0b", y[0], HALF, N)]
-        nc.sync.dma_start(wt_sb[:, :, :PACK], wt.rearrange("b (p t) o -> p b (t o)", t=PACK))
-        x1_raw = load("x1_raw", xT[1])
-        xm0b_raw = load("xm0b_raw", xm[0], HALF, D)
-        y1 = load("y1", y[1])
-        xm1_raw = load("xm1_raw", xm[1])
-
-        windows = []
-        for j in range(D // P - 1):
-            windows.append(tile([P, T], F32, "window%d" % j))
-            nc.vector.memset(windows[j][:], 0.0)
-
-        w_grouped = [tile([P, N * PACK], BF16, "w0_grouped")]
-        early = [tile([P, 2, N], BF16, "w%d_early" % b) for b in range(B)]
-        late = w1_late[:, :2 * N].rearrange("p (e i) -> p e i", e=2)
-
         def slots(first, end):
             return offsets[:, first // PER_COLUMN:end // PER_COLUMN]
 
-        def gather(b, t):
-            if t < 2:
-                dst = early[b][:, t, :]
-            elif b == 0:
-                dst = w_grouped[0][:].rearrange("p (i t) -> p t i", t=PACK)[:, t, :]
-            else:
-                dst = late[:, t - 2, :]
-            nc.vector.tensor_copy(dst, planes[t][:].indirect(slots(b * N, (b + 1) * N)))
+        def mx_tiles(name, width, reuse=None):
+            return tile([P, width], U32, name + "_codes", reuse), tile([P, width], U8, name + "_scales")
 
-        def cast_x(grouped, raw, first, copy=nc.scalar.copy):
+        def quantize(q, grouped, fmt, first=0):
+            end = first + grouped.shape[1] // PACK
+            nc.vector.quantize_mx(out=q[0][:, first:end].bitcast(fmt), scales=q[1][:, first:end], in_=grouped)
+
+        def places(grouped):
+            return grouped[:].rearrange("p (i t) -> p i t", t=PACK)
+
+        def copy_on(engine):
+            if engine == "gpsimd":
+                return lambda dst, src: nc.gpsimd.tensor_scalar(dst, src, 1.0, 0.0, ALU.mult, ALU.add)
+            return nc.vector.tensor_copy if engine == "vector" else nc.scalar.copy
+
+        def cast_x(engine, grouped, raw, first, end):
             dst = grouped[:].rearrange("p (t m j) -> p m j t", t=PACK, j=PACK)
-            copy(dst[:, first // PACK:(first + raw.shape[2]) // PACK], raw.rearrange("p j (m t) -> p m j t", t=PACK))
+            src = raw[:].rearrange("p j (m t) -> p m j t", t=PACK)
+            copy_on(engine)(dst[:, first // PACK:end // PACK], src[:, first // PACK:end // PACK])
 
-        xm_q = {}
-        g_q = []
-
-        def zero_second_half(words, engine):
-            g_q.append((words[:, :N], words[:, N:].bitcast(U8)))
-            engine.memset(g_q[-1][0][:, HALF:], 0)
-            engine.memset(g_q[-1][1][:, HALF:].bitcast(U32), 0)
-
-        zero_second_half(tile([P, N + N // PACK], U32, "g0_quantised"), nc.gpsimd)
-        zero_second_half(tile([P, N + N // PACK], U32, "g1_quantised"), nc.vector)
-
-        def quantize_g(b, h, g):
-            cols = slice(h * HALF, (h + 1) * HALF)
-            nc.vector.quantize_mx(out=g_q[b][0][:, cols].bitcast(E5M2), scales=g_q[b][1][:, cols], in_=g[:])
-
-        def cast_xm(grouped, raw):
-            dst = grouped[:].rearrange("p (c i t) -> p c t i", i=RUN, t=PACK)
+        def cast_xm(engine, grouped, raw):
+            if engine == "gpsimd":
+                copy_on(engine)(grouped.rearrange("p (i t) -> p i t", t=PACK), raw.rearrange("p t i -> p i t"))
+                return
+            dst = grouped.rearrange("p (c i t) -> p c t i", i=RUN, t=PACK)
             src = raw.rearrange("p t (c i) -> p c t i", i=RUN)
-            nc.scalar.copy(dst, src)
+            copy_on(engine)(dst, src)
 
-        def quantize_xm(b, first, grouped, reuse=None):
-            xm_q[b, first // HALF] = quantize("xm%d%d" % (b, first // HALF), grouped, E4M3, reuse)
-
-        def scores(c, x_q, w_q):
+        def scores(number, c, x_q, w_q):
             cols = slice(c * CHUNK, (c + 1) * CHUNK)
-            a_ps = ps_a.tile([P, PACK, CHUNK], F32, name="a_ps")
+            a_ps = bank("a_ps", number, [P, PACK, CHUNK])
             for t in range(PACK):
                 rows = slice(t * P, (t + 1) * P)
                 nc.tensor.matmul_mx(out=a_ps[:, t, :], lhsT=x_q[0][:, rows].bitcast(E4M3), lhsT_scale=x_q[1][:, rows],
                                     rhs=w_q[0][:, cols].bitcast(E4M3), rhs_scale=w_q[1][:, cols], start=True, stop=True)
             return a_ps
 
-        def tanh_grouped(name, residual, th=None):
-            if th is None:
-                th = tile([P, CHUNK * PACK], F32, name)
+        def subtract(name, a_ps, y_sb, c, reuse=None):
+            residual = tile([P, PACK, CHUNK], F32, "residual" + name, reuse)
+            nc.vector.tensor_tensor(residual[:], a_ps[:], y_sb[:, :, c * CHUNK:(c + 1) * CHUNK], ALU.subtract)
+            return residual
+
+        def tanh_grouped(name, residual, reuse=None):
+            th = tile([P, CHUNK * PACK], F32, "th" + name, reuse)
             nc.scalar.activation(th[:].rearrange("p (c i t) -> p c t i", i=2, t=PACK),
                                  residual[:].rearrange("p t (c i) -> p c t i", i=2), ACT.Tanh)
             return th
 
         def weigh(engine, g, c, th, weights):
-            engine.tensor_tensor(g[:, c * CHUNK * PACK:(c + 1) * CHUNK * PACK].rearrange("p (i t) -> p i t", t=PACK),
-                                 th[:].rearrange("p (i t) -> p i t", t=PACK), weights, ALU.mult)
+            engine.tensor_tensor(places(g)[:, c * CHUNK:(c + 1) * CHUNK], places(th), weights, ALU.mult)
 
         def wt_of(b):
             return wt_sb[:, b:b + 1, :PACK].to_broadcast([P, CHUNK, PACK])
 
-        def gradient(b, j, bank=None):
+        def product(dw_ps, xm_q, j, g_q, first, end):
             rows = slice(j % 2 * P, (j % 2 + 1) * P)
-            codes, scales = xm_q[b, j // 2]
-            dw_ps = ps_dw.tile([P, N], F32, name="dw_ps", tag="dw%d" % (j if bank is None else bank))
-            nc.tensor.matmul_mx(out=dw_ps[:], lhsT=codes[:, rows].bitcast(E4M3), lhsT_scale=scales[:, rows],
-                                rhs=g_q[b][0][:].bitcast(E5M2), rhs_scale=g_q[b][1][:], start=True, stop=True)
-            return b, j, dw_ps
+            nc.tensor.matmul_mx(out=dw_ps, lhsT=xm_q[0][:, rows].bitcast(E4M3), lhsT_scale=xm_q[1][:, rows],
+                                rhs=g_q[0][:, first:end].bitcast(E5M2), rhs_scale=g_q[1][:, first:end], start=True, stop=True)
 
-        def copy_out(product, first, end, reuse=None, dw=None):
-            b, j, dw_ps = product
-            if dw is None:
-                dw = tile([P, end - first], F32, "dw%d%d_%d" % (b, j, first), reuse)
-            nc.scalar.copy(dw[:], dw_ps[:, first:end])
-            return b, j, first, end, dw
+        def copy_out(engine, name, dw_ps, reuse=None):
+            dw = tile([P, N], F32, name, reuse)
+            copy_on(engine)(dw[:], dw_ps[:])
+            return dw
 
-        def scatter(piece):
-            b, j, first, end, dw = piece
-            nc.vector.tensor_copy(windows[j][:].indirect(slots(b * N + first, b * N + end)), dw[:])
-            if b == B - 1 and end == N:
-                nc.sync.dma_start(out[j * P:(j + 1) * P, :], windows[j][:])
+        def scatter(engine, j, dw, first, end):
+            window = windows[j][:].indirect(slots(first, end))
+            if engine == "vector":
+                nc.vector.tensor_copy(window, dw)
+            else:
+                nc.scalar.activation(window, dw, ACT.Copy)
 
-        def copy_scores(a_sb, a_ps):
-            nc.scalar.copy(a_sb, a_ps[:])
-            return a_sb
+        def store(j):
+            nc.sync.dma_start(out[j * P:(j + 1) * P, :], windows[j][:])
 
-        def subtract(engine, name, a, y_sb, c, residual=None):
-            if residual is None:
-                residual = tile([P, PACK, CHUNK], F32, "residual" + name)
-            engine.tensor_tensor(residual[:], a[:], y_sb[:, :, c * CHUNK:(c + 1) * CHUNK], ALU.subtract)
-            return residual
+        offsets = tile([P, B * N // PER_COLUMN], U16, "offsets")
+        wt_rows = tile([P, B * 2 * PACK], F32, "wt_rows")
+        wt_sb = wt_rows[:].rearrange("p (b t) -> p b t", b=B)
+        planes = [tile([P, T], F32, "plane%d" % t) for t in range(PACK)]
+        nc.sync.dma_start(planes[0][:], by_fours(wT)[:, 0, :])
+        nc.sync.dma_start(offsets[:], offs)
+        nc.sync.dma_start(planes[1][:], by_fours(wT)[:, 1, :])
+        nc.sync.dma_start(wt_sb[:, :, :PACK], wt.rearrange("b (p t) o -> p b (t o)", t=PACK))
+        nc.sync.dma_start(planes[2][:], by_fours(wT)[:, 2, :])
+        nc.sync.dma_start(planes[3][:], by_fours(wT)[:, 3, :])
+        x0_raw = load("x0_raw", xT[0])
+        y0 = load("y0", y[0])
+        xm0a_raw = load("xm0a_raw", xm[0], 0, HALF)
+        x1_raw = load("x1_raw", xT[1])
+        y1 = load("y1", y[1])
+        xm1a_raw = load("xm1a_raw", xm[1], 0, HALF)
+        xm0b_raw = load("xm0b_raw", xm[0], HALF, D)
+        xm1b_raw = load("xm1b_raw", xm[1], HALF, D)
 
-        def scores_turned(c, x_q, w_q):
-            cols = slice(c * CHUNK, (c + 1) * CHUNK)
-            a_ps = ps_a.tile([P, PACK, CHUNK], F32, name="a_ps")
-            nc.tensor.matmul_mx(out=a_ps[:].rearrange("p t i -> p (t i)"), lhsT=w_q[0][:, cols].bitcast(E4M3), lhsT_scale=w_q[1][:, cols],
-                                rhs=x_q[0][:].bitcast(E4M3), rhs_scale=x_q[1][:], start=True, stop=True)
-            return a_ps
+        windows = []
+        for j in range(D // P):
+            windows.append(tile([P, T], F32, "window%d" % j))
+            nc.vector.memset(windows[j][:], 0.0)
 
-        def minus_y_turned(minus_y, y_sb, c):
-            y_ps = ps_a.tile([P, PACK, CHUNK], F32, name="a_ps")
-            for t in range(PACK):
-                nc.tensor.transpose(y_ps[:, t, :], y_sb[:, t, c * CHUNK:(c + 1) * CHUNK], identity[:])
-            nc.scalar.activation(minus_y[:], y_ps[:], ACT.Copy, scale=-1.0)
-            return minus_y
+        w_grouped = [tile([P, N * PACK], BF16, "w0_grouped")]
 
-        def add_turned(first, second):
-            total = ps_a.tile([P, PACK, CHUNK], F32, name="a_ps")
-            for t in range(PACK):
-                nc.tensor.matmul(total[:, t, :], first[:, t, :], identity[:], start=True, stop=False, is_transpose=True)
-                nc.tensor.matmul(total[:, t, :], second[:, t, :], identity[:], start=False, stop=True, is_transpose=True)
-            return total
+        def gather0(t, first=0, end=N):
+            nc.vector.tensor_copy(places(w_grouped[0])[:, first:end, t], planes[t][:].indirect(slots(first, end)))
 
-        identity = tile([P, P], F32, "identity")
-        make_identity(nc, identity[:])
+        x_grouped = [tile([P, R * PACK], BF16, "x%d_grouped" % b) for b in range(B)]
+        x_q = [mx_tiles("x%d" % b, R) for b in range(B)]
+        w_q = [mx_tiles("w0", N)]
+        g_q = [mx_tiles("g%d" % b, N) for b in range(B)]
 
-        gather(0, 0)
-        gather(1, 0)
-        windows.append(tile([P, T], F32, "window3", "plane0"))
-        nc.gpsimd.memset(windows[3][:], 0.0)
-        gather(0, 1)
-        plane1_bf = tile([P, T], BF16, "plane1_bf")
-        nc.scalar.activation(plane1_bf[:], planes[1][:], ACT.Copy)
-        nc.scalar.activation(early[1][:, 1, :HALF], plane1_bf[:].indirect(slots(N, N + HALF)), ACT.Copy)
-        nc.vector.tensor_copy(early[1][:, 1, HALF:], planes[1][:].indirect(slots(N + HALF, 2 * N)))
-        nc.scalar.copy(w_grouped[0][:].rearrange("p (i t) -> p i t", t=PACK)[:, :, :2], early[0][:].rearrange("p e i -> p i e"))
-        gather(0, 2)
-        gather(1, 2)
-        gather(0, 3)
-        x0_grouped = tile([P, R * PACK], BF16, "x0_grouped")
-        cast_x(x0_grouped, x0_raw[:, :, :R - X0_ON_VECTOR], 0)
-        cast_x(x0_grouped, x0_raw[:, :, R - X0_ON_VECTOR:], R - X0_ON_VECTOR, nc.vector.tensor_copy)
-        w0_q = quantize("w0", w_grouped[0], E4M3)
-        x0_q = quantize("x0", x0_grouped, E4M3, parts=2)
-        gather(1, 3)
-        xm0a_grouped = tile([P, HALF * PACK], BF16, "xm0a_grouped")
-        cast_xm(xm0a_grouped, xm0a_raw[:])
-        w1_grouped = tile([P, N * PACK], BF16, "w1_grouped")
-        nc.scalar.copy(w1_grouped[:].rearrange("p (i t) -> p i t", t=PACK)[:, :, :2], early[1][:].rearrange("p e i -> p i e"))
-        w1_places = w1_grouped[:].rearrange("p (i t) -> p i t", t=PACK)[:, :, 2:]
-        late_by_slot = late.rearrange("p e i -> p i e")
-        nc.scalar.copy(w1_places[:, :WEAVE_ON_SCALAR], late_by_slot[:, :WEAVE_ON_SCALAR])
-        nc.gpsimd.tensor_scalar(w1_places[:, WEAVE_ON_SCALAR:], late_by_slot[:, WEAVE_ON_SCALAR:], 1.0, 0.0, ALU.mult, ALU.add)
+        def group_xm(engine, name, raw, reuse=None):
+            grouped = tile([P, HALF * PACK], BF16, name + "_grouped", reuse)
+            cast_xm(engine, grouped[:], raw)
+            return grouped
 
-        res0 = [subtract(nc.vector, "0%d" % c, scores(c, x0_q, w0_q), y0[c // 2], c % 2) for c in range(4)]
-        th0 = [tanh_grouped("th0%d" % c, res0[c]) for c in range(4)]
-        g0 = [tile([P, HALF * PACK], BF16, "g00"), tile([P, HALF * PACK], BF16, "g01")]
+        def quantize_xm(name, grouped, reuse=None):
+            q = mx_tiles(name, HALF, reuse)
+            quantize(q, grouped[:], E4M3)
+            return q
+
+        def pair(number, xm_q, b, h):
+            dw_ps = bank("pair", number, [P, N])
+            for j in range(2):
+                product(dw_ps[:, j * HALF:(j + 1) * HALF], xm_q, j, g_q[b], h * HALF, (h + 1) * HALF)
+            return dw_ps
+
+        def whole(number, xm_q, b, j):
+            dw_ps = bank("whole", number, [P, N])
+            product(dw_ps[:], xm_q, j, g_q[b], 0, N)
+            return dw_ps
+
+        held = {}
+
+        def copy_dw(engine, dw_ps, pieces, reuse=None):
+            name = "dw%d_%d" % pieces[0][:2]
+            dw = tile([P, dw_ps.shape[1]], F32, name, reuse)
+            copy_on(engine)(dw[:], dw_ps)
+            at = 0
+            for j, first, end in pieces:
+                held[j, first] = (dw, at, end)
+                at = at + end - first
+
+        def put(engine, j, first, end):
+            start = max(f for (w, f) in held if w == j and f <= first)
+            dw, at, limit = held[j, start]
+            assert end <= limit
+            scatter(engine, j, dw[:, at + first - start:at + end - start], first, end)
+            if end == B * N:
+                store(j)
+
+        w1_halves = [tile([P, HALF * PACK], BF16, "w1a_grouped")]
+        w1_raw = tile([P, PACK, N], BF16, "w1_raw")
+
+        def gather1(t):
+            nc.scalar.activation(w1_raw[:, t, :], planes[t][:].indirect(slots(N, 2 * N)), ACT.Copy)
+            if t % 2:
+                nc.scalar.copy(places(w1_halves[0])[:, :, t - 1:t + 1], w1_raw[:, t - 1:t + 1, :HALF].rearrange("p e i -> p i e"))
+
+        for t in range(PACK):
+            gather0(t)
+            gather1(t)
+        quantize(w_q[0], w_grouped[0][:], E4M3)
+        cast_x("scalar", x_grouped[0], x0_raw, 0, 192)
+        cast_x("vector", x_grouped[0], x0_raw, 192, R)
+        for h in range(2):
+            quantize(x_q[0], x_grouped[0][:, h * HALF * PACK:(h + 1) * HALF * PACK], E4M3, h * HALF)
+        w1_halves.append(tile([P, HALF * PACK], BF16, "w1b_grouped", "x0_raw"))
+        cast_xm("scalar", w1_halves[1][:], w1_raw[:, :, HALF:])
+        w_q.append(mx_tiles("w1", N, "x0_grouped"))
+        for h in range(2):
+            quantize(w_q[1], w1_halves[h][:], E4M3, h * HALF)
+
+        a0 = [scores(c, c, x_q[0], w_q[0]) for c in range(4)]
+        xm0a_grouped = group_xm("gpsimd", "xm0a", xm0a_raw[:])
+        th0 = [tanh_grouped("0%d" % c, subtract("0%d" % c, a0[c], y0, c)) for c in range(4)]
+        g0 = [tile([P, HALF * PACK], BF16, "g0%d" % h) for h in range(2)]
         for c in range(2):
             weigh(nc.vector, g0[0], c, th0[c], wt_of(0))
-        quantize_xm(0, 0, xm0a_grouped, "th00")
-        quantize_g(0, 0, g0[0])
-        first = gradient(0, 0)
+        xm0a_q = quantize_xm("xm0a", xm0a_grouped)
+        quantize(g_q[0], g0[0][:], E5M2)
+        first = pair(4, xm0a_q, 0, 0)
+        cast_x("scalar", x_grouped[1], x1_raw, 0, R)
         for c in range(2):
             weigh(nc.vector, g0[1], c, th0[2 + c], wt_of(0))
-        w1_q = quantize("w1", w1_grouped, E4M3, "th02")
-        quantize_g(0, 1, g0[1])
-        prod = [gradient(0, 1)]
-        x1_grouped = tile([P, R * PACK], BF16, "x1_grouped")
-        cast_x(x1_grouped, x1_raw[:], 0)
-        x1_q = quantize("x1", x1_grouped, E4M3)
-        after_x1 = tile([P, 3 * HALF], F32, "after_x1", "x1_raw")
-        scatter(copy_out(first, 0, HALF, dw=after_x1[:, :HALF]))
-        xm0b_grouped = after_x1[:, HALF:].bitcast(BF16)
-        cast_xm(xm0b_grouped, xm0b_raw[:])
-        quantize_xm(0, HALF, xm0b_grouped)
-        after_xm0 = tile([P, N + 3 * PACK * CHUNK], F32, "after_xm0", "xm0b_raw")
-        scatter(copy_out(prod[0], 0, N, dw=after_xm0[:, :N]))
-        a1_sb = after_xm0[:, N:].rearrange("p (c t i) -> p c t i", t=PACK, i=CHUNK)
-        weights1 = tile([P, CHUNK, PACK], F32, "weights1", "x1_grouped")
-        nc.gpsimd.tensor_scalar(weights1[:], wt_of(1), 1.0, 0.0, ALU.mult, ALU.add)
-        a1 = [scores(c, x1_q, w1_q) for c in range(2)] + [scores_turned(2, x1_q, w1_q)]
-        a_sb = [copy_scores(a1_sb[:, c], a1[c]) for c in range(3)]
-        res1 = [subtract(nc.gpsimd, "1%d" % c, a_sb[c], y1, c) for c in range(2)]
-        scatter(copy_out(gradient(0, 2), 0, N))
-        a1.append(scores_turned(3, x1_q, w1_q))
-        held = [gradient(0, 0, 1)]
-        prod = [None, gradient(0, 3)]
-        th1 = [tanh_grouped("th1%d" % c, res1[c]) for c in range(2)]
-        scatter(copy_out(held[0], HALF, N, "residual10"))
-        g1 = [tile([P, HALF * PACK], BF16, "g10")]
+        quantize(g_q[0], g0[1][:], E5M2, HALF)
+        second = pair(5, xm0a_q, 0, 1)
+        quantize(x_q[1], x_grouped[1][:], E4M3)
+        a1 = [scores(c, c, x_q[1], w_q[1]) for c in range(4)]
+        copy_dw("scalar", first[:], [(0, 0, HALF), (1, 0, HALF)])
+        copy_dw("scalar", second[:, :HALF], [(0, HALF, N)])
+        put("scalar", 0, 0, HALF)
+        put("vector", 1, 0, HALF)
+        put("scalar", 0, HALF, N)
+        xm1a_grouped = group_xm("gpsimd", "xm1a", xm1a_raw[:], "x1_grouped")
+        xm0b_grouped = group_xm("gpsimd", "xm0b", xm0b_raw[:])
+        res1 = [subtract("1%d" % c, a1[c], y1, c) for c in range(4)]
+        th1 = [tanh_grouped("1%d" % c, res1[c]) for c in range(3)]
+        copy_dw("scalar", second[:, HALF:], [(1, HALF, N)], "residual11")
+        th1.append(tanh_grouped("13", res1[3]))
+        xm1a_q = quantize_xm("xm1a", xm1a_grouped)
+        xm0b_q = quantize_xm("xm0b", xm0b_grouped)
+        g1 = [tile([P, HALF * PACK], BF16, "g1%d" % h) for h in range(2)]
         for c in range(2):
-            weigh(nc.gpsimd, g1[0], c, th1[c], weights1[:])
-        res1.append(add_turned(a_sb[2], minus_y_turned(tile([P, PACK, CHUNK], F32, "minus_y2"), y1, 2)))
-        after_th11 = tile([P, 3 * PACK * CHUNK], F32, "after_th11", "residual11")
-        xm1a_grouped = after_th11[:, :PACK * CHUNK].bitcast(BF16)
-        last = after_th11[:].rearrange("p (c t i) -> p c t i", t=PACK, i=CHUNK)
-        res1.append(add_turned(copy_scores(last[:, 1], a1[3]), minus_y_turned(last[:, 2], y1, 3)))
-        cast_xm(xm1a_grouped, xm1_raw[:, :, :HALF])
-        quantize_xm(1, 0, xm1a_grouped, "th10")
-        quantize_g(1, 0, g1[0])
-        after_g1a = tile([P, N + PACK * CHUNK], F32, "after_g1a", "th11")
-        scatter(copy_out(prod[1], 0, N, dw=after_g1a[:, :N]))
-        th1.append(tanh_grouped("", res1[2], after_g1a[:, N:]))
-        prod = [gradient(1, j) for j in range(2)]
-        scatter(copy_out(prod[0], 0, HALF))
-        th1.append(tanh_grouped("th13", res1[3]))
-        xm1b_grouped = after_th11[:, 2 * PACK * CHUNK:].bitcast(BF16)
-        cast_xm(xm1b_grouped, xm1_raw[:, :, HALF:])
-        g1.append(tile([P, HALF * PACK], BF16, "g11", "g10"))
-        for c in range(2):
-            weigh(nc.gpsimd, g1[1], c, th1[2 + c], weights1[:])
-        quantize_xm(1, HALF, xm1b_grouped, "th11")
-        quantize_g(1, 1, g1[1])
-        scatter(copy_out(prod[1], 0, HALF, "th13"))
-        for j in range(2):
-            scatter(copy_out(gradient(1, j), HALF, N))
-        for j in range(2, 4):
-            scatter(copy_out(gradient(1, j), 0, N))
+            weigh(nc.vector, g1[0], c, th1[c], wt_of(1))
+        weigh(nc.vector, g1[1], 0, th1[2], wt_of(1))
+        quantize(g_q[1], g1[0][:], E5M2)
+        late3 = whole(0, xm0b_q, 0, 1)
+        third = pair(4, xm1a_q, 1, 0)
+        weigh(nc.vector, g1[1], 1, th1[3], wt_of(1))
+        put("scalar", 1, HALF, N)
+        copy_dw("scalar", late3[:], [(3, 0, N)], "residual13")
+        quantize(g_q[1], g1[1][:], E5M2, HALF)
+        copy_dw("vector", third[:], [(0, N, N + HALF), (1, N, N + HALF)])
+        fourth = pair(5, xm1a_q, 1, 1)
+        xm1b_grouped = group_xm("gpsimd", "xm1b", xm1b_raw[:], "g11")
+        put("vector", 0, N, N + HALF)
+        put("scalar", 3, 0, HALF)
+        put("scalar", 1, N, N + HALF)
+        copy_dw("vector", fourth[:], [(0, N + HALF, 2 * N), (1, N + HALF, 2 * N)])
+        xm1b_q = quantize_xm("xm1b", xm1b_grouped)
+        put("vector", 0, N + HALF, 2 * N)
+        copy_dw("vector", whole(5, xm0b_q, 0, 0)[:], [(2, 0, N)])
+        put("scalar", 3, HALF, N)
+        put("scalar", 1, N + HALF, 2 * N)
+        put("vector", 2, 0, N)
+        copy_dw("scalar", whole(2, xm1b_q, 1, 0)[:], [(2, N, 2 * N)])
+        copy_dw("scalar", whole(3, xm1b_q, 1, 1)[:], [(3, N, 2 * N)])
+        put("vector", 2, N, 2 * N)
+        put("scalar", 3, N, N + HALF)
+        put("scalar", 3, N + HALF, 2 * N)

@@ -175,24 +175,16 @@ def tile_attend_glch_w_kernel(tc, xT, wT, y, wt, xm, offs, out):
             product(dw_ps[:], xm_q, j, g_q[b], 0, N)
             return dw_ps
 
-        held = {}
+        def copy_dw(engine, dw, dw_ps):
+            copy_on(engine)(dw, dw_ps)
 
-        def copy_dw(engine, dw_ps, pieces, reuse=None):
-            name = "dw%d_%d" % pieces[0][:2]
-            dw = tile([P, dw_ps.shape[1]], F32, name, reuse)
-            copy_on(engine)(dw[:], dw_ps)
-            at = 0
-            for j, first, end in pieces:
-                held[j, first] = (dw, at, end)
-                at = at + end - first
+        def put(engine, j, dw, first, end, at=0):
+            scatter(engine, j, dw[:, first - at:end - at], first, end)
 
-        def put(engine, j, first, end):
-            start = max(f for (w, f) in held if w == j and f <= first)
-            dw, at, limit = held[j, start]
-            assert end <= limit
-            scatter(engine, j, dw[:, at + first - start:at + end - start], first, end)
-            if end == B * N:
-                store(j)
+        def product_of(number, xm_q, column, b):
+            dw_ps = bank("whole", number, [P, N])
+            product(dw_ps[:], xm_q, column, g_q[b], 0, N)
+            return dw_ps
 
         w1_halves = [tile([P, HALF * PACK], BF16, "w1a_grouped")]
         w1_raw = tile([P, PACK, N], BF16, "w1_raw")
@@ -232,45 +224,54 @@ def tile_attend_glch_w_kernel(tc, xT, wT, y, wt, xm, offs, out):
         second = pair(5, xm0a_q, 0, 1)
         quantize(x_q[1], x_grouped[1][:], E4M3)
         a1 = [scores(c, c, x_q[1], w_q[1]) for c in range(4)]
-        copy_dw("scalar", first[:], [(0, 0, HALF), (1, 0, HALF)])
-        copy_dw("scalar", second[:, :HALF], [(0, HALF, N)])
-        put("scalar", 0, 0, HALF)
-        put("vector", 1, 0, HALF)
-        put("scalar", 0, HALF, N)
+        dw_first = tile([P, N], F32, "dw_first")
+        copy_dw("scalar", dw_first[:], first[:])
+        put("scalar", 0, dw_first, 0, HALF)
+        put("vector", 1, dw_first, 0, HALF, -HALF)
+        dw0b = tile([P, HALF], F32, "dw0b")
+        copy_dw("scalar", dw0b[:], second[:, :HALF])
+        put("scalar", 0, dw0b, HALF, N, HALF)
+
         xm1a_grouped = group_xm("gpsimd", "xm1a", xm1a_raw[:], "x1_grouped")
         xm0b_grouped = group_xm("gpsimd", "xm0b", xm0b_raw[:])
         res1 = [subtract("1%d" % c, a1[c], y1, c) for c in range(4)]
         th1 = [tanh_grouped("1%d" % c, res1[c]) for c in range(3)]
-        copy_dw("scalar", second[:, HALF:], [(1, HALF, N)], "residual11")
+        dw1b = tile([P, HALF], F32, "dw1b", "residual11")
+        copy_dw("scalar", dw1b[:], second[:, HALF:])
         th1.append(tanh_grouped("13", res1[3]))
-        xm1a_q = quantize_xm("xm1a", xm1a_grouped)
         xm0b_q = quantize_xm("xm0b", xm0b_grouped)
-        g1 = [tile([P, HALF * PACK], BF16, "g1%d" % h) for h in range(2)]
-        for c in range(2):
-            weigh(nc.vector, g1[0], c, th1[c], wt_of(1))
-        weigh(nc.vector, g1[1], 0, th1[2], wt_of(1))
-        quantize(g_q[1], g1[0][:], E5M2)
-        late3 = whole(0, xm0b_q, 0, 1)
-        third = pair(4, xm1a_q, 1, 0)
-        weigh(nc.vector, g1[1], 1, th1[3], wt_of(1))
-        put("scalar", 1, HALF, N)
-        copy_dw("scalar", late3[:], [(3, 0, N)], "residual13")
-        quantize(g_q[1], g1[1][:], E5M2, HALF)
-        copy_dw("vector", third[:], [(0, N, N + HALF), (1, N, N + HALF)])
-        fourth = pair(5, xm1a_q, 1, 1)
-        xm1b_grouped = group_xm("gpsimd", "xm1b", xm1b_raw[:], "g11")
-        put("vector", 0, N, N + HALF)
-        put("scalar", 3, 0, HALF)
-        put("scalar", 1, N, N + HALF)
-        copy_dw("vector", fourth[:], [(0, N + HALF, 2 * N), (1, N + HALF, 2 * N)])
-        xm1b_q = quantize_xm("xm1b", xm1b_grouped)
-        put("vector", 0, N + HALF, 2 * N)
-        copy_dw("vector", whole(5, xm0b_q, 0, 0)[:], [(2, 0, N)])
-        put("scalar", 3, HALF, N)
-        put("scalar", 1, N + HALF, 2 * N)
-        put("vector", 2, 0, N)
-        copy_dw("scalar", whole(2, xm1b_q, 1, 0)[:], [(2, N, 2 * N)])
-        copy_dw("scalar", whole(3, xm1b_q, 1, 1)[:], [(3, N, 2 * N)])
-        put("vector", 2, N, 2 * N)
-        put("scalar", 3, N, N + HALF)
-        put("scalar", 3, N + HALF, 2 * N)
+        xm1a_q = quantize_xm("xm1a", xm1a_grouped)
+        late = [whole(j, xm0b_q, 0, j) for j in range(2)]
+        g1 = tile([P, N * PACK], BF16, "g1")
+        put("scalar", 1, dw1b, HALF, N, HALF)
+        for c in range(4):
+            weigh(nc.vector, g1, c, th1[c], wt_of(1))
+        dw2 = tile([P, 2 * N], F32, "dw2", "residual13")
+        dw3 = tile([P, 2 * N], F32, "dw3", "th12")
+        copy_dw("vector", dw3[:, :N], late[1][:])
+        copy_dw("scalar", dw2[:, :N], late[0][:])
+        quantize(g_q[1], g1[:], E5M2)
+        xm1b_grouped = tile([P, HALF * PACK], BF16, "xm1b_grouped", "g1")
+        xm1b_q = mx_tiles("xm1b", HALF)
+        for j in range(2):
+            cast_xm("gpsimd", xm1b_grouped[:, j * P * PACK:(j + 1) * P * PACK], xm1b_raw[:, :, j * P:(j + 1) * P])
+        last = [whole(4 + j, xm1a_q, 1, j) for j in range(2)]
+        put("vector", 3, dw3, 0, HALF)
+        put("scalar", 2, dw2, 0, 256)
+        dw01 = [tile([P, N], F32, "dw%d1" % j) for j in range(2)]
+        copy_dw("vector", dw01[0][:], last[0][:])
+        copy_dw("scalar", dw01[1][:], last[1][:])
+        quantize(xm1b_q, xm1b_grouped[:, :P * PACK], E4M3)
+        put("vector", 0, dw01[0], N, 2 * N, N)
+        store(0)
+        copy_dw("scalar", dw2[:, N:], whole(6, xm1b_q, 1, 0)[:])
+        quantize(xm1b_q, xm1b_grouped[:, P * PACK:], E4M3, P)
+        put("scalar", 1, dw01[1], N, N + HALF, N)
+        put("scalar", 1, dw01[1], N + HALF, 2 * N, N)
+        store(1)
+        copy_dw("scalar", dw3[:, N:], whole(7, xm1b_q, 1, 1)[:])
+        put("vector", 2, dw2, 256, 2 * N)
+        store(2)
+        put("scalar", 3, dw3, HALF, HALF + 384)
+        put("scalar", 3, dw3, HALF + 384, 2 * N)
+        store(3)

@@ -101,7 +101,7 @@ def tile_attend_glch_w_kernel(tc, xT, wT, y, wt, xm, offs, out):
             return wt_sb[:, b:b + 1, :PACK].to_broadcast([P, CHUNK, PACK])
 
         def product(dw_ps, xm_q, j, g_q, first, end):
-            rows = slice(j % 2 * P, (j % 2 + 1) * P)
+            rows = slice(j * P, (j + 1) * P)
             nc.tensor.matmul_mx(out=dw_ps, lhsT=xm_q[0][:, rows].bitcast(E4M3), lhsT_scale=xm_q[1][:, rows],
                                 rhs=g_q[0][:, first:end].bitcast(E5M2), rhs_scale=g_q[1][:, first:end], start=True, stop=True)
 
@@ -127,17 +127,17 @@ def tile_attend_glch_w_kernel(tc, xT, wT, y, wt, xm, offs, out):
         nc.sync.dma_start(planes[0][:], by_fours(wT)[:, 0, :])
         nc.sync.dma_start(offsets[:], offs)
         nc.sync.dma_start(planes[1][:], by_fours(wT)[:, 1, :])
-        nc.sync.dma_start(wt_sb[:, :, :PACK], wt.rearrange("b (p t) o -> p b (t o)", t=PACK))
+        nc.scalar.dma_start(wt_sb[:, :, :PACK], wt.rearrange("b (p t) o -> p b (t o)", t=PACK))
         nc.sync.dma_start(planes[2][:], by_fours(wT)[:, 2, :])
         nc.sync.dma_start(planes[3][:], by_fours(wT)[:, 3, :])
         x0_raw = load("x0_raw", xT[0])
         y0 = load("y0", y[0])
         xm0a_raw = load("xm0a_raw", xm[0], 0, HALF)
         x1_raw = load("x1_raw", xT[1])
+        xm1_raw = load("xm1_raw", xm[1], 0, 3 * P)
         y1 = load("y1", y[1])
-        xm1a_raw = load("xm1a_raw", xm[1], 0, HALF)
         xm0b_raw = load("xm0b_raw", xm[0], HALF, D)
-        xm1b_raw = load("xm1b_raw", xm[1], HALF, D)
+        xm1_last_raw = load("xm1_last_raw", xm[1], 3 * P, D)
 
         windows = []
         for j in range(D // P):
@@ -151,7 +151,7 @@ def tile_attend_glch_w_kernel(tc, xT, wT, y, wt, xm, offs, out):
 
         x_grouped = [tile([P, R * PACK], BF16, "x%d_grouped" % b) for b in range(B)]
         x_q = [mx_tiles("x%d" % b, R) for b in range(B)]
-        w_q = [mx_tiles("w0", N)]
+        w_first = mx_tiles("w_first", HALF)
         g_q = [mx_tiles("g%d" % b, N) for b in range(B)]
 
         def group_xm(engine, name, raw, reuse=None):
@@ -197,18 +197,19 @@ def tile_attend_glch_w_kernel(tc, xT, wT, y, wt, xm, offs, out):
         for t in range(PACK):
             gather0(t)
             gather1(t)
-        quantize(w_q[0], w_grouped[0][:], E4M3)
+        quantize(w_first, w_grouped[0][:, :HALF * PACK], E4M3)
         cast_x("scalar", x_grouped[0], x0_raw, 0, 192)
         cast_x("vector", x_grouped[0], x0_raw, 192, R)
         for h in range(2):
             quantize(x_q[0], x_grouped[0][:, h * HALF * PACK:(h + 1) * HALF * PACK], E4M3, h * HALF)
         w1_halves.append(tile([P, HALF * PACK], BF16, "w1b_grouped", "x0_raw"))
         cast_xm("scalar", w1_halves[1][:], w1_raw[:, :, HALF:])
-        w_q.append(mx_tiles("w1", N, "x0_grouped"))
+        w_rest = mx_tiles("w_rest", 3 * HALF, "x0_grouped")
+        quantize(w_rest, w_grouped[0][:, HALF * PACK:], E4M3)
         for h in range(2):
-            quantize(w_q[1], w1_halves[h][:], E4M3, h * HALF)
+            quantize(w_rest, w1_halves[h][:], E4M3, (1 + h) * HALF)
 
-        a0 = [scores(c, c, x_q[0], w_q[0]) for c in range(4)]
+        a0 = [scores(c, c % 2, x_q[0], w_rest if c // 2 else w_first) for c in range(4)]
         xm0a_grouped = group_xm("gpsimd", "xm0a", xm0a_raw[:])
         th0 = [tanh_grouped("0%d" % c, subtract("0%d" % c, a0[c], y0, c)) for c in range(4)]
         g0 = [tile([P, HALF * PACK], BF16, "g0%d" % h) for h in range(2)]
@@ -223,7 +224,7 @@ def tile_attend_glch_w_kernel(tc, xT, wT, y, wt, xm, offs, out):
         quantize(g_q[0], g0[1][:], E5M2, HALF)
         second = pair(5, xm0a_q, 0, 1)
         quantize(x_q[1], x_grouped[1][:], E4M3)
-        a1 = [scores(c, c, x_q[1], w_q[1]) for c in range(4)]
+        a1 = [scores(c, 2 + c, x_q[1], w_rest) for c in range(4)]
         dw_first = tile([P, N], F32, "dw_first")
         copy_dw("scalar", dw_first[:], first[:])
         put("scalar", 0, dw_first, 0, HALF)
@@ -232,15 +233,16 @@ def tile_attend_glch_w_kernel(tc, xT, wT, y, wt, xm, offs, out):
         copy_dw("scalar", dw0b[:], second[:, :HALF])
         put("scalar", 0, dw0b, HALF, N, HALF)
 
-        xm1a_grouped = group_xm("gpsimd", "xm1a", xm1a_raw[:], "x1_grouped")
+        xm1_grouped = tile([P, 3 * P * PACK], BF16, "xm1_grouped", "x1_grouped")
+        cast_xm("gpsimd", xm1_grouped[:], xm1_raw[:])
         xm0b_grouped = group_xm("gpsimd", "xm0b", xm0b_raw[:])
         res1 = [subtract("1%d" % c, a1[c], y1, c) for c in range(4)]
-        th1 = [tanh_grouped("1%d" % c, res1[c]) for c in range(3)]
-        dw1b = tile([P, HALF], F32, "dw1b", "residual11")
-        copy_dw("scalar", dw1b[:], second[:, HALF:])
-        th1.append(tanh_grouped("13", res1[3]))
+        th1 = [tanh_grouped("1%d" % c, res1[c]) for c in range(4)]
+        dw1b = tile([P, HALF], F32, "dw1b", "xm1_raw")
+        copy_dw("vector", dw1b[:], second[:, HALF:])
         xm0b_q = quantize_xm("xm0b", xm0b_grouped)
-        xm1a_q = quantize_xm("xm1a", xm1a_grouped)
+        xm1_q = mx_tiles("xm1", D)
+        quantize(xm1_q, xm1_grouped[:], E4M3)
         late = [whole(j, xm0b_q, 0, j) for j in range(2)]
         g1 = tile([P, N * PACK], BF16, "g1")
         put("scalar", 1, dw1b, HALF, N, HALF)
@@ -251,26 +253,24 @@ def tile_attend_glch_w_kernel(tc, xT, wT, y, wt, xm, offs, out):
         copy_dw("vector", dw3[:, :N], late[1][:])
         copy_dw("scalar", dw2[:, :N], late[0][:])
         quantize(g_q[1], g1[:], E5M2)
-        xm1b_grouped = tile([P, HALF * PACK], BF16, "xm1b_grouped", "g1")
-        xm1b_q = mx_tiles("xm1b", HALF)
-        for j in range(2):
-            cast_xm("gpsimd", xm1b_grouped[:, j * P * PACK:(j + 1) * P * PACK], xm1b_raw[:, :, j * P:(j + 1) * P])
-        last = [whole(4 + j, xm1a_q, 1, j) for j in range(2)]
+        xm1_last = tile([P, P * PACK], BF16, "xm1_last", "g1")
+        cast_xm("gpsimd", xm1_last[:], xm1_last_raw[:])
+        last = [whole(4 + j, xm1_q, 1, j) for j in range(3)]
         put("vector", 3, dw3, 0, HALF)
-        put("scalar", 2, dw2, 0, 256)
+        put("scalar", 2, dw2, 0, 320)
         dw01 = [tile([P, N], F32, "dw%d1" % j) for j in range(2)]
         copy_dw("vector", dw01[0][:], last[0][:])
         copy_dw("scalar", dw01[1][:], last[1][:])
-        quantize(xm1b_q, xm1b_grouped[:, :P * PACK], E4M3)
+        copy_dw("scalar", dw2[:, N:], last[2][:])
+        quantize(xm1_q, xm1_last[:], E4M3, 3 * P)
+        last.append(whole(7, xm1_q, 1, 3))
         put("vector", 0, dw01[0], N, 2 * N, N)
         store(0)
-        copy_dw("scalar", dw2[:, N:], whole(6, xm1b_q, 1, 0)[:])
-        quantize(xm1b_q, xm1b_grouped[:, P * PACK:], E4M3, P)
         put("scalar", 1, dw01[1], N, N + HALF, N)
+        copy_dw("scalar", dw3[:, N:], last[3][:])
         put("scalar", 1, dw01[1], N + HALF, 2 * N, N)
         store(1)
-        copy_dw("scalar", dw3[:, N:], whole(7, xm1b_q, 1, 1)[:])
-        put("vector", 2, dw2, 256, 2 * N)
+        put("vector", 2, dw2, 320, 2 * N)
         store(2)
         put("scalar", 3, dw3, HALF, HALF + 384)
         put("scalar", 3, dw3, HALF + 384, 2 * N)

@@ -66,6 +66,11 @@ def tile_attend_glch_w_kernel(tc, xT, wT, y, wt, xm, offs, out):
             src = raw[:].rearrange("p j (m t) -> p m j t", t=PACK)
             copy_on(engine)(dst[:, first // PACK:end // PACK], src[:, first // PACK:end // PACK])
 
+        def cast_x_places(engine, grouped, raw, first, end):
+            dst = grouped[:].rearrange("p (t m j) -> p m j t", t=PACK, j=PACK)
+            src = raw[:].rearrange("p j (m t) -> p m j t", t=PACK)
+            copy_on(engine)(dst[:, :, :, first:end], src[:, :, :, first:end])
+
         def cast_xm(engine, grouped, raw):
             if engine == "gpsimd":
                 copy_on(engine)(grouped.rearrange("p (i t) -> p i t", t=PACK), raw.rearrange("p t i -> p i t"))
@@ -74,31 +79,35 @@ def tile_attend_glch_w_kernel(tc, xT, wT, y, wt, xm, offs, out):
             src = raw.rearrange("p t (c i) -> p c t i", i=RUN)
             copy_on(engine)(dst, src)
 
-        def scores(number, c, x_q, w_q):
-            cols = slice(c * CHUNK, (c + 1) * CHUNK)
-            a_ps = bank("a_ps", number, [P, PACK, CHUNK])
-            for t in range(PACK):
-                rows = slice(t * P, (t + 1) * P)
-                nc.tensor.matmul_mx(out=a_ps[:, t, :], lhsT=x_q[0][:, rows].bitcast(E4M3), lhsT_scale=x_q[1][:, rows],
+        def scores(number, c, x_q, w_q, first):
+            cols = slice(first, first + HALF)
+            a_ps = bank("a_ps", number, [P, 2, HALF])
+            for e in range(2):
+                rows = slice((c % 2 * 2 + e) * P, (c % 2 * 2 + e + 1) * P)
+                nc.tensor.matmul_mx(out=a_ps[:, e, :], lhsT=x_q[0][:, rows].bitcast(E4M3), lhsT_scale=x_q[1][:, rows],
                                     rhs=w_q[0][:, cols].bitcast(E4M3), rhs_scale=w_q[1][:, cols], start=True, stop=True)
             return a_ps
 
         def subtract(name, a_ps, y_sb, c, reuse=None):
-            residual = tile([P, PACK, CHUNK], F32, "residual" + name, reuse)
-            nc.vector.tensor_tensor(residual[:], a_ps[:], y_sb[:, :, c * CHUNK:(c + 1) * CHUNK], ALU.subtract)
+            residual = tile([P, 2, HALF], F32, "residual" + name, reuse)
+            nc.vector.tensor_tensor(residual[:], a_ps[:], y_sb[:, c % 2 * 2:c % 2 * 2 + 2, c // 2 * HALF:(c // 2 + 1) * HALF],
+                                    ALU.subtract)
             return residual
 
-        def tanh_grouped(name, residual, reuse=None):
-            th = tile([P, CHUNK * PACK], F32, "th" + name, reuse)
-            nc.scalar.activation(th[:].rearrange("p (c i t) -> p c t i", i=2, t=PACK),
-                                 residual[:].rearrange("p t (c i) -> p c t i", i=2), ACT.Tanh)
-            return th
+        th_halves = {}
 
-        def weigh(engine, g, c, th, weights):
-            engine.tensor_tensor(places(g)[:, c * CHUNK:(c + 1) * CHUNK], places(th), weights, ALU.mult)
+        def tanh_grouped(name, residual):
+            c = int(name[1])
+            key = name[0] + "ab"[c // 2]
+            if key not in th_halves:
+                th_halves[key] = tile([P, PACK, HALF], F32, "th" + key)
+            nc.scalar.activation(th_halves[key][:, c % 2 * 2:c % 2 * 2 + 2, :], residual[:], ACT.Tanh)
+            return th_halves[key]
 
-        def wt_of(b):
-            return wt_sb[:, b:b + 1, :PACK].to_broadcast([P, CHUNK, PACK])
+        def weigh(engine, g, th, b):
+            engine.tensor_tensor(g.rearrange("p (c i t) -> p c t i", i=RUN, t=PACK),
+                                 th[:].rearrange("p t (c i) -> p c t i", i=RUN),
+                                 wt_sb[:, b, :PACK].unsqueeze(1).unsqueeze(3).to_broadcast([P, HALF // RUN, PACK, RUN]), ALU.mult)
 
         def product(dw_ps, xm_q, j, g_q, first, end):
             rows = slice(j * P, (j + 1) * P)
@@ -198,8 +207,8 @@ def tile_attend_glch_w_kernel(tc, xT, wT, y, wt, xm, offs, out):
             gather0(t)
             gather1(t)
         quantize(w_first, w_grouped[0][:, :HALF * PACK], E4M3)
-        cast_x("scalar", x_grouped[0], x0_raw, 0, 192)
-        cast_x("vector", x_grouped[0], x0_raw, 192, R)
+        cast_x_places("scalar", x_grouped[0], x0_raw, 2, 4)
+        cast_x_places("vector", x_grouped[0], x0_raw, 0, 2)
         for h in range(2):
             quantize(x_q[0], x_grouped[0][:, h * HALF * PACK:(h + 1) * HALF * PACK], E4M3, h * HALF)
         w1_halves.append(tile([P, HALF * PACK], BF16, "w1b_grouped", "x0_raw"))
@@ -209,22 +218,20 @@ def tile_attend_glch_w_kernel(tc, xT, wT, y, wt, xm, offs, out):
         for h in range(2):
             quantize(w_rest, w1_halves[h][:], E4M3, (1 + h) * HALF)
 
-        a0 = [scores(c, c % 2, x_q[0], w_rest if c // 2 else w_first) for c in range(4)]
+        a0 = [scores(c, c, x_q[0], w_rest if c // 2 else w_first, 0) for c in range(4)]
         xm0a_grouped = group_xm("gpsimd", "xm0a", xm0a_raw[:])
         th0 = [tanh_grouped("0%d" % c, subtract("0%d" % c, a0[c], y0, c)) for c in range(4)]
         g0 = [tile([P, HALF * PACK], BF16, "g0%d" % h) for h in range(2)]
-        for c in range(2):
-            weigh(nc.vector, g0[0], c, th0[c], wt_of(0))
+        weigh(nc.vector, g0[0][:], th0[0], 0)
         xm0a_q = quantize_xm("xm0a", xm0a_grouped)
         quantize(g_q[0], g0[0][:], E5M2)
         first = pair(4, xm0a_q, 0, 0)
         cast_x("scalar", x_grouped[1], x1_raw, 0, R)
-        for c in range(2):
-            weigh(nc.vector, g0[1], c, th0[2 + c], wt_of(0))
+        weigh(nc.vector, g0[1][:], th0[2], 0)
         quantize(g_q[0], g0[1][:], E5M2, HALF)
         second = pair(5, xm0a_q, 0, 1)
         quantize(x_q[1], x_grouped[1][:], E4M3)
-        a1 = [scores(c, 2 + c, x_q[1], w_rest) for c in range(4)]
+        a1 = [scores(c, c, x_q[1], w_rest, (1 + c // 2) * HALF) for c in range(4)]
         dw_first = tile([P, N], F32, "dw_first")
         copy_dw("scalar", dw_first[:], first[:])
         put("scalar", 0, dw_first, 0, HALF)
@@ -246,10 +253,10 @@ def tile_attend_glch_w_kernel(tc, xT, wT, y, wt, xm, offs, out):
         late = [whole(j, xm0b_q, 0, j) for j in range(2)]
         g1 = tile([P, N * PACK], BF16, "g1")
         put("scalar", 1, dw1b, HALF, N, HALF)
-        for c in range(4):
-            weigh(nc.vector, g1, c, th1[c], wt_of(1))
+        for h in range(2):
+            weigh(nc.vector, g1[:, h * HALF * PACK:(h + 1) * HALF * PACK], th1[2 * h], 1)
         dw2 = tile([P, 2 * N], F32, "dw2", "residual13")
-        dw3 = tile([P, 2 * N], F32, "dw3", "th12")
+        dw3 = tile([P, 2 * N], F32, "dw3", "th1a")
         copy_dw("vector", dw3[:, :N], late[1][:])
         copy_dw("scalar", dw2[:, :N], late[0][:])
         quantize(g_q[1], g1[:], E5M2)

@@ -1,6 +1,7 @@
 from contextlib import ExitStack
 
 import concourse.mybir as mybir
+from concourse.masks import make_identity
 
 B, N, T, D, R = 2, 512, 2048, 512, 512
 FLOPS = 2 * B * (R * N * D + D * N * R)
@@ -18,8 +19,9 @@ ALU = mybir.AluOpType
 P = 128
 PACK = 4
 PER_COLUMN = 16
-CHUNK = 128
 HALF = 256
+SPLIT = 640
+LATE = 32
 RUN = 4
 
 
@@ -61,16 +63,6 @@ def tile_attend_glch_w_kernel(tc, xT, wT, y, wt, xm, offs, out):
                 return lambda dst, src: nc.gpsimd.tensor_scalar(dst, src, 1.0, 0.0, ALU.mult, ALU.add)
             return nc.vector.tensor_copy if engine == "vector" else nc.scalar.copy
 
-        def cast_x(engine, grouped, raw, first, end):
-            dst = grouped[:].rearrange("p (t m j) -> p m j t", t=PACK, j=PACK)
-            src = raw[:].rearrange("p j (m t) -> p m j t", t=PACK)
-            copy_on(engine)(dst[:, first // PACK:end // PACK], src[:, first // PACK:end // PACK])
-
-        def cast_x_places(engine, grouped, raw, first, end):
-            dst = grouped[:].rearrange("p (t m j) -> p m j t", t=PACK, j=PACK)
-            src = raw[:].rearrange("p j (m t) -> p m j t", t=PACK)
-            copy_on(engine)(dst[:, :, :, first:end], src[:, :, :, first:end])
-
         def cast_xm(engine, grouped, raw):
             if engine == "gpsimd":
                 copy_on(engine)(grouped.rearrange("p (i t) -> p i t", t=PACK), raw.rearrange("p t i -> p i t"))
@@ -88,11 +80,27 @@ def tile_attend_glch_w_kernel(tc, xT, wT, y, wt, xm, offs, out):
                                     rhs=w_q[0][:, cols].bitcast(E4M3), rhs_scale=w_q[1][:, cols], start=True, stop=True)
             return a_ps
 
-        def subtract(name, a_ps, y_sb, c, reuse=None):
-            residual = tile([P, 2, HALF], F32, "residual" + name, reuse)
+        def subtract(name, a_ps, y_sb, c, residual=None):
+            if residual is None:
+                residual = tile([P, 2, HALF], F32, "residual" + name)
             nc.vector.tensor_tensor(residual[:], a_ps[:], y_sb[:, c % 2 * 2:c % 2 * 2 + 2, c // 2 * HALF:(c // 2 + 1) * HALF],
                                     ALU.subtract)
             return residual
+
+        def scores_by_slots(number, x_q, w_q, first):
+            cols = slice(first, first + P)
+            a_ps = bank("a_ps", number, [P, PACK, P])
+            for t in range(PACK):
+                rows = slice(t * P, (t + 1) * P)
+                nc.tensor.matmul_mx(out=a_ps[:, t, :], lhsT=x_q[0][:, rows].bitcast(E4M3), lhsT_scale=x_q[1][:, rows],
+                                    rhs=w_q[0][:, cols].bitcast(E4M3), rhs_scale=w_q[1][:, cols], start=True, stop=True)
+            return a_ps
+
+        def subtract_by_slots(residual, a_ps, y_sb, first):
+            nc.vector.tensor_tensor(residual, a_ps[:], y_sb[:, :, first:first + P], ALU.subtract)
+
+        def tanh_side_by_side(th, residual):
+            nc.scalar.activation(th.rearrange("p (c i t) -> p c t i", i=2, t=PACK), residual.rearrange("p t (c i) -> p c t i", i=2), ACT.Tanh)
 
         th_halves = {}
 
@@ -104,20 +112,21 @@ def tile_attend_glch_w_kernel(tc, xT, wT, y, wt, xm, offs, out):
             nc.scalar.activation(th_halves[key][:, c % 2 * 2:c % 2 * 2 + 2, :], residual[:], ACT.Tanh)
             return th_halves[key]
 
-        def weigh(engine, g, th, b):
-            engine.tensor_tensor(g.rearrange("p (c i t) -> p c t i", i=RUN, t=PACK),
-                                 th[:].rearrange("p t (c i) -> p c t i", i=RUN),
-                                 wt_sb[:, b, :PACK].unsqueeze(1).unsqueeze(3).to_broadcast([P, HALF // RUN, PACK, RUN]), ALU.mult)
+        def weigh_on_vector(g, th, b):
+            nc.vector.tensor_tensor(g.rearrange("p (c i t) -> p c t i", i=RUN, t=PACK),
+                                    th.rearrange("p t (c i) -> p c t i", i=RUN),
+                                    wt_ps[:, b, :, :RUN].unsqueeze(1).to_broadcast([P, th.shape[2] // RUN, PACK, RUN]), ALU.mult)
+
+        def cast_x_pair(engine, name, raw, first, reuse=None):
+            grouped = tile([P, 2 * P * PACK], BF16, name, reuse)
+            copy_on(engine)(grouped[:].rearrange("p (t m j) -> p m j t", t=2, j=PACK),
+                            raw[:].rearrange("p j (m t) -> p m j t", t=PACK)[:, :, :, first:first + 2])
+            return grouped
 
         def product(dw_ps, xm_q, j, g_q, first, end):
             rows = slice(j * P, (j + 1) * P)
             nc.tensor.matmul_mx(out=dw_ps, lhsT=xm_q[0][:, rows].bitcast(E4M3), lhsT_scale=xm_q[1][:, rows],
                                 rhs=g_q[0][:, first:end].bitcast(E5M2), rhs_scale=g_q[1][:, first:end], start=True, stop=True)
-
-        def copy_out(engine, name, dw_ps, reuse=None):
-            dw = tile([P, N], F32, name, reuse)
-            copy_on(engine)(dw[:], dw_ps[:])
-            return dw
 
         def scatter(engine, j, dw, first, end):
             window = windows[j][:].indirect(slots(first, end))
@@ -143,33 +152,34 @@ def tile_attend_glch_w_kernel(tc, xT, wT, y, wt, xm, offs, out):
         y0 = load("y0", y[0])
         xm0a_raw = load("xm0a_raw", xm[0], 0, HALF)
         x1_raw = load("x1_raw", xT[1])
-        xm1_raw = load("xm1_raw", xm[1], 0, 3 * P)
         y1 = load("y1", y[1])
         xm0b_raw = load("xm0b_raw", xm[0], HALF, D)
-        xm1_last_raw = load("xm1_last_raw", xm[1], 3 * P, D)
+        xm1_raw = load("xm1_raw", xm[1])
+
+        identity = tile([P, P], F32, "identity")
+        make_identity(nc, identity[:])
 
         windows = []
         for j in range(D // P):
             windows.append(tile([P, T], F32, "window%d" % j))
             nc.vector.memset(windows[j][:], 0.0)
 
-        w_grouped = [tile([P, N * PACK], BF16, "w0_grouped")]
+        w_vector = tile([P, SPLIT * PACK], BF16, "w_vector")
 
-        def gather0(t, first=0, end=N):
-            nc.vector.tensor_copy(places(w_grouped[0])[:, first:end, t], planes[t][:].indirect(slots(first, end)))
+        def gather_vector(t, first, end):
+            nc.vector.tensor_copy(places(w_vector)[:, first:end, t], planes[t][:].indirect(slots(first, end)))
 
-        x_grouped = [tile([P, R * PACK], BF16, "x%d_grouped" % b) for b in range(B)]
         x_q = [mx_tiles("x%d" % b, R) for b in range(B)]
         w_first = mx_tiles("w_first", HALF)
         g_q = [mx_tiles("g%d" % b, N) for b in range(B)]
 
         def group_xm(engine, name, raw, reuse=None):
-            grouped = tile([P, HALF * PACK], BF16, name + "_grouped", reuse)
+            grouped = tile([P, raw.shape[2] * PACK], BF16, name + "_grouped", reuse)
             cast_xm(engine, grouped[:], raw)
             return grouped
 
         def quantize_xm(name, grouped, reuse=None):
-            q = mx_tiles(name, HALF, reuse)
+            q = mx_tiles(name, grouped.shape[1] // PACK, reuse)
             quantize(q, grouped[:], E4M3)
             return q
 
@@ -190,95 +200,114 @@ def tile_attend_glch_w_kernel(tc, xT, wT, y, wt, xm, offs, out):
         def put(engine, j, dw, first, end, at=0):
             scatter(engine, j, dw[:, first - at:end - at], first, end)
 
-        def product_of(number, xm_q, column, b):
-            dw_ps = bank("whole", number, [P, N])
-            product(dw_ps[:], xm_q, column, g_q[b], 0, N)
-            return dw_ps
+        w_scalar = tile([P, (2 * N - SPLIT) * PACK], BF16, "w_scalar")
+        w_rows = tile([P, PACK, 2 * N - SPLIT], BF16, "w_rows")
 
-        w1_halves = [tile([P, HALF * PACK], BF16, "w1a_grouped")]
-        w1_raw = tile([P, PACK, N], BF16, "w1_raw")
-
-        def gather1(t):
-            nc.scalar.activation(w1_raw[:, t, :], planes[t][:].indirect(slots(N, 2 * N)), ACT.Copy)
+        def gather_scalar(t):
+            nc.scalar.activation(w_rows[:, t, :], planes[t][:].indirect(slots(SPLIT, 2 * N)), ACT.Copy)
             if t % 2:
-                nc.scalar.copy(places(w1_halves[0])[:, :, t - 1:t + 1], w1_raw[:, t - 1:t + 1, :HALF].rearrange("p e i -> p i e"))
+                nc.scalar.copy(places(w_scalar)[:, :, t - 1:t + 1], w_rows[:, t - 1:t + 1, :].rearrange("p e i -> p i e"))
 
-        for t in range(PACK):
-            gather0(t)
-            gather1(t)
-        quantize(w_first, w_grouped[0][:, :HALF * PACK], E4M3)
-        cast_x_places("scalar", x_grouped[0], x0_raw, 2, 4)
-        cast_x_places("vector", x_grouped[0], x0_raw, 0, 2)
-        for h in range(2):
-            quantize(x_q[0], x_grouped[0][:, h * HALF * PACK:(h + 1) * HALF * PACK], E4M3, h * HALF)
-        w1_halves.append(tile([P, HALF * PACK], BF16, "w1b_grouped", "x0_raw"))
-        cast_xm("scalar", w1_halves[1][:], w1_raw[:, :, HALF:])
-        w_rest = mx_tiles("w_rest", 3 * HALF, "x0_grouped")
-        quantize(w_rest, w_grouped[0][:, HALF * PACK:], E4M3)
-        for h in range(2):
-            quantize(w_rest, w1_halves[h][:], E4M3, (1 + h) * HALF)
+        gather_vector(0, 0, SPLIT)
+        gather_scalar(0)
+        wt_spread = tile([P, B, PACK, P // (B * PACK)], F32, "wt_spread")
+        nc.scalar.copy(wt_spread[:], wt_sb[:, :, :PACK].unsqueeze(3).to_broadcast([P, B, PACK, P // (B * PACK)]))
+        wt_turned_ps = bank("wt_turned_ps", 6, [P, P])
+        nc.tensor.transpose(wt_turned_ps[:], wt_spread[:].rearrange("p b t i -> p (b t i)"), identity[:])
+        wt_turned = tile([P, P], F32, "wt_turned")
+        nc.scalar.copy(wt_turned[:], wt_turned_ps[:])
+        wt_bank = bank("wt_bank", 7, [P, P])
+        nc.tensor.transpose(wt_bank[:], wt_turned[:], identity[:])
+        wt_ps = wt_bank[:].rearrange("p (b t i) -> p b t i", b=B, t=PACK)
 
+        weights1 = tile([P, 1, PACK], F32, "weights1")
+        nc.scalar.copy(weights1[:], wt_sb[:, 1:2, :PACK])
+        for t in range(1, PACK - 1):
+            gather_vector(t, 0, SPLIT)
+            gather_scalar(t)
+        gather_vector(PACK - 1, 0, HALF)
+        gather_vector(PACK - 1, HALF, SPLIT)
+        gather_scalar(PACK - 1)
+        quantize(w_first, w_vector[:, :HALF * PACK], E4M3)
+        x0b = cast_x_pair("scalar", "x0b", x0_raw, 2)
+        x0a = cast_x_pair("vector", "x0a", x0_raw, 0)
+        quantize(x_q[0], x0a[:], E4M3)
+        quantize(x_q[0], x0b[:], E4M3, HALF)
+        w_rest = mx_tiles("w_rest", 3 * HALF, "x0_raw")
+        quantize(w_rest, w_vector[:, HALF * PACK:], E4M3)
+        quantize(w_rest, w_scalar[:], E4M3, SPLIT - HALF)
         a0 = [scores(c, c, x_q[0], w_rest if c // 2 else w_first, 0) for c in range(4)]
         xm0a_grouped = group_xm("gpsimd", "xm0a", xm0a_raw[:])
         th0 = [tanh_grouped("0%d" % c, subtract("0%d" % c, a0[c], y0, c)) for c in range(4)]
         g0 = [tile([P, HALF * PACK], BF16, "g0%d" % h) for h in range(2)]
-        weigh(nc.vector, g0[0][:], th0[0], 0)
+        weigh_on_vector(g0[0][:], th0[0][:], 0)
         xm0a_q = quantize_xm("xm0a", xm0a_grouped)
         quantize(g_q[0], g0[0][:], E5M2)
-        first = pair(4, xm0a_q, 0, 0)
-        cast_x("scalar", x_grouped[1], x1_raw, 0, R)
-        weigh(nc.vector, g0[1][:], th0[2], 0)
+        first = [bank("first%d" % j, 4 + 2 * j, [P, HALF]) for j in range(2)]
+        for j in range(2):
+            product(first[j][:], xm0a_q, j, g_q[0], 0, HALF)
+        x1a = cast_x_pair("scalar", "x1a", x1_raw, 0)
+        weigh_on_vector(g0[1][:], th0[2][:], 0)
+        x1b = cast_x_pair("vector", "x1b", x1_raw, 2)
+        dw0 = [tile([P, HALF], F32, "dw0%d" % h) for h in range(2)]
+        dw1 = [tile([P, HALF], F32, "dw10")]
+        copy_dw("scalar", dw0[0][:], first[0][:])
+        copy_dw("scalar", dw1[0][:], first[1][:])
+        put("scalar", 0, dw0[0], 0, HALF)
         quantize(g_q[0], g0[1][:], E5M2, HALF)
+        quantize(x_q[1], x1a[:], E4M3)
+        quantize(x_q[1], x1b[:], E4M3, HALF)
         second = pair(5, xm0a_q, 0, 1)
-        quantize(x_q[1], x_grouped[1][:], E4M3)
-        a1 = [scores(c, c, x_q[1], w_rest, (1 + c // 2) * HALF) for c in range(4)]
-        dw_first = tile([P, N], F32, "dw_first")
-        copy_dw("scalar", dw_first[:], first[:])
-        put("scalar", 0, dw_first, 0, HALF)
-        put("vector", 1, dw_first, 0, HALF, -HALF)
-        dw0b = tile([P, HALF], F32, "dw0b")
-        copy_dw("scalar", dw0b[:], second[:, :HALF])
-        put("scalar", 0, dw0b, HALF, N, HALF)
-
-        xm1_grouped = tile([P, 3 * P * PACK], BF16, "xm1_grouped", "x1_grouped")
-        cast_xm("gpsimd", xm1_grouped[:], xm1_raw[:])
-        xm0b_grouped = group_xm("gpsimd", "xm0b", xm0b_raw[:])
-        res1 = [subtract("1%d" % c, a1[c], y1, c) for c in range(4)]
-        th1 = [tanh_grouped("1%d" % c, res1[c]) for c in range(4)]
-        dw1b = tile([P, HALF], F32, "dw1b", "xm1_raw")
-        copy_dw("vector", dw1b[:], second[:, HALF:])
+        a1 = [scores_by_slots(c, x_q[1], w_rest, HALF + c * P) for c in range(2)] + [scores(c, c, x_q[1], w_rest, 2 * HALF) for c in range(2, 4)]
+        xm0b_grouped = group_xm("gpsimd", "xm0b", xm0b_raw[:], "x1b")
+        put("vector", 1, dw1[0], 0, HALF)
+        copy_dw("scalar", dw0[1][:], second[:, :HALF])
+        put("scalar", 0, dw0[1], HALF, N, HALF)
+        residual10 = tile([P, PACK, P], F32, "residual10")
+        subtract_by_slots(residual10[:], a1[0], y1, 0)
         xm0b_q = quantize_xm("xm0b", xm0b_grouped)
-        xm1_q = mx_tiles("xm1", D)
-        quantize(xm1_q, xm1_grouped[:], E4M3)
-        late = [whole(j, xm0b_q, 0, j) for j in range(2)]
+        xm1a_grouped = group_xm("gpsimd", "xm1a", xm1_raw[:, :, :HALF], "x1b")
+        late = [whole(4 + 2 * j, xm0b_q, 0, j) for j in range(2)]
+        held = tile([P, 3 * N], F32, "held", "xm0b_raw")
+        residual11 = held[:, :N].rearrange("p (t i) -> p t i", t=PACK)
+        subtract_by_slots(residual11, a1[1], y1, P)
+        res1 = [subtract("", a1[c], y1, c, held[:, (c - 1) * N:c * N].rearrange("p (t i) -> p t i", t=2)) for c in range(2, 4)]
+        th1a_dw3 = tile([P, HALF * PACK - LATE + 2 * N], F32, "th1a_dw3")
+        th1a = th1a_dw3[:, :HALF * PACK]
+        dw3 = th1a_dw3[:, HALF * PACK - LATE:]
+        tanh_side_by_side(th1a[:, :N], residual10[:])
+        tanh_side_by_side(th1a[:, N:], residual11)
+        th1b = [tanh_grouped("1%d" % (2 + c), res1[c]) for c in range(2)][0]
         g1 = tile([P, N * PACK], BF16, "g1")
-        put("scalar", 1, dw1b, HALF, N, HALF)
-        for h in range(2):
-            weigh(nc.vector, g1[:, h * HALF * PACK:(h + 1) * HALF * PACK], th1[2 * h], 1)
-        dw2 = tile([P, 2 * N], F32, "dw2", "residual13")
-        dw3 = tile([P, 2 * N], F32, "dw3", "th1a")
-        copy_dw("vector", dw3[:, :N], late[1][:])
-        copy_dw("scalar", dw2[:, :N], late[0][:])
+        nc.gpsimd.tensor_tensor(places(g1)[:, :HALF], th1a.rearrange("p (i t) -> p i t", t=PACK), weights1[:].to_broadcast([P, HALF, PACK]), ALU.mult)
+        dw2 = tile([P, 2 * N], F32, "dw2")
+        copy_dw("vector", held[:, :HALF], second[:, HALF:])
+        copy_dw("vector", dw2[:, :N], late[0][:])
+        copy_dw("vector", dw3[:, LATE:N], late[1][:, LATE:])
+        put("scalar", 1, held, HALF, N, HALF)
+        weigh_on_vector(g1[:, HALF * PACK:], th1b[:], 1)
+        copy_dw("vector", dw3[:, :LATE], late[1][:, :LATE])
+        xm1a_q = quantize_xm("xm1a", xm1a_grouped, "weights1")
         quantize(g_q[1], g1[:], E5M2)
-        xm1_last = tile([P, P * PACK], BF16, "xm1_last", "g1")
-        cast_xm("gpsimd", xm1_last[:], xm1_last_raw[:])
-        last = [whole(4 + j, xm1_q, 1, j) for j in range(3)]
-        put("vector", 3, dw3, 0, HALF)
+        xm1b_grouped = group_xm("gpsimd", "xm1b", xm1_raw[:, :, HALF:], "x1b")
+        last = [whole(j, xm1a_q, 1, j) for j in range(2)]
         put("scalar", 2, dw2, 0, 320)
+        put("vector", 3, dw3, 0, 256)
         dw01 = [tile([P, N], F32, "dw%d1" % j) for j in range(2)]
-        copy_dw("vector", dw01[0][:], last[0][:])
-        copy_dw("scalar", dw01[1][:], last[1][:])
-        copy_dw("scalar", dw2[:, N:], last[2][:])
-        quantize(xm1_q, xm1_last[:], E4M3, 3 * P)
-        last.append(whole(7, xm1_q, 1, 3))
+        copy_dw("scalar", dw01[0][:], last[0][:])
+        copy_dw("scalar", dw01[1][:, :HALF], last[1][:, :HALF])
+        copy_dw("scalar", dw01[1][:, HALF:], last[1][:, HALF:])
+        xm1b_q = quantize_xm("xm1b", xm1b_grouped)
+        last = last + [whole(2 + j, xm1b_q, 1, j) for j in range(2)]
         put("vector", 0, dw01[0], N, 2 * N, N)
         store(0)
         put("scalar", 1, dw01[1], N, N + HALF, N)
+        copy_dw("scalar", dw2[:, N:], last[2][:])
         copy_dw("scalar", dw3[:, N:], last[3][:])
         put("scalar", 1, dw01[1], N + HALF, 2 * N, N)
         store(1)
         put("vector", 2, dw2, 320, 2 * N)
         store(2)
-        put("scalar", 3, dw3, HALF, HALF + 384)
-        put("scalar", 3, dw3, HALF + 384, 2 * N)
+        put("scalar", 3, dw3, 256, (256 + 2 * N) // 2)
+        put("scalar", 3, dw3, (256 + 2 * N) // 2, 2 * N)
         store(3)

@@ -22,6 +22,7 @@ PER_COLUMN = 16
 HALF = 256
 SPLIT = 640
 LATE = 32
+ON_VECTOR = 32
 RUN = 4
 
 
@@ -117,11 +118,9 @@ def tile_attend_glch_w_kernel(tc, xT, wT, y, wt, xm, offs, out):
                                     th.rearrange("p t (c i) -> p c t i", i=RUN),
                                     wt_ps[:, b, :, :RUN].unsqueeze(1).to_broadcast([P, th.shape[2] // RUN, PACK, RUN]), ALU.mult)
 
-        def cast_x_pair(engine, name, raw, first, reuse=None):
-            grouped = tile([P, 2 * P * PACK], BF16, name, reuse)
-            copy_on(engine)(grouped[:].rearrange("p (t m j) -> p m j t", t=2, j=PACK),
-                            raw[:].rearrange("p j (m t) -> p m j t", t=PACK)[:, :, :, first:first + 2])
-            return grouped
+        def cast_x_pair(engine, grouped, raw, place, first=0, end=P):
+            copy_on(engine)(grouped[:].rearrange("p (t m j) -> p m j t", t=2, j=PACK)[:, first:end],
+                            raw[:].rearrange("p j (m t) -> p m j t", t=PACK)[:, first:end, :, place:place + 2])
 
         def product(dw_ps, xm_q, j, g_q, first, end):
             rows = slice(j * P, (j + 1) * P)
@@ -135,8 +134,8 @@ def tile_attend_glch_w_kernel(tc, xT, wT, y, wt, xm, offs, out):
             else:
                 nc.scalar.activation(window, dw, ACT.Copy)
 
-        def store(j):
-            nc.sync.dma_start(out[j * P:(j + 1) * P, :], windows[j][:])
+        def store(j, queue=nc.sync):
+            queue.dma_start(out[j * P:(j + 1) * P, :], windows[j][:])
 
         offsets = tile([P, B * N // PER_COLUMN], U16, "offsets")
         wt_rows = tile([P, B * 2 * PACK], F32, "wt_rows")
@@ -153,14 +152,18 @@ def tile_attend_glch_w_kernel(tc, xT, wT, y, wt, xm, offs, out):
         xm0a_raw = load("xm0a_raw", xm[0], 0, HALF)
         x1_raw = load("x1_raw", xT[1])
         y1 = load("y1", y[1])
-        xm0b_raw = load("xm0b_raw", xm[0], HALF, D)
+        stage = tile([P, HALF - LATE + 3 * N], F32, "stage")
+        dw1b = stage[:, :HALF]
+        held = stage[:, HALF - LATE:]
+        xm0b_raw = held[:, N - LATE // 2:3 * N - LATE // 2].rearrange("p (t c) -> p t c", t=PACK)
+        nc.sync.dma_start(xm0b_raw, by_fours(xm[0])[:, :, HALF:])
         xm1_raw = load("xm1_raw", xm[1])
 
         identity = tile([P, P], F32, "identity")
         make_identity(nc, identity[:])
 
         windows = []
-        for j in range(D // P):
+        for j in range(D // P - 1):
             windows.append(tile([P, T], F32, "window%d" % j))
             nc.vector.memset(windows[j][:], 0.0)
 
@@ -210,6 +213,8 @@ def tile_attend_glch_w_kernel(tc, xT, wT, y, wt, xm, offs, out):
 
         gather_vector(0, 0, SPLIT)
         gather_scalar(0)
+        windows.append(tile([P, T], F32, "window3", "plane0"))
+        nc.gpsimd.memset(windows[3][:], 0.0)
         wt_spread = tile([P, B, PACK, P // (B * PACK)], F32, "wt_spread")
         nc.scalar.copy(wt_spread[:], wt_sb[:, :, :PACK].unsqueeze(3).to_broadcast([P, B, PACK, P // (B * PACK)]))
         wt_turned_ps = bank("wt_turned_ps", 6, [P, P])
@@ -229,8 +234,9 @@ def tile_attend_glch_w_kernel(tc, xT, wT, y, wt, xm, offs, out):
         gather_vector(PACK - 1, HALF, SPLIT)
         gather_scalar(PACK - 1)
         quantize(w_first, w_vector[:, :HALF * PACK], E4M3)
-        x0b = cast_x_pair("scalar", "x0b", x0_raw, 2)
-        x0a = cast_x_pair("vector", "x0a", x0_raw, 0)
+        x0a, x0b, x1a, x1b = [tile([P, 2 * P * PACK], BF16, name) for name in ("x0a", "x0b", "x1a", "x1b")]
+        cast_x_pair("scalar", x0b, x0_raw, 2)
+        cast_x_pair("vector", x0a, x0_raw, 0)
         quantize(x_q[0], x0a[:], E4M3)
         quantize(x_q[0], x0b[:], E4M3, HALF)
         w_rest = mx_tiles("w_rest", 3 * HALF, "x0_raw")
@@ -246,9 +252,9 @@ def tile_attend_glch_w_kernel(tc, xT, wT, y, wt, xm, offs, out):
         first = [bank("first%d" % j, 4 + 2 * j, [P, HALF]) for j in range(2)]
         for j in range(2):
             product(first[j][:], xm0a_q, j, g_q[0], 0, HALF)
-        x1a = cast_x_pair("scalar", "x1a", x1_raw, 0)
+        cast_x_pair("scalar", x1a, x1_raw, 0)
         weigh_on_vector(g0[1][:], th0[2][:], 0)
-        x1b = cast_x_pair("vector", "x1b", x1_raw, 2)
+        cast_x_pair("vector", x1b, x1_raw, 2)
         dw0 = [tile([P, HALF], F32, "dw0%d" % h) for h in range(2)]
         dw1 = [tile([P, HALF], F32, "dw10")]
         copy_dw("scalar", dw0[0][:], first[0][:])
@@ -258,33 +264,35 @@ def tile_attend_glch_w_kernel(tc, xT, wT, y, wt, xm, offs, out):
         quantize(x_q[1], x1a[:], E4M3)
         quantize(x_q[1], x1b[:], E4M3, HALF)
         second = pair(5, xm0a_q, 0, 1)
-        a1 = [scores_by_slots(c, x_q[1], w_rest, HALF + c * P) for c in range(2)] + [scores(c, c, x_q[1], w_rest, 2 * HALF) for c in range(2, 4)]
-        xm0b_grouped = group_xm("gpsimd", "xm0b", xm0b_raw[:], "x1b")
+        a1 = [scores_by_slots(c, x_q[1], w_rest, HALF + (1 - c) * P) for c in range(2)] + [scores(c, c, x_q[1], w_rest, 2 * HALF) for c in range(2, 4)]
+        xm0b_grouped = group_xm("gpsimd", "xm0b", xm0b_raw, "x1b")
         put("vector", 1, dw1[0], 0, HALF)
         copy_dw("scalar", dw0[1][:], second[:, :HALF])
+        copy_dw("scalar", dw1b[:, :HALF - LATE], second[:, HALF:N - LATE])
         put("scalar", 0, dw0[1], HALF, N, HALF)
         residual10 = tile([P, PACK, P], F32, "residual10")
-        subtract_by_slots(residual10[:], a1[0], y1, 0)
+        subtract_by_slots(residual10[:], a1[0], y1, P)
         xm0b_q = quantize_xm("xm0b", xm0b_grouped)
         xm1a_grouped = group_xm("gpsimd", "xm1a", xm1_raw[:, :, :HALF], "x1b")
         late = [whole(4 + 2 * j, xm0b_q, 0, j) for j in range(2)]
-        held = tile([P, 3 * N], F32, "held", "xm0b_raw")
         residual11 = held[:, :N].rearrange("p (t i) -> p t i", t=PACK)
-        subtract_by_slots(residual11, a1[1], y1, P)
+        subtract_by_slots(residual11, a1[1], y1, 0)
         res1 = [subtract("", a1[c], y1, c, held[:, (c - 1) * N:c * N].rearrange("p (t i) -> p t i", t=2)) for c in range(2, 4)]
         th1a_dw3 = tile([P, HALF * PACK - LATE + 2 * N], F32, "th1a_dw3")
         th1a = th1a_dw3[:, :HALF * PACK]
         dw3 = th1a_dw3[:, HALF * PACK - LATE:]
-        tanh_side_by_side(th1a[:, :N], residual10[:])
-        tanh_side_by_side(th1a[:, N:], residual11)
+        tanh_side_by_side(th1a[:, N:], residual10[:])
+        tanh_side_by_side(th1a[:, :N], residual11)
         th1b = [tanh_grouped("1%d" % (2 + c), res1[c]) for c in range(2)][0]
         g1 = tile([P, N * PACK], BF16, "g1")
-        nc.gpsimd.tensor_tensor(places(g1)[:, :HALF], th1a.rearrange("p (i t) -> p i t", t=PACK), weights1[:].to_broadcast([P, HALF, PACK]), ALU.mult)
+        th1a_places = th1a.rearrange("p (i t) -> p i t", t=PACK)
+        nc.gpsimd.tensor_tensor(places(g1)[:, ON_VECTOR:HALF], th1a_places[:, ON_VECTOR:], weights1[:].to_broadcast([P, HALF - ON_VECTOR, PACK]), ALU.mult)
         dw2 = tile([P, 2 * N], F32, "dw2")
-        copy_dw("vector", held[:, :HALF], second[:, HALF:])
+        copy_dw("vector", dw1b[:, HALF - LATE:], second[:, N - LATE:])
         copy_dw("vector", dw2[:, :N], late[0][:])
         copy_dw("vector", dw3[:, LATE:N], late[1][:, LATE:])
-        put("scalar", 1, held, HALF, N, HALF)
+        put("scalar", 1, dw1b, HALF, N, HALF)
+        nc.vector.tensor_tensor(places(g1)[:, :ON_VECTOR], th1a_places[:, :ON_VECTOR], wt_ps[:, 1, :, 0].unsqueeze(1).to_broadcast([P, ON_VECTOR, PACK]), ALU.mult)
         weigh_on_vector(g1[:, HALF * PACK:], th1b[:], 1)
         copy_dw("vector", dw3[:, :LATE], late[1][:, :LATE])
         xm1a_q = quantize_xm("xm1a", xm1a_grouped, "weights1")
@@ -310,4 +318,4 @@ def tile_attend_glch_w_kernel(tc, xT, wT, y, wt, xm, offs, out):
         store(2)
         put("scalar", 3, dw3, 256, (256 + 2 * N) // 2)
         put("scalar", 3, dw3, (256 + 2 * N) // 2, 2 * N)
-        store(3)
+        store(3, nc.scalar)

@@ -20,7 +20,7 @@ P = 128
 PACK = 4
 PER_COLUMN = 16
 HALF = 256
-SPLIT = 640
+SPLIT = 512
 LATE = 32
 ON_VECTOR = 32
 RUN = 4
@@ -204,12 +204,9 @@ def tile_attend_glch_w_kernel(tc, xT, wT, y, wt, xm, offs, out):
             scatter(engine, j, dw[:, first - at:end - at], first, end)
 
         w_scalar = tile([P, (2 * N - SPLIT) * PACK], BF16, "w_scalar")
-        w_rows = tile([P, PACK, 2 * N - SPLIT], BF16, "w_rows")
 
         def gather_scalar(t):
-            nc.scalar.activation(w_rows[:, t, :], planes[t][:].indirect(slots(SPLIT, 2 * N)), ACT.Copy)
-            if t % 2:
-                nc.scalar.copy(places(w_scalar)[:, :, t - 1:t + 1], w_rows[:, t - 1:t + 1, :].rearrange("p e i -> p i e"))
+            nc.scalar.activation(places(w_scalar)[:, :, t], planes[t][:].indirect(slots(SPLIT, 2 * N)), ACT.Copy)
 
         gather_vector(0, 0, SPLIT)
         gather_scalar(0)

@@ -23,7 +23,7 @@ HALF = 256
 SPLIT = 512
 LATE = 32
 ON_VECTOR = 32
-RUN = 4
+RUN = 2
 
 
 def tile_attend_glch_w_kernel(tc, xT, wT, y, wt, xm, offs, out):

from contextlib import ExitStack

import concourse.mybir as mybir
from concourse.masks import make_identity

B, N, T, D, R = 2, 512, 2048, 512, 512
FLOPS = 2 * B * (R * N * D + D * N * R)

F32 = mybir.dt.float32
BF16 = mybir.dt.bfloat16
U32 = mybir.dt.uint32
U16 = mybir.dt.uint16
U8 = mybir.dt.uint8
E4M3 = mybir.dt.float8_e4m3fn_x4
E5M2 = mybir.dt.float8_e5m2_x4
ACT = mybir.ActivationFunctionType
ALU = mybir.AluOpType

P = 128
PACK = 4
PER_COLUMN = 16
HALF = 256
SPLIT = 512
LATE = 32
ON_VECTOR = 32
RUN = 2


def tile_attend_glch_w_kernel(tc, xT, wT, y, wt, xm, offs, out):
    nc = tc.nc
    with ExitStack() as ctx:
        sb = ctx.enter_context(tc.tile_pool(name="sb", bufs=1))
        ps = ctx.enter_context(tc.psum_pool(name="ps", bufs=1))

        def tile(shape, dtype, name, reuse=None):
            return sb.tile(shape, dtype, name=name, tag=reuse or name, align_bytes=64)

        def bank(name, number, shape):
            return ps.tile(shape, F32, name=name, tag="bank%d" % number)

        def by_fours(rows):
            return rows.rearrange("(p t) c -> p t c", t=PACK)

        def load(name, rows, first=0, end=512):
            raw = tile([P, PACK, end - first], F32, name)
            nc.sync.dma_start(raw[:], by_fours(rows)[:, :, first:end])
            return raw

        def slots(first, end):
            return offsets[:, first // PER_COLUMN:end // PER_COLUMN]

        def mx_tiles(name, width, reuse=None):
            return tile([P, width], U32, name + "_codes", reuse), tile([P, width], U8, name + "_scales")

        def quantize(q, grouped, fmt, first=0):
            end = first + grouped.shape[1] // PACK
            nc.vector.quantize_mx(out=q[0][:, first:end].bitcast(fmt), scales=q[1][:, first:end], in_=grouped)

        def places(grouped):
            return grouped[:].rearrange("p (i t) -> p i t", t=PACK)

        def copy_on(engine):
            if engine == "gpsimd":
                return lambda dst, src: nc.gpsimd.tensor_scalar(dst, src, 1.0, 0.0, ALU.mult, ALU.add)
            return nc.vector.tensor_copy if engine == "vector" else nc.scalar.copy

        def cast_xm(engine, grouped, raw):
            if engine == "gpsimd":
                copy_on(engine)(grouped.rearrange("p (i t) -> p i t", t=PACK), raw.rearrange("p t i -> p i t"))
                return
            dst = grouped.rearrange("p (c i t) -> p c t i", i=RUN, t=PACK)
            src = raw.rearrange("p t (c i) -> p c t i", i=RUN)
            copy_on(engine)(dst, src)

        def scores(number, c, x_q, w_q, first):
            cols = slice(first, first + HALF)
            a_ps = bank("a_ps", number, [P, 2, HALF])
            for e in range(2):
                rows = slice((c % 2 * 2 + e) * P, (c % 2 * 2 + e + 1) * P)
                nc.tensor.matmul_mx(out=a_ps[:, e, :], lhsT=x_q[0][:, rows].bitcast(E4M3), lhsT_scale=x_q[1][:, rows],
                                    rhs=w_q[0][:, cols].bitcast(E4M3), rhs_scale=w_q[1][:, cols], start=True, stop=True)
            return a_ps

        def subtract(name, a_ps, y_sb, c, residual=None):
            if residual is None:
                residual = tile([P, 2, HALF], F32, "residual" + name)
            nc.vector.tensor_tensor(residual[:], a_ps[:], y_sb[:, c % 2 * 2:c % 2 * 2 + 2, c // 2 * HALF:(c // 2 + 1) * HALF],
                                    ALU.subtract)
            return residual

        def scores_by_slots(number, x_q, w_q, first):
            cols = slice(first, first + P)
            a_ps = bank("a_ps", number, [P, PACK, P])
            for t in range(PACK):
                rows = slice(t * P, (t + 1) * P)
                nc.tensor.matmul_mx(out=a_ps[:, t, :], lhsT=x_q[0][:, rows].bitcast(E4M3), lhsT_scale=x_q[1][:, rows],
                                    rhs=w_q[0][:, cols].bitcast(E4M3), rhs_scale=w_q[1][:, cols], start=True, stop=True)
            return a_ps

        def subtract_by_slots(residual, a_ps, y_sb, first):
            nc.vector.tensor_tensor(residual, a_ps[:], y_sb[:, :, first:first + P], ALU.subtract)

        def tanh_side_by_side(th, residual):
            nc.scalar.activation(th.rearrange("p (c i t) -> p c t i", i=2, t=PACK), residual.rearrange("p t (c i) -> p c t i", i=2), ACT.Tanh)

        th_halves = {}

        def tanh_grouped(name, residual):
            c = int(name[1])
            key = name[0] + "ab"[c // 2]
            if key not in th_halves:
                th_halves[key] = tile([P, PACK, HALF], F32, "th" + key)
            nc.scalar.activation(th_halves[key][:, c % 2 * 2:c % 2 * 2 + 2, :], residual[:], ACT.Tanh)
            return th_halves[key]

        def weigh_on_vector(g, th, b):
            nc.vector.tensor_tensor(g.rearrange("p (c i t) -> p c t i", i=RUN, t=PACK),
                                    th.rearrange("p t (c i) -> p c t i", i=RUN),
                                    wt_ps[:, b, :, :RUN].unsqueeze(1).to_broadcast([P, th.shape[2] // RUN, PACK, RUN]), ALU.mult)

        def cast_x_pair(engine, grouped, raw, place, first=0, end=P):
            copy_on(engine)(grouped[:].rearrange("p (t m j) -> p m j t", t=2, j=PACK)[:, first:end],
                            raw[:].rearrange("p j (m t) -> p m j t", t=PACK)[:, first:end, :, place:place + 2])

        def product(dw_ps, xm_q, j, g_q, first, end):
            rows = slice(j * P, (j + 1) * P)
            nc.tensor.matmul_mx(out=dw_ps, lhsT=xm_q[0][:, rows].bitcast(E4M3), lhsT_scale=xm_q[1][:, rows],
                                rhs=g_q[0][:, first:end].bitcast(E5M2), rhs_scale=g_q[1][:, first:end], start=True, stop=True)

        def scatter(engine, j, dw, first, end):
            window = windows[j][:].indirect(slots(first, end))
            if engine == "vector":
                nc.vector.tensor_copy(window, dw)
            else:
                nc.scalar.activation(window, dw, ACT.Copy)

        def store(j, queue=nc.sync):
            queue.dma_start(out[j * P:(j + 1) * P, :], windows[j][:])

        offsets = tile([P, B * N // PER_COLUMN], U16, "offsets")
        wt_rows = tile([P, B * 2 * PACK], F32, "wt_rows")
        wt_sb = wt_rows[:].rearrange("p (b t) -> p b t", b=B)
        planes = [tile([P, T], F32, "plane%d" % t) for t in range(PACK)]
        nc.sync.dma_start(planes[0][:], by_fours(wT)[:, 0, :])
        nc.sync.dma_start(offsets[:], offs)
        nc.sync.dma_start(planes[1][:], by_fours(wT)[:, 1, :])
        nc.scalar.dma_start(wt_sb[:, :, :PACK], wt.rearrange("b (p t) o -> p b (t o)", t=PACK))
        nc.sync.dma_start(planes[2][:], by_fours(wT)[:, 2, :])
        nc.sync.dma_start(planes[3][:], by_fours(wT)[:, 3, :])
        x0_raw = load("x0_raw", xT[0])
        y0 = load("y0", y[0])
        xm0a_raw = load("xm0a_raw", xm[0], 0, HALF)
        x1_raw = load("x1_raw", xT[1])
        y1 = load("y1", y[1])
        stage = tile([P, HALF - LATE + 3 * N], F32, "stage")
        dw1b = stage[:, :HALF]
        held = stage[:, HALF - LATE:]
        xm0b_raw = held[:, N - LATE // 2:3 * N - LATE // 2].rearrange("p (t c) -> p t c", t=PACK)
        nc.sync.dma_start(xm0b_raw, by_fours(xm[0])[:, :, HALF:])
        xm1_raw = load("xm1_raw", xm[1])

        identity = tile([P, P], F32, "identity")
        make_identity(nc, identity[:])

        windows = []
        for j in range(D // P - 1):
            windows.append(tile([P, T], F32, "window%d" % j))
            nc.vector.memset(windows[j][:], 0.0)

        w_vector = tile([P, SPLIT * PACK], BF16, "w_vector")

        def gather_vector(t, first, end):
            nc.vector.tensor_copy(places(w_vector)[:, first:end, t], planes[t][:].indirect(slots(first, end)))

        x_q = [mx_tiles("x%d" % b, R) for b in range(B)]
        w_first = mx_tiles("w_first", HALF)
        g_q = [mx_tiles("g%d" % b, N) for b in range(B)]

        def group_xm(engine, name, raw, reuse=None):
            grouped = tile([P, raw.shape[2] * PACK], BF16, name + "_grouped", reuse)
            cast_xm(engine, grouped[:], raw)
            return grouped

        def quantize_xm(name, grouped, reuse=None):
            q = mx_tiles(name, grouped.shape[1] // PACK, reuse)
            quantize(q, grouped[:], E4M3)
            return q

        def pair(number, xm_q, b, h):
            dw_ps = bank("pair", number, [P, N])
            for j in range(2):
                product(dw_ps[:, j * HALF:(j + 1) * HALF], xm_q, j, g_q[b], h * HALF, (h + 1) * HALF)
            return dw_ps

        def whole(number, xm_q, b, j):
            dw_ps = bank("whole", number, [P, N])
            product(dw_ps[:], xm_q, j, g_q[b], 0, N)
            return dw_ps

        def copy_dw(engine, dw, dw_ps):
            copy_on(engine)(dw, dw_ps)

        def put(engine, j, dw, first, end, at=0):
            scatter(engine, j, dw[:, first - at:end - at], first, end)

        w_scalar = tile([P, (2 * N - SPLIT) * PACK], BF16, "w_scalar")

        def gather_scalar(t):
            nc.scalar.activation(places(w_scalar)[:, :, t], planes[t][:].indirect(slots(SPLIT, 2 * N)), ACT.Copy)

        gather_vector(0, 0, SPLIT)
        gather_scalar(0)
        windows.append(tile([P, T], F32, "window3", "plane0"))
        nc.gpsimd.memset(windows[3][:], 0.0)
        wt_spread = tile([P, B, PACK, P // (B * PACK)], F32, "wt_spread")
        nc.scalar.copy(wt_spread[:], wt_sb[:, :, :PACK].unsqueeze(3).to_broadcast([P, B, PACK, P // (B * PACK)]))
        wt_turned_ps = bank("wt_turned_ps", 6, [P, P])
        nc.tensor.transpose(wt_turned_ps[:], wt_spread[:].rearrange("p b t i -> p (b t i)"), identity[:])
        wt_turned = tile([P, P], F32, "wt_turned")
        nc.scalar.copy(wt_turned[:], wt_turned_ps[:])
        wt_bank = bank("wt_bank", 7, [P, P])
        nc.tensor.transpose(wt_bank[:], wt_turned[:], identity[:])
        wt_ps = wt_bank[:].rearrange("p (b t i) -> p b t i", b=B, t=PACK)

        weights1 = tile([P, 1, PACK], F32, "weights1")
        nc.scalar.copy(weights1[:], wt_sb[:, 1:2, :PACK])
        for t in range(1, PACK - 1):
            gather_vector(t, 0, SPLIT)
            gather_scalar(t)
        gather_vector(PACK - 1, 0, HALF)
        gather_vector(PACK - 1, HALF, SPLIT)
        gather_scalar(PACK - 1)
        quantize(w_first, w_vector[:, :HALF * PACK], E4M3)
        x0a, x0b, x1a, x1b = [tile([P, 2 * P * PACK], BF16, name) for name in ("x0a", "x0b", "x1a", "x1b")]
        cast_x_pair("scalar", x0b, x0_raw, 2)
        cast_x_pair("vector", x0a, x0_raw, 0)
        quantize(x_q[0], x0a[:], E4M3)
        quantize(x_q[0], x0b[:], E4M3, HALF)
        w_rest = mx_tiles("w_rest", 3 * HALF, "x0_raw")
        quantize(w_rest, w_vector[:, HALF * PACK:], E4M3)
        quantize(w_rest, w_scalar[:], E4M3, SPLIT - HALF)
        a0 = [scores(c, c, x_q[0], w_rest if c // 2 else w_first, 0) for c in range(4)]
        xm0a_grouped = group_xm("gpsimd", "xm0a", xm0a_raw[:])
        th0 = [tanh_grouped("0%d" % c, subtract("0%d" % c, a0[c], y0, c)) for c in range(4)]
        g0 = [tile([P, HALF * PACK], BF16, "g0%d" % h) for h in range(2)]
        weigh_on_vector(g0[0][:], th0[0][:], 0)
        xm0a_q = quantize_xm("xm0a", xm0a_grouped)
        quantize(g_q[0], g0[0][:], E5M2)
        first = [bank("first%d" % j, 4 + 2 * j, [P, HALF]) for j in range(2)]
        for j in range(2):
            product(first[j][:], xm0a_q, j, g_q[0], 0, HALF)
        cast_x_pair("scalar", x1a, x1_raw, 0)
        weigh_on_vector(g0[1][:], th0[2][:], 0)
        cast_x_pair("vector", x1b, x1_raw, 2)
        dw0 = [tile([P, HALF], F32, "dw0%d" % h) for h in range(2)]
        dw1 = [tile([P, HALF], F32, "dw10")]
        copy_dw("scalar", dw0[0][:], first[0][:])
        copy_dw("scalar", dw1[0][:], first[1][:])
        put("scalar", 0, dw0[0], 0, HALF)
        quantize(g_q[0], g0[1][:], E5M2, HALF)
        quantize(x_q[1], x1a[:], E4M3)
        quantize(x_q[1], x1b[:], E4M3, HALF)
        second = pair(5, xm0a_q, 0, 1)
        a1 = [scores_by_slots(c, x_q[1], w_rest, HALF + (1 - c) * P) for c in range(2)] + [scores(c, c, x_q[1], w_rest, 2 * HALF) for c in range(2, 4)]
        xm0b_grouped = group_xm("gpsimd", "xm0b", xm0b_raw, "x1b")
        put("vector", 1, dw1[0], 0, HALF)
        copy_dw("scalar", dw0[1][:], second[:, :HALF])
        copy_dw("scalar", dw1b[:, :HALF - LATE], second[:, HALF:N - LATE])
        put("scalar", 0, dw0[1], HALF, N, HALF)
        residual10 = tile([P, PACK, P], F32, "residual10")
        subtract_by_slots(residual10[:], a1[0], y1, P)
        xm0b_q = quantize_xm("xm0b", xm0b_grouped)
        xm1a_grouped = group_xm("gpsimd", "xm1a", xm1_raw[:, :, :HALF], "x1b")
        late = [whole(4 + 2 * j, xm0b_q, 0, j) for j in range(2)]
        residual11 = held[:, :N].rearrange("p (t i) -> p t i", t=PACK)
        subtract_by_slots(residual11, a1[1], y1, 0)
        res1 = [subtract("", a1[c], y1, c, held[:, (c - 1) * N:c * N].rearrange("p (t i) -> p t i", t=2)) for c in range(2, 4)]
        th1a_dw3 = tile([P, HALF * PACK - LATE + 2 * N], F32, "th1a_dw3")
        th1a = th1a_dw3[:, :HALF * PACK]
        dw3 = th1a_dw3[:, HALF * PACK - LATE:]
        tanh_side_by_side(th1a[:, N:], residual10[:])
        tanh_side_by_side(th1a[:, :N], residual11)
        th1b = [tanh_grouped("1%d" % (2 + c), res1[c]) for c in range(2)][0]
        g1 = tile([P, N * PACK], BF16, "g1")
        th1a_places = th1a.rearrange("p (i t) -> p i t", t=PACK)
        nc.gpsimd.tensor_tensor(places(g1)[:, ON_VECTOR:HALF], th1a_places[:, ON_VECTOR:], weights1[:].to_broadcast([P, HALF - ON_VECTOR, PACK]), ALU.mult)
        dw2 = tile([P, 2 * N], F32, "dw2")
        copy_dw("vector", dw1b[:, HALF - LATE:], second[:, N - LATE:])
        copy_dw("vector", dw2[:, :N], late[0][:])
        copy_dw("vector", dw3[:, LATE:N], late[1][:, LATE:])
        put("scalar", 1, dw1b, HALF, N, HALF)
        nc.vector.tensor_tensor(places(g1)[:, :ON_VECTOR], th1a_places[:, :ON_VECTOR], wt_ps[:, 1, :, 0].unsqueeze(1).to_broadcast([P, ON_VECTOR, PACK]), ALU.mult)
        weigh_on_vector(g1[:, HALF * PACK:], th1b[:], 1)
        copy_dw("vector", dw3[:, :LATE], late[1][:, :LATE])
        xm1a_q = quantize_xm("xm1a", xm1a_grouped, "weights1")
        quantize(g_q[1], g1[:], E5M2)
        xm1b_grouped = group_xm("gpsimd", "xm1b", xm1_raw[:, :, HALF:], "x1b")
        last = [whole(j, xm1a_q, 1, j) for j in range(2)]
        put("scalar", 2, dw2, 0, 320)
        put("vector", 3, dw3, 0, 256)
        dw01 = [tile([P, N], F32, "dw%d1" % j) for j in range(2)]
        copy_dw("scalar", dw01[0][:], last[0][:])
        copy_dw("scalar", dw01[1][:, :HALF], last[1][:, :HALF])
        copy_dw("scalar", dw01[1][:, HALF:], last[1][:, HALF:])
        xm1b_q = quantize_xm("xm1b", xm1b_grouped)
        last = last + [whole(2 + j, xm1b_q, 1, j) for j in range(2)]
        put("vector", 0, dw01[0], N, 2 * N, N)
        store(0)
        put("scalar", 1, dw01[1], N, N + HALF, N)
        copy_dw("scalar", dw2[:, N:], last[2][:])
        copy_dw("scalar", dw3[:, N:], last[3][:])
        put("scalar", 1, dw01[1], N + HALF, 2 * N, N)
        store(1)
        put("vector", 2, dw2, 320, 2 * N)
        store(2)
        put("scalar", 3, dw3, 256, (256 + 2 * N) // 2)
        put("scalar", 3, dw3, (256 + 2 * N) // 2, 2 * N)
        store(3, nc.scalar)
